import numpy as np
import ml_dtypes


def mxq(x, axis, fmt="e4m3"):
    dtype, down = {"e4m3": (ml_dtypes.float8_e4m3fn, 7), "e5m2": (ml_dtypes.float8_e5m2, 14)}[fmt]
    v = np.moveaxis(np.asarray(x, np.float32).astype(ml_dtypes.bfloat16).astype(np.float64), axis, -1)
    blocks = v.reshape(v.shape[:-1] + (-1, 32))
    amax = np.abs(blocks).max(-1, keepdims=True)
    byte = np.maximum(np.where(amax > 0, np.frexp(amax)[1] - 1 + 127, 0) - down, 1)
    scale = np.exp2(byte - 127.0)
    codes = (blocks / scale).astype(np.float32).astype(dtype).astype(np.float64)
    return np.moveaxis((codes * scale).reshape(v.shape), -1, axis)


WIDE = False


def mx_kscale(k):
    if not WIDE:
        return np.ones(k)
    levels = np.array([10, -10, 5, -5, 0])
    if k % 512:
        return np.exp2(np.random.permutation(np.resize(levels, k // 32))).repeat(32)
    a = np.empty((k // 512, 16))
    for p in range(k // 512):
        a[p, :8] = np.random.permutation(np.resize(levels, 8))
        for g in range(8):
            far = levels[np.abs(levels - a[p, g]) >= 10]
            a[p, g + 8] = far[np.random.randint(len(far))]
    return np.exp2(a.ravel()).repeat(32)


def f64(x):
    return np.asarray(x).astype(np.float64)


def striped(idx):
    return np.tile(idx.reshape(-1, 16).T, (8, 1)).astype(np.uint16)


def unstriped(offs):
    return offs[:16].T.reshape(-1).astype(np.int64)


E2M1 = np.array([0.0, 0.5, 1.0, 1.5, 2.0, 3.0, 4.0, 6.0, -0.0, -0.5, -1.0, -1.5, -2.0, -3.0, -4.0, -6.0])


def pack_weight(w, fmt):
    k, n = w.shape
    w = f64(np.asarray(w, np.float32).astype(ml_dtypes.bfloat16)).reshape(k // 32, 32, n)
    amax = np.abs(w).max(1)
    if fmt == "e4m3":
        byte = np.frexp(amax)[1] - 1 + 127 - 7
    else:
        mant, ex = np.frexp(amax / 6.0)
        byte = np.where(mant > 0.5, ex, ex - 1) + 127
    byte = np.clip(np.where(amax > 0, byte, 1), 1, 254)
    scaled = (w * np.exp2(127.0 - byte)[:, None, :]).reshape(k, n).astype(np.float32)
    by_word = np.ascontiguousarray(scaled.reshape(k // 512, 128, 4, n).transpose(0, 1, 3, 2))
    if fmt == "e4m3":
        words = by_word.astype(ml_dtypes.float8_e4m3fn).view(np.uint8)
    else:
        c = by_word.astype(ml_dtypes.float4_e2m1fn).view(np.uint8) & 0xF
        words = (c[..., 0::2] | (c[..., 1::2] << 4)).reshape(k // 512, 128, 2 * n)
    return np.ascontiguousarray(words), np.ascontiguousarray(byte.astype(np.uint8).reshape(k // 512, 16, n))


def unpack_weight(words, scales, fmt):
    g, _, n = scales.shape
    words = np.ascontiguousarray(words).reshape(g, 128, n, -1)
    if fmt == "e4m3":
        vals = words.view(ml_dtypes.float8_e4m3fn).astype(np.float64)
    else:
        nib = np.empty((g, 128, n, 4), np.uint8)
        nib[..., 0::2] = words & 0xF
        nib[..., 1::2] = words >> 4
        vals = E2M1[nib]
    vals = vals * np.repeat(np.exp2(scales.astype(np.float64) - 127.0), 8, axis=1)[..., None]
    return vals.transpose(0, 1, 3, 2).reshape(g * 512, n)


def gelu(v):
    return 0.5 * v * (1.0 + np.tanh(np.sqrt(2.0 / np.pi) * (v + 0.044715 * v**3)))


def bf(x):
    return np.asarray(x, np.float32).astype(ml_dtypes.bfloat16)

def planes(Y):
    n, m = Y.shape
    b = f64(bf(Y)).reshape(n // 32, 32, m)
    amax = np.abs(b).max(1)
    byte = np.clip(np.where(amax > 0, np.frexp(amax)[1] - 1 + 127 - 7, 1), 1, 254)
    codes = (b * np.exp2(127.0 - byte)[:, None, :]).reshape(n, m).astype(np.float32).astype(ml_dtypes.float8_e4m3fn).view(np.uint8)
    words = codes.reshape(n // 512, 128, 4, m).transpose(0, 1, 3, 2)
    return np.ascontiguousarray(words), np.ascontiguousarray(byte.astype(np.uint8).reshape(n // 512, 16, m))


K, T, S, M, N = 512, 2048, 1024, 1024, 512

def setup_inputs():
    n = np.random.standard_normal
    s = mx_kscale(K)[:, None]
    u = mx_kscale(S)
    idx = np.random.permutation(T)[:S]
    c = np.exp(0.8 * n(N))
    v = 2.0 * n((K, T)) * s / np.sqrt(K)
    x = n((K, M)) / s
    w4 = n((K, N)) * s / np.sqrt(K) * c[None, :]
    wdT = n((N, T)) / np.sqrt(S) * c[:, None]
    wdT[:, idx] /= u
    g = np.exp(0.3 * n(S)) / 6.0 * u
    tab_words, tab_scales = pack_weight(v, "e4m3")
    w4_words, w4_scales = pack_weight(w4, "e2m1")
    return {"tab_words": tab_words, "tab_scales": tab_scales,
            "offs": striped(idx), "x": x.astype(np.float32),
            "w4_words": w4_words, "w4_scales": w4_scales,
            "wdT": wdT.astype(np.float32), "g": g.astype(np.float32)}

def reference(tab_words, tab_scales, offs, x, w4_words, w4_scales, wdT, g):
    v = unpack_weight(tab_words, tab_scales, "e4m3")[:, unstriped(offs)]
    w4 = unpack_weight(w4_words, w4_scales, "e2m1")
    wd = f64(wdT)[:, unstriped(offs)]
    xq = mxq(f64(x), 0, "e4m3")
    a = v.T @ xq
    h = a * np.minimum(np.maximum(a + 3.0, 0.0), 6.0) * f64(g)[:, None]
    y = mxq(wd, 1, "e4m3") @ mxq(h, 0, "e4m3") + w4.T @ xq
    words, scales = planes(y)
    return y, words, scales

@@ -1,0 +1,309 @@
+from contextlib import ExitStack
+
+import concourse.mybir as mybir
+from concourse.masks import make_identity
+
+K, T, S, M, N = 512, 2048, 1024, 1024, 512
+FLOPS = 2 * M * (K * S + S * N + K * N)
+
+F32 = mybir.dt.float32
+BF16 = mybir.dt.bfloat16
+I32 = mybir.dt.int32
+U32 = mybir.dt.uint32
+U16 = mybir.dt.uint16
+U8 = mybir.dt.uint8
+FP8X4 = mybir.dt.float8_e4m3fn_x4
+FP4X4 = mybir.dt.float4_e2m1fn_x4
+ALU = mybir.AluOpType
+ACT = mybir.ActivationFunctionType
+
+P = 128
+PACK = 4
+RUN = 8
+PASSES = S // (P * PACK)
+BANK_M = 128
+CHUNK = 256
+CHUNKS = M // CHUNK
+X_LOADS = ((0, 256), (256, 512), (512, 1024))
+
+
+def tile_list_listed_hardswish_bottleneck_kernel(
+    tc, tab_words, tab_scales, offs, x, w4_words, w4_scales, wdT, g, out_0, out_1, out_2
+):
+    nc = tc.nc
+    with ExitStack() as ctx:
+        keep = ctx.enter_context(tc.tile_pool(name="keep", bufs=1))
+        ring = ctx.enter_context(tc.tile_pool(name="ring", bufs=3))
+        a_psum = ctx.enter_context(tc.psum_pool(name="a_psum", bufs=6))
+        y_psum = ctx.enter_context(tc.psum_pool(name="y_psum", bufs=2))
+
+        offsets = keep.tile([P, S // 16], U16, name="offsets")
+        nc.sync.dma_start(offsets[:], offs)
+
+        tab_plane = keep.tile([P, T], U8, name="tab_plane", align_bytes=64)
+        nc.vector.memset(tab_plane[:].bitcast(I32), 0)
+        for q in range(4):
+            nc.scalar.dma_start(
+                tab_plane[32 * q : 32 * q + 4, :].bitcast(I32), tab_scales[0, 4 * q : 4 * q + 4, :].bitcast(I32)
+            )
+        tab_codes = keep.tile([P, T], U32, name="tab_codes", align_bytes=64)
+        nc.sync.dma_start(tab_codes[:].bitcast(I32), tab_words[0].rearrange("p n i -> p (n i)").bitcast(I32))
+
+        g_rows = keep.tile([P, P], F32, name="g_rows")
+        nc.vector.memset(g_rows[:], 0.0)
+        g_view = g.rearrange("(b q t r) -> b t q r", b=PASSES, t=PACK, r=RUN)
+        for b in range(PASSES):
+            nc.scalar.dma_start(
+                g_rows[PACK * b : PACK * (b + 1), :].rearrange("t (q r) -> t q r", r=RUN), g_view[b]
+            )
+
+        x_view = x.rearrange("(p i) m -> p i m", i=PACK)
+        x_raw = []
+        wd_raw = []
+
+        def load_x(n):
+            lo, hi = X_LOADS[n]
+            raw = keep.tile([P, PACK, hi - lo], F32, name=f"x_raw{n}")
+            nc.sync.dma_start(raw[:], x_view[:, :, lo:hi])
+            for c0 in range(0, hi - lo, CHUNK):
+                x_raw.append(raw[:, :, c0 : c0 + CHUNK])
+
+        load_x(0)
+        wd_view = wdT.rearrange("(p s) c -> p s c", s=PACK)
+        for s in range(PACK):
+            raw = keep.tile([P, T], F32, name=f"wd_raw{s}")
+            nc.sync.dma_start(raw[:], wd_view[:, s, :])
+            wd_raw.append(raw)
+        load_x(1)
+        w4_raw = keep.tile([P, 2 * N], U8, name="w4_raw", align_bytes=64)
+        nc.sync.dma_start(w4_raw[:].bitcast(I32), w4_words[0].bitcast(I32))
+        load_x(2)
+
+        ident_bf = keep.tile([P, P], BF16, name="ident_bf")
+        make_identity(nc, ident_bf[:])
+        ident_f32 = keep.tile([P, P], F32, name="ident_f32")
+        make_identity(nc, ident_f32[:])
+
+        w4_plane_raw = keep.tile([P, N], U8, name="w4_plane_raw", align_bytes=64)
+        nc.vector.memset(w4_plane_raw[:].bitcast(I32), 0)
+        for q in range(4):
+            nc.gpsimd.dma_start(
+                w4_plane_raw[32 * q : 32 * q + 4, :].bitcast(I32), w4_scales[0, 4 * q : 4 * q + 4, :].bitcast(I32)
+            )
+
+        picked_plane = keep.tile([P, S], U8, name="picked_plane", align_bytes=64)
+        nc.vector.tensor_copy(picked_plane[:], tab_plane[:].indirect(offsets[:]))
+        v_codes = keep.tile([P, S], U32, name="v_codes", align_bytes=64)
+        nc.vector.tensor_copy(
+            v_codes[:].rearrange("p (t s r) -> p s t r", t=PACK, r=RUN), tab_codes[:].indirect(offsets[:])
+        )
+        v_plane = keep.tile([P, S], U8, name="v_plane", align_bytes=64)
+        nc.vector.tensor_copy(
+            v_plane[:].bitcast(I32).rearrange("p (t s w) -> p t s w", t=PACK, w=RUN // 4),
+            picked_plane[:].bitcast(I32).rearrange("p (s t w) -> p t s w", t=PACK, w=RUN // 4),
+        )
+
+        g_bank = y_psum.tile([P, P], F32, name="g_bank", tag="y")
+        nc.tensor.transpose(g_bank[:], g_rows[:], ident_f32[:])
+        gain = keep.tile([P, PASSES * PACK], F32, name="gain")
+        nc.scalar.copy(gain[:], g_bank[:, : PASSES * PACK])
+
+        x_codes = keep.tile([P, M], U32, name="x_codes", align_bytes=64)
+        x_plane = keep.tile([P, M], U8, name="x_plane", align_bytes=64)
+        x_bf = {}
+
+        def round_x(k):
+            x_bf[k] = ring.tile([P, CHUNK * PACK], BF16, name="x_bf", align_bytes=64)
+            nc.scalar.copy(
+                x_bf[k][:].rearrange("p (c e i) -> p c i e", e=2, i=PACK),
+                x_raw[k].rearrange("p i (c e) -> p c i e", e=2),
+            )
+
+        def quantize_x(k):
+            cols = slice(k * CHUNK, (k + 1) * CHUNK)
+            nc.vector.quantize_mx(out=x_codes[:, cols].bitcast(FP8X4), scales=x_plane[:, cols], in_=x_bf[k][:])
+
+        wd_codes = keep.tile([P, PACK, PASSES * P], U32, name="wd_codes", align_bytes=64)
+        wd_plane = keep.tile([P, PACK, PASSES * P], U8, name="wd_plane", align_bytes=64)
+        wd_bf = {}
+
+        def gather_wd(s):
+            picked = ring.tile([P, S], BF16, name="wd_picked")
+            nc.vector.tensor_copy(
+                picked[:].rearrange("p (t s r) -> p s t r", t=PACK, r=RUN), wd_raw[s][:].indirect(offsets[:])
+            )
+            turned = y_psum.tile([P, PASSES, PACK, P], BF16, name="turned", tag="y")
+            for b in range(PASSES):
+                for t in range(PACK):
+                    c0 = (t * PASSES + b) * P
+                    nc.tensor.transpose(turned[:, b, t, :], picked[:, c0 : c0 + P], ident_bf[:])
+            wd_bf[s] = ring.tile([P, PASSES, P, PACK], BF16, name="wd_bf", align_bytes=64)
+            nc.scalar.copy(wd_bf[s][:], turned[:].rearrange("p b t n -> p b n t"))
+
+        def quantize_wd(s):
+            nc.vector.quantize_mx(
+                out=wd_codes[:, s, :].bitcast(FP8X4),
+                scales=wd_plane[:, s, :],
+                in_=wd_bf[s][:].rearrange("p b n t -> p (b n t)"),
+            )
+
+        w4_codes = keep.tile([P, PACK, P, 2], U8, name="w4_codes", align_bytes=64)
+        w4_plane = keep.tile([P, PACK, P], U8, name="w4_plane", align_bytes=64)
+
+        def deal_w4():
+            nc.vector.tensor_copy(w4_codes[:], w4_raw[:].rearrange("p (n s e) -> p s n e", s=PACK, e=2))
+            nc.vector.tensor_copy(w4_plane[:], w4_plane_raw[:].rearrange("p (n s) -> p s n", s=PACK))
+
+        a_banks = {}
+        lifted = {}
+        gated = {}
+        h_bf = {}
+        h_codes = {}
+        h_plane = {}
+
+        def project(u):
+            k, b = divmod(u, PASSES)
+            lifted[u] = ring.tile([P, PACK, CHUNK], F32, name="lifted")
+            for half in range(CHUNK // BANK_M):
+                bank = a_psum.tile([P, PACK, BANK_M], F32, name="a_bank")
+                a_banks[u, half] = bank
+                cols = slice(k * CHUNK + half * BANK_M, k * CHUNK + (half + 1) * BANK_M)
+                for t in range(PACK):
+                    c0 = (t * PASSES + b) * P
+                    nc.tensor.matmul_mx(
+                        out=bank[:, t, :],
+                        lhsT=v_codes[:, c0 : c0 + P].bitcast(FP8X4),
+                        lhsT_scale=v_plane[:, c0 : c0 + P],
+                        rhs=x_codes[:, cols].bitcast(FP8X4),
+                        rhs_scale=x_plane[:, cols],
+                        start=True,
+                        stop=True,
+                    )
+                nc.scalar.activation(
+                    lifted[u][:, :, half * BANK_M : (half + 1) * BANK_M], bank[:], ACT.Relu, bias=3.0
+                )
+
+        def gate(u):
+            b = u % PASSES
+            gated[u] = ring.tile([P, PACK, CHUNK], F32, name="gated")
+            for t in range(PACK):
+                col = b * PACK + t
+                nc.vector.tensor_scalar(
+                    gated[u][:, t, :], lifted[u][:, t, :], 6.0, gain[:, col : col + 1], ALU.min, ALU.mult
+                )
+
+        def swish(u):
+            h_bf[u] = ring.tile([P, CHUNK * PACK], BF16, name="h_bf", align_bytes=64)
+            for half in range(CHUNK // BANK_M):
+                lo = half * BANK_M
+                nc.vector.tensor_tensor(
+                    h_bf[u][:, lo * PACK : (lo + BANK_M) * PACK].rearrange("p (c e t) -> p c t e", e=2, t=PACK),
+                    a_banks[u, half][:].rearrange("p t (c e) -> p c t e", e=2),
+                    gated[u][:, :, lo : lo + BANK_M].rearrange("p t (c e) -> p c t e", e=2),
+                    ALU.mult,
+                )
+
+        def quantize_h(u):
+            h_codes[u] = keep.tile([P, CHUNK], U32, name=f"h_codes{u}", align_bytes=64)
+            h_plane[u] = keep.tile([P, CHUNK], U8, name=f"h_plane{u}", align_bytes=64)
+            nc.vector.quantize_mx(out=h_codes[u][:].bitcast(FP8X4), scales=h_plane[u][:], in_=h_bf[u][:])
+
+        y_codes = keep.tile([P, M], U32, name="y_codes", align_bytes=64)
+        y_plane = keep.tile([P, M], U8, name="y_plane", align_bytes=64)
+        y_view = out_0.rearrange("(p s) m -> p s m", s=PACK)
+        y_words = out_1[0].rearrange("p m t -> p (m t)")
+        y_bf = {}
+
+        def down(k):
+            y_f32 = ring.tile([P, PACK, CHUNK], F32, name="y_f32")
+            y_bf[k] = ring.tile([P, CHUNK, PACK], BF16, name="y_bf", align_bytes=64)
+            for half in range(CHUNK // BANK_M):
+                lo = half * BANK_M
+                bank = y_psum.tile([P, PACK, BANK_M], F32, name="y_bank", tag="y")
+                cols = slice(k * CHUNK + lo, k * CHUNK + lo + BANK_M)
+                for s in range(PACK):
+                    nc.tensor.matmul_mx(
+                        out=bank[:, s, :],
+                        lhsT=w4_codes[:, s, :, :].rearrange("p n e -> p (n e)").bitcast(FP4X4),
+                        lhsT_scale=w4_plane[:, s, :],
+                        rhs=x_codes[:, cols].bitcast(FP8X4),
+                        rhs_scale=x_plane[:, cols],
+                        start=(s == 0),
+                        stop=False,
+                    )
+                for b in range(PASSES):
+                    u = k * PASSES + b
+                    for s in range(PACK):
+                        nc.tensor.matmul_mx(
+                            out=bank[:, s, :],
+                            lhsT=wd_codes[:, s, b * P : (b + 1) * P].bitcast(FP8X4),
+                            lhsT_scale=wd_plane[:, s, b * P : (b + 1) * P],
+                            rhs=h_codes[u][:, lo : lo + BANK_M].bitcast(FP8X4),
+                            rhs_scale=h_plane[u][:, lo : lo + BANK_M],
+                            start=False,
+                            stop=(b == PASSES - 1 and s == PACK - 1),
+                        )
+                nc.scalar.copy(y_bf[k][:, lo : lo + BANK_M, :], bank[:].rearrange("p s m -> p m s"))
+                nc.scalar.copy(y_f32[:, :, lo : lo + BANK_M], bank[:])
+            nc.sync.dma_start(y_view[:, :, k * CHUNK : (k + 1) * CHUNK], y_f32[:])
+
+        def quantize_y(k):
+            cols = slice(k * CHUNK, (k + 1) * CHUNK)
+            nc.vector.quantize_mx(
+                out=y_codes[:, cols].bitcast(FP8X4),
+                scales=y_plane[:, cols],
+                in_=y_bf[k][:].rearrange("p m s -> p (m s)"),
+            )
+            nc.sync.dma_start(
+                y_words[:, k * CHUNK * PACK : (k + 1) * CHUNK * PACK].bitcast(I32), y_codes[:, cols].bitcast(I32)
+            )
+
+        round_x(0)
+        quantize_x(0)
+        project(0)
+        project(1)
+        gather_wd(0)
+        gate(0)
+        gate(1)
+        swish(0)
+        gather_wd(1)
+        quantize_wd(0)
+        swish(1)
+        quantize_h(0)
+        gather_wd(2)
+        quantize_wd(1)
+        quantize_h(1)
+        round_x(1)
+        gather_wd(3)
+        quantize_x(1)
+        quantize_wd(2)
+        project(2)
+        deal_w4()
+        round_x(2)
+        quantize_wd(3)
+        gate(2)
+        units = CHUNKS * PASSES
+        for u in range(2, units):
+            k, b = divmod(u, PASSES)
+            if u + 1 < units:
+                project(u + 1)
+                gate(u + 1)
+            swish(u)
+            if u > 2:
+                quantize_h(u - 1)
+            if b == 0:
+                down(k - 1)
+                if k + 1 < CHUNKS:
+                    quantize_x(k + 1)
+                if k + 2 < CHUNKS:
+                    round_x(k + 2)
+            else:
+                quantize_y(k - 1)
+        quantize_h(units - 1)
+        down(CHUNKS - 1)
+        quantize_y(CHUNKS - 1)
+        for q in range(4):
+            queue = nc.sync if q % 2 == 0 else nc.scalar
+            queue.dma_start(
+                out_2[0, 4 * q : 4 * q + 4, :].bitcast(I32), y_plane[32 * q : 32 * q + 4, :].bitcast(I32)
+            )

@@ -24,7 +24,9 @@ PASSES = S // (P * PACK)
 BANK_M = 128
 CHUNK = 256
 CHUNKS = M // CHUNK
-X_LOADS = ((0, 256), (256, 512), (512, 1024))
+LIFT = {0: "pair_raw0"}
+TAG = {"x_bf1": "picked2", "x_bf2": "x_raw1", "x_bf3": "x_raw2", "w4_codes": "wd_raw3", "w4_plane": "pair_words", "gated0": "wd_raw2", "picked3": "h_first0"}
+X_LOADS = ((0, 256), (256, 512), (512, 768), (768, 1024))
 
 
 def tile_list_listed_hardswish_bottleneck_kernel(
@@ -40,80 +42,95 @@ def tile_list_listed_hardswish_bottleneck_kernel(
         offsets = keep.tile([P, S // 16], U16, name="offsets")
         nc.sync.dma_start(offsets[:], offs)
 
-        tab_plane = keep.tile([P, T], U8, name="tab_plane", align_bytes=64)
-        nc.vector.memset(tab_plane[:].bitcast(I32), 0)
-        for q in range(4):
-            nc.scalar.dma_start(
-                tab_plane[32 * q : 32 * q + 4, :].bitcast(I32), tab_scales[0, 4 * q : 4 * q + 4, :].bitcast(I32)
-            )
-        tab_codes = keep.tile([P, T], U32, name="tab_codes", align_bytes=64)
-        nc.sync.dma_start(tab_codes[:].bitcast(I32), tab_words[0].rearrange("p n i -> p (n i)").bitcast(I32))
-
-        g_rows = keep.tile([P, P], F32, name="g_rows")
-        nc.vector.memset(g_rows[:], 0.0)
-        g_view = g.rearrange("(b q t r) -> b t q r", b=PASSES, t=PACK, r=RUN)
-        for b in range(PASSES):
-            nc.scalar.dma_start(
-                g_rows[PACK * b : PACK * (b + 1), :].rearrange("t (q r) -> t q r", r=RUN), g_view[b]
-            )
-
         x_view = x.rearrange("(p i) m -> p i m", i=PACK)
         x_raw = []
-        wd_raw = []
 
         def load_x(n):
             lo, hi = X_LOADS[n]
-            raw = keep.tile([P, PACK, hi - lo], F32, name=f"x_raw{n}")
+            raw = keep.tile([P, PACK, hi - lo], F32, name=f"x_raw{n}", align_bytes=64)
             nc.sync.dma_start(raw[:], x_view[:, :, lo:hi])
             for c0 in range(0, hi - lo, CHUNK):
                 x_raw.append(raw[:, :, c0 : c0 + CHUNK])
 
-        load_x(0)
-        wd_view = wdT.rearrange("(p s) c -> p s c", s=PACK)
-        for s in range(PACK):
-            raw = keep.tile([P, T], F32, name=f"wd_raw{s}")
-            nc.sync.dma_start(raw[:], wd_view[:, s, :])
-            wd_raw.append(raw)
-        load_x(1)
-        w4_raw = keep.tile([P, 2 * N], U8, name="w4_raw", align_bytes=64)
-        nc.sync.dma_start(w4_raw[:].bitcast(I32), w4_words[0].bitcast(I32))
-        load_x(2)
+        tab_codes = keep.tile([P, T], U32, name="tab_codes", align_bytes=64)
+        nc.sync.dma_start(tab_codes[:].bitcast(I32), tab_words[0].rearrange("p n i -> p (n i)").bitcast(I32))
 
-        ident_bf = keep.tile([P, P], BF16, name="ident_bf")
-        make_identity(nc, ident_bf[:])
+        tab_plane = keep.tile([P, T], U8, name="tab_plane", align_bytes=64)
+        nc.vector.memset(tab_plane[:].bitcast(I32), 0)
+        for q in range(4):
+            nc.sync.dma_start(
+                tab_plane[32 * q : 32 * q + 4, :].bitcast(I32), tab_scales[0, 4 * q : 4 * q + 4, :].bitcast(I32)
+            )
+        load_x(0)
+
+        g_rows = keep.tile([P, PASSES * P], F32, name="g_rows")
+        nc.vector.memset(g_rows[:], 0.0)
+        nc.sync.dma_start(
+            g_rows[:PACK, :].rearrange("t (s r) -> t s r", r=RUN), g.rearrange("(s t r) -> t s r", t=PACK, r=RUN)
+        )
+
+        wd_view = wdT.rearrange("(p s) c -> p s c", s=PACK)
+        pair_raw = []
+        wd_raw = {}
+
+        def load_pair(n):
+            raw = keep.tile([P, 2, T // 2], F32, name=f"pair_raw{n}", align_bytes=64)
+            nc.sync.dma_start(raw[:], wd_view[:, 0:2, n * T // 2 : (n + 1) * T // 2])
+            pair_raw.append(raw)
+
+        w4_raw = keep.tile([P, 2 * N], U8, name="w4_raw", align_bytes=64)
+        w4_plane_raw = keep.tile([P, N], U8, name="w4_plane_raw", align_bytes=64)
+
+        def load_w4():
+            nc.sync.dma_start(w4_raw[:].bitcast(I32), w4_words[0].bitcast(I32))
+            nc.gpsimd.memset(w4_plane_raw[:].bitcast(I32), 0)
+            for q in range(4):
+                nc.sync.dma_start(
+                    w4_plane_raw[32 * q : 32 * q + 4, :].bitcast(I32), w4_scales[0, 4 * q : 4 * q + 4, :].bitcast(I32)
+                )
+
+        def load_wd(s):
+            wd_raw[s] = keep.tile([P, T], F32, name=f"wd_raw{s}", align_bytes=64)
+            nc.sync.dma_start(wd_raw[s][:], wd_view[:, s, :])
+
+        load_pair(0)
+        load_wd(2)
+        load_pair(1)
+        load_x(1)
+        load_wd(3)
+        load_x(2)
+        load_x(3)
+        load_w4()
+
         ident_f32 = keep.tile([P, P], F32, name="ident_f32")
         make_identity(nc, ident_f32[:])
-
-        w4_plane_raw = keep.tile([P, N], U8, name="w4_plane_raw", align_bytes=64)
-        nc.vector.memset(w4_plane_raw[:].bitcast(I32), 0)
-        for q in range(4):
-            nc.gpsimd.dma_start(
-                w4_plane_raw[32 * q : 32 * q + 4, :].bitcast(I32), w4_scales[0, 4 * q : 4 * q + 4, :].bitcast(I32)
-            )
+        ident_bf = keep.tile([P, P], BF16, name="ident_bf")
+        make_identity(nc, ident_bf[:])
 
         picked_plane = keep.tile([P, S], U8, name="picked_plane", align_bytes=64)
         nc.vector.tensor_copy(picked_plane[:], tab_plane[:].indirect(offsets[:]))
+        v_plane = keep.tile([P, S], U8, name="v_plane", align_bytes=64)
         v_codes = keep.tile([P, S], U32, name="v_codes", align_bytes=64)
         nc.vector.tensor_copy(
             v_codes[:].rearrange("p (t s r) -> p s t r", t=PACK, r=RUN), tab_codes[:].indirect(offsets[:])
         )
-        v_plane = keep.tile([P, S], U8, name="v_plane", align_bytes=64)
         nc.vector.tensor_copy(
             v_plane[:].bitcast(I32).rearrange("p (t s w) -> p t s w", t=PACK, w=RUN // 4),
             picked_plane[:].bitcast(I32).rearrange("p (s t w) -> p t s w", t=PACK, w=RUN // 4),
         )
 
-        g_bank = y_psum.tile([P, P], F32, name="g_bank", tag="y")
-        nc.tensor.transpose(g_bank[:], g_rows[:], ident_f32[:])
+        g_bank = y_psum.tile([P, PASSES, P], F32, name="g_bank", tag="y")
+        for b in range(PASSES):
+            nc.tensor.transpose(g_bank[:, b, :], g_rows[:, b * P : (b + 1) * P], ident_f32[:])
         gain = keep.tile([P, PASSES * PACK], F32, name="gain")
-        nc.scalar.copy(gain[:], g_bank[:, : PASSES * PACK])
+        nc.scalar.copy(gain[:].rearrange("p (b t) -> p b t", t=PACK), g_bank[:, :, :PACK])
 
         x_codes = keep.tile([P, M], U32, name="x_codes", align_bytes=64)
         x_plane = keep.tile([P, M], U8, name="x_plane", align_bytes=64)
         x_bf = {}
 
         def round_x(k):
-            x_bf[k] = ring.tile([P, CHUNK * PACK], BF16, name="x_bf", align_bytes=64)
+            x_bf[k] = keep.tile([P, CHUNK * PACK], BF16, name=f"x_bf{k}", tag=TAG.get(f"x_bf{k}", f"x_bf{k}"), align_bytes=64)
             nc.scalar.copy(
                 x_bf[k][:].rearrange("p (c e i) -> p c i e", e=2, i=PACK),
                 x_raw[k].rearrange("p i (c e) -> p c i e", e=2),
@@ -125,10 +142,10 @@ def tile_list_listed_hardswish_bottleneck_kernel(
 
         wd_codes = keep.tile([P, PACK, PASSES * P], U32, name="wd_codes", align_bytes=64)
         wd_plane = keep.tile([P, PACK, PASSES * P], U8, name="wd_plane", align_bytes=64)
-        wd_bf = {}
+        wd_bf = [keep.tile([P, 2, PASSES, P, PACK], BF16, name=f"wd_bf{n}", align_bytes=64) for n in range(2)]
 
         def gather_wd(s):
-            picked = ring.tile([P, S], BF16, name="wd_picked")
+            picked = keep.tile([P, S], BF16, name=f"picked{s}", tag=TAG.get(f"picked{s}", f"picked{s}"), align_bytes=64)
             nc.vector.tensor_copy(
                 picked[:].rearrange("p (t s r) -> p s t r", t=PACK, r=RUN), wd_raw[s][:].indirect(offsets[:])
             )
@@ -137,20 +154,45 @@ def tile_list_listed_hardswish_bottleneck_kernel(
                 for t in range(PACK):
                     c0 = (t * PASSES + b) * P
                     nc.tensor.transpose(turned[:, b, t, :], picked[:, c0 : c0 + P], ident_bf[:])
-            wd_bf[s] = ring.tile([P, PASSES, P, PACK], BF16, name="wd_bf", align_bytes=64)
-            nc.scalar.copy(wd_bf[s][:], turned[:].rearrange("p b t n -> p b n t"))
+            nc.scalar.copy(wd_bf[1][:, s - 2, :, :, :], turned[:].rearrange("p b t n -> p b n t"))
 
-        def quantize_wd(s):
-            nc.vector.quantize_mx(
-                out=wd_codes[:, s, :].bitcast(FP8X4),
-                scales=wd_plane[:, s, :],
-                in_=wd_bf[s][:].rearrange("p b n t -> p (b n t)"),
+        pair_words = keep.tile([P, T], U32, name="pair_words", align_bytes=64)
+
+        def round_pair(n):
+            nc.scalar.copy(
+                pair_words[:, n * T // 2 : (n + 1) * T // 2].bitcast(BF16).rearrange("p (c e) -> p c e", e=2),
+                pair_raw[n][:].rearrange("p e c -> p c e"),
             )
 
-        w4_codes = keep.tile([P, PACK, P, 2], U8, name="w4_codes", align_bytes=64)
-        w4_plane = keep.tile([P, PACK, P], U8, name="w4_plane", align_bytes=64)
+        def gather_pair():
+            picked = keep.tile([P, S], U32, name="pair_picked", tag=TAG.get("pair_picked", "pair_picked"), align_bytes=64)
+            nc.vector.tensor_copy(
+                picked[:].rearrange("p (t s r) -> p s t r", t=PACK, r=RUN), pair_words[:].indirect(offsets[:])
+            )
+            for b in range(PASSES):
+                turned = y_psum.tile([P, PACK, P], F32, name="turned_pair", tag="y")
+                for t in range(PACK):
+                    c0 = (t * PASSES + b) * P
+                    nc.tensor.transpose(turned[:, t, :], picked[:, c0 : c0 + P].bitcast(F32), ident_f32[:])
+                nc.scalar.copy(
+                    wd_bf[0][:, :, b, :, :],
+                    turned[:].bitcast(BF16).rearrange("p t (n e) -> p e n t", e=2),
+                )
+
+        def quantize_wd(pair):
+            nc.vector.quantize_mx(
+                out=wd_codes[:, 2 * pair : 2 * pair + 2, :].rearrange("p s c -> p (s c)").bitcast(FP8X4),
+                scales=wd_plane[:, 2 * pair : 2 * pair + 2, :].rearrange("p s c -> p (s c)"),
+                in_=wd_bf[pair][:].rearrange("p s b n t -> p (s b n t)"),
+            )
+
+        w4 = {}
 
         def deal_w4():
+            w4_codes = keep.tile([P, PACK, P, 2], U8, name="w4_codes", tag=TAG.get("w4_codes", "w4_codes"), align_bytes=64)
+            w4_plane = keep.tile([P, PACK, P], U8, name="w4_plane", tag=TAG.get("w4_plane", "w4_plane"), align_bytes=64)
+            w4["codes"] = w4_codes
+            w4["plane"] = w4_plane
             nc.vector.tensor_copy(w4_codes[:], w4_raw[:].rearrange("p (n s e) -> p s n e", s=PACK, e=2))
             nc.vector.tensor_copy(w4_plane[:], w4_plane_raw[:].rearrange("p (n s) -> p s n", s=PACK))
 
@@ -163,7 +205,12 @@ def tile_list_listed_hardswish_bottleneck_kernel(
 
         def project(u):
             k, b = divmod(u, PASSES)
-            lifted[u] = ring.tile([P, PACK, CHUNK], F32, name="lifted")
+            if k in LIFT:
+                if b == 0:
+                    both = keep.tile([P, PASSES, PACK, CHUNK], F32, name=f"lifted{k}", tag=LIFT[k], align_bytes=64)
+                    lifted[u], lifted[u + 1] = both[:, 0, :, :], both[:, 1, :, :]
+            else:
+                lifted[u] = ring.tile([P, PACK, CHUNK], F32, name="lifted")
             for half in range(CHUNK // BANK_M):
                 bank = a_psum.tile([P, PACK, BANK_M], F32, name="a_bank")
                 a_banks[u, half] = bank
@@ -185,16 +232,23 @@ def tile_list_listed_hardswish_bottleneck_kernel(
 
         def gate(u):
             b = u % PASSES
-            gated[u] = ring.tile([P, PACK, CHUNK], F32, name="gated")
+            if f"gated{u}" in TAG:
+                gated[u] = keep.tile([P, PACK, CHUNK], F32, name=f"gated{u}", tag=TAG[f"gated{u}"], align_bytes=64)
+            else:
+                gated[u] = ring.tile([P, PACK, CHUNK], F32, name="gated")
             for t in range(PACK):
                 col = b * PACK + t
                 nc.vector.tensor_scalar(
                     gated[u][:, t, :], lifted[u][:, t, :], 6.0, gain[:, col : col + 1], ALU.min, ALU.mult
                 )
 
-        def swish(u):
-            h_bf[u] = ring.tile([P, CHUNK * PACK], BF16, name="h_bf", align_bytes=64)
-            for half in range(CHUNK // BANK_M):
+        def swish(u, *halves):
+            if u not in h_bf:
+                if u < 2:
+                    h_bf[u] = keep.tile([P, CHUNK * PACK], BF16, name=f"h_first{u}", align_bytes=64)
+                else:
+                    h_bf[u] = ring.tile([P, CHUNK * PACK], BF16, name="h_bf", align_bytes=64)
+            for half in halves or range(CHUNK // BANK_M):
                 lo = half * BANK_M
                 nc.vector.tensor_tensor(
                     h_bf[u][:, lo * PACK : (lo + BANK_M) * PACK].rearrange("p (c e t) -> p c t e", e=2, t=PACK),
@@ -203,10 +257,15 @@ def tile_list_listed_hardswish_bottleneck_kernel(
                     ALU.mult,
                 )
 
-        def quantize_h(u):
-            h_codes[u] = keep.tile([P, CHUNK], U32, name=f"h_codes{u}", align_bytes=64)
-            h_plane[u] = keep.tile([P, CHUNK], U8, name=f"h_plane{u}", align_bytes=64)
-            nc.vector.quantize_mx(out=h_codes[u][:].bitcast(FP8X4), scales=h_plane[u][:], in_=h_bf[u][:])
+        def quantize_h(u, lo=0, hi=CHUNK):
+            if lo == 0:
+                h_codes[u] = keep.tile([P, CHUNK], U32, name=f"h_codes{u}", align_bytes=64)
+                h_plane[u] = keep.tile([P, CHUNK], U8, name=f"h_plane{u}", align_bytes=64)
+            nc.vector.quantize_mx(
+                out=h_codes[u][:, lo:hi].bitcast(FP8X4),
+                scales=h_plane[u][:, lo:hi],
+                in_=h_bf[u][:, lo * PACK : hi * PACK],
+            )
 
         y_codes = keep.tile([P, M], U32, name="y_codes", align_bytes=64)
         y_plane = keep.tile([P, M], U8, name="y_plane", align_bytes=64)
@@ -214,94 +273,119 @@ def tile_list_listed_hardswish_bottleneck_kernel(
         y_words = out_1[0].rearrange("p m t -> p (m t)")
         y_bf = {}
 
-        def down(k):
-            y_f32 = ring.tile([P, PACK, CHUNK], F32, name="y_f32")
-            y_bf[k] = ring.tile([P, CHUNK, PACK], BF16, name="y_bf", align_bytes=64)
-            for half in range(CHUNK // BANK_M):
-                lo = half * BANK_M
-                bank = y_psum.tile([P, PACK, BANK_M], F32, name="y_bank", tag="y")
-                cols = slice(k * CHUNK + lo, k * CHUNK + lo + BANK_M)
+        y_f32 = {}
+        y_banks = {}
+
+        def down(k, half):
+            if half == 0:
+                y_f32[k] = ring.tile([P, PACK, CHUNK], F32, name="y_f32")
+                y_bf[k] = ring.tile([P, CHUNK, PACK], BF16, name="y_bf", align_bytes=64)
+            lo = half * BANK_M
+            bank = y_psum.tile([P, PACK, BANK_M], F32, name="y_bank", tag="y")
+            y_banks[k, half] = bank
+            cols = slice(k * CHUNK + lo, k * CHUNK + lo + BANK_M)
+            for s in range(PACK):
+                nc.tensor.matmul_mx(
+                    out=bank[:, s, :],
+                    lhsT=w4["codes"][:, s, :, :].rearrange("p n e -> p (n e)").bitcast(FP4X4),
+                    lhsT_scale=w4["plane"][:, s, :],
+                    rhs=x_codes[:, cols].bitcast(FP8X4),
+                    rhs_scale=x_plane[:, cols],
+                    start=(s == 0),
+                    stop=False,
+                )
+            for b in range(PASSES):
+                u = k * PASSES + b
                 for s in range(PACK):
                     nc.tensor.matmul_mx(
                         out=bank[:, s, :],
-                        lhsT=w4_codes[:, s, :, :].rearrange("p n e -> p (n e)").bitcast(FP4X4),
-                        lhsT_scale=w4_plane[:, s, :],
-                        rhs=x_codes[:, cols].bitcast(FP8X4),
-                        rhs_scale=x_plane[:, cols],
-                        start=(s == 0),
-                        stop=False,
+                        lhsT=wd_codes[:, s, b * P : (b + 1) * P].bitcast(FP8X4),
+                        lhsT_scale=wd_plane[:, s, b * P : (b + 1) * P],
+                        rhs=h_codes[u][:, lo : lo + BANK_M].bitcast(FP8X4),
+                        rhs_scale=h_plane[u][:, lo : lo + BANK_M],
+                        start=False,
+                        stop=(b == PASSES - 1 and s == PACK - 1),
                     )
-                for b in range(PASSES):
-                    u = k * PASSES + b
-                    for s in range(PACK):
-                        nc.tensor.matmul_mx(
-                            out=bank[:, s, :],
-                            lhsT=wd_codes[:, s, b * P : (b + 1) * P].bitcast(FP8X4),
-                            lhsT_scale=wd_plane[:, s, b * P : (b + 1) * P],
-                            rhs=h_codes[u][:, lo : lo + BANK_M].bitcast(FP8X4),
-                            rhs_scale=h_plane[u][:, lo : lo + BANK_M],
-                            start=False,
-                            stop=(b == PASSES - 1 and s == PACK - 1),
-                        )
-                nc.scalar.copy(y_bf[k][:, lo : lo + BANK_M, :], bank[:].rearrange("p s m -> p m s"))
-                nc.scalar.copy(y_f32[:, :, lo : lo + BANK_M], bank[:])
-            nc.sync.dma_start(y_view[:, :, k * CHUNK : (k + 1) * CHUNK], y_f32[:])
+            nc.scalar.copy(y_bf[k][:, lo : lo + BANK_M, :], bank[:].rearrange("p s m -> p m s"))
 
-        def quantize_y(k):
-            cols = slice(k * CHUNK, (k + 1) * CHUNK)
+        def copy_y(k, half, copy):
+            lo = half * BANK_M
+            copy(y_f32[k][:, :, lo : lo + BANK_M], y_banks[k, half][:])
+
+        def store_y(k, lo=0, hi=CHUNK):
+            nc.sync.dma_start(y_view[:, :, k * CHUNK + lo : k * CHUNK + hi], y_f32[k][:, :, lo:hi])
+
+        def quantize_y(k, lo=0, hi=CHUNK):
+            cols = slice(k * CHUNK + lo, k * CHUNK + hi)
             nc.vector.quantize_mx(
                 out=y_codes[:, cols].bitcast(FP8X4),
                 scales=y_plane[:, cols],
-                in_=y_bf[k][:].rearrange("p m s -> p (m s)"),
+                in_=y_bf[k][:, lo:hi, :].rearrange("p m s -> p (m s)"),
             )
             nc.sync.dma_start(
-                y_words[:, k * CHUNK * PACK : (k + 1) * CHUNK * PACK].bitcast(I32), y_codes[:, cols].bitcast(I32)
+                y_words[:, cols.start * PACK : cols.stop * PACK].bitcast(I32), y_codes[:, cols].bitcast(I32)
             )
+
+        def down_whole(k):
+            for half in range(CHUNK // BANK_M):
+                down(k, half)
+                copy_y(k, half, nc.scalar.copy)
+            store_y(k)
 
         round_x(0)
         quantize_x(0)
+        round_pair(0)
         project(0)
         project(1)
-        gather_wd(0)
-        gate(0)
-        gate(1)
-        swish(0)
-        gather_wd(1)
-        quantize_wd(0)
-        swish(1)
-        quantize_h(0)
         gather_wd(2)
-        quantize_wd(1)
-        quantize_h(1)
+        round_pair(1)
+        gate(0)
+        swish(0)
         round_x(1)
-        gather_wd(3)
+        gate(1)
+        quantize_h(0)
+        swish(1)
         quantize_x(1)
-        quantize_wd(2)
+        gather_pair()
         project(2)
-        deal_w4()
+        project(3)
+        quantize_h(1)
+        gather_wd(3)
         round_x(2)
-        quantize_wd(3)
         gate(2)
+        quantize_wd(0)
+        quantize_x(2)
+        deal_w4()
+        quantize_wd(1)
+        round_x(3)
         units = CHUNKS * PASSES
-        for u in range(2, units):
+        for u in range(2, units - 1):
             k, b = divmod(u, PASSES)
-            if u + 1 < units:
-                project(u + 1)
-                gate(u + 1)
-            swish(u)
-            if u > 2:
-                quantize_h(u - 1)
+            if u + 2 < units:
+                project(u + 2)
             if b == 0:
-                down(k - 1)
-                if k + 1 < CHUNKS:
-                    quantize_x(k + 1)
-                if k + 2 < CHUNKS:
-                    round_x(k + 2)
-            else:
+                down_whole(k - 1)
+            swish(u)
+            if u == 3:
+                quantize_x(3)
+            gate(u + 1)
+            quantize_h(u)
+            if b == 1:
                 quantize_y(k - 1)
-        quantize_h(units - 1)
-        down(CHUNKS - 1)
-        quantize_y(CHUNKS - 1)
+        last = CHUNKS - 1
+        swish(units - 1, 0)
+        quantize_y(last - 1)
+        quantize_h(units - 1, 0, BANK_M)
+        down(last, 0)
+        swish(units - 1, 1)
+        quantize_h(units - 1, BANK_M, CHUNK)
+        down(last, 1)
+        quantize_y(last, 0, BANK_M)
+        copy_y(last, 0, nc.vector.tensor_copy)
+        store_y(last, 0, BANK_M)
+        quantize_y(last, BANK_M, CHUNK)
+        copy_y(last, 1, nc.scalar.copy)
+        store_y(last, BANK_M, CHUNK)
         for q in range(4):
             queue = nc.sync if q % 2 == 0 else nc.scalar
             queue.dma_start(

@@ -21,12 +21,10 @@ P = 128
 PACK = 4
 RUN = 8
 PASSES = S // (P * PACK)
+QUADRANTS = 4
 BANK_M = 128
-CHUNK = 256
-CHUNKS = M // CHUNK
-LIFT = {0: "pair_raw0"}
-TAG = {"x_bf1": "picked2", "x_bf2": "x_raw1", "x_bf3": "x_raw2", "w4_codes": "wd_raw3", "w4_plane": "pair_words", "gated0": "wd_raw2", "picked3": "h_first0"}
-X_LOADS = ((0, 256), (256, 512), (512, 768), (768, 1024))
+STRIP = 256
+CHUNKS = ((0, 256), (256, 768), (768, 1024))
 
 
 def tile_list_listed_hardswish_bottleneck_kernel(
@@ -39,355 +37,337 @@ def tile_list_listed_hardswish_bottleneck_kernel(
         a_psum = ctx.enter_context(tc.psum_pool(name="a_psum", bufs=6))
         y_psum = ctx.enter_context(tc.psum_pool(name="y_psum", bufs=2))
 
+        def held(shape, dtype, name, after=None):
+            return keep.tile(shape, dtype, name=name, tag=after or name, align_bytes=64)
+
+        def load_plane(plane, scale_rows):
+            for q in range(QUADRANTS):
+                nc.sync.dma_start(
+                    plane[32 * q : 32 * q + 4, :].bitcast(I32), scale_rows[4 * q : 4 * q + 4, :].bitcast(I32)
+                )
+
+        tab_codes = held([P, T], U32, "tab_codes")
+        nc.sync.dma_start(tab_codes[:].bitcast(I32), tab_words[0].rearrange("p c i -> p (c i)").bitcast(I32))
         offsets = keep.tile([P, S // 16], U16, name="offsets")
         nc.sync.dma_start(offsets[:], offs)
 
-        x_view = x.rearrange("(p i) m -> p i m", i=PACK)
-        x_raw = []
-
-        def load_x(n):
-            lo, hi = X_LOADS[n]
-            raw = keep.tile([P, PACK, hi - lo], F32, name=f"x_raw{n}", align_bytes=64)
-            nc.sync.dma_start(raw[:], x_view[:, :, lo:hi])
-            for c0 in range(0, hi - lo, CHUNK):
-                x_raw.append(raw[:, :, c0 : c0 + CHUNK])
-
-        tab_codes = keep.tile([P, T], U32, name="tab_codes", align_bytes=64)
-        nc.sync.dma_start(tab_codes[:].bitcast(I32), tab_words[0].rearrange("p n i -> p (n i)").bitcast(I32))
-
-        tab_plane = keep.tile([P, T], U8, name="tab_plane", align_bytes=64)
+        tab_plane = held([P, T], U8, "tab_plane")
         nc.vector.memset(tab_plane[:].bitcast(I32), 0)
-        for q in range(4):
-            nc.sync.dma_start(
-                tab_plane[32 * q : 32 * q + 4, :].bitcast(I32), tab_scales[0, 4 * q : 4 * q + 4, :].bitcast(I32)
-            )
+        load_plane(tab_plane, tab_scales[0])
+
+        x_rows = x.rearrange("(p i) m -> p i m", i=PACK)
+        x_raw = {}
+
+        def load_x(k):
+            lo, hi = CHUNKS[k]
+            x_raw[k] = held([P, PACK, hi - lo], F32, f"x_raw{k}")
+            nc.sync.dma_start(x_raw[k][:], x_rows[:, :, lo:hi])
+
         load_x(0)
 
-        g_rows = keep.tile([P, PASSES * P], F32, name="g_rows")
+        g_rows = held([P, PASSES * P], F32, "g_rows")
         nc.vector.memset(g_rows[:], 0.0)
         nc.sync.dma_start(
-            g_rows[:PACK, :].rearrange("t (s r) -> t s r", r=RUN), g.rearrange("(s t r) -> t s r", t=PACK, r=RUN)
+            g_rows[:PACK, :].rearrange("t (q r) -> t q r", r=RUN), g.rearrange("(q t r) -> t q r", t=PACK, r=RUN)
         )
 
-        wd_view = wdT.rearrange("(p s) c -> p s c", s=PACK)
-        pair_raw = []
+        wd_rows = wdT.rearrange("(p s) c -> p s c", s=PACK)
+        pair_raw = {}
         wd_raw = {}
 
-        def load_pair(n):
-            raw = keep.tile([P, 2, T // 2], F32, name=f"pair_raw{n}", align_bytes=64)
-            nc.sync.dma_start(raw[:], wd_view[:, 0:2, n * T // 2 : (n + 1) * T // 2])
-            pair_raw.append(raw)
+        def load_wd_pair_half(half):
+            pair_raw[half] = held([P, 2, T // 2], F32, f"pair_raw{half}")
+            nc.sync.dma_start(pair_raw[half][:], wd_rows[:, 0:2, half * T // 2 : (half + 1) * T // 2])
 
-        w4_raw = keep.tile([P, 2 * N], U8, name="w4_raw", align_bytes=64)
-        w4_plane_raw = keep.tile([P, N], U8, name="w4_plane_raw", align_bytes=64)
+        def load_wd_rows(s):
+            wd_raw[s] = held([P, T], F32, f"wd_raw{s}")
+            nc.sync.dma_start(wd_raw[s][:], wd_rows[:, s, :])
+
+        w4_raw = held([P, 2 * N], U8, "w4_raw")
+        w4_plane_raw = held([P, N], U8, "w4_plane_raw")
 
         def load_w4():
             nc.sync.dma_start(w4_raw[:].bitcast(I32), w4_words[0].bitcast(I32))
             nc.gpsimd.memset(w4_plane_raw[:].bitcast(I32), 0)
-            for q in range(4):
-                nc.sync.dma_start(
-                    w4_plane_raw[32 * q : 32 * q + 4, :].bitcast(I32), w4_scales[0, 4 * q : 4 * q + 4, :].bitcast(I32)
-                )
+            load_plane(w4_plane_raw, w4_scales[0])
 
-        def load_wd(s):
-            wd_raw[s] = keep.tile([P, T], F32, name=f"wd_raw{s}", align_bytes=64)
-            nc.sync.dma_start(wd_raw[s][:], wd_view[:, s, :])
-
-        load_pair(0)
-        load_wd(2)
-        load_pair(1)
+        load_wd_pair_half(0)
+        load_wd_rows(2)
+        load_wd_pair_half(1)
         load_x(1)
-        load_wd(3)
+        load_wd_rows(3)
         load_x(2)
-        load_x(3)
         load_w4()
 
-        ident_f32 = keep.tile([P, P], F32, name="ident_f32")
+        ident_f32 = held([P, P], F32, "ident_f32")
         make_identity(nc, ident_f32[:])
-        ident_bf = keep.tile([P, P], BF16, name="ident_bf")
+        ident_bf = held([P, P], BF16, "ident_bf")
         make_identity(nc, ident_bf[:])
 
-        picked_plane = keep.tile([P, S], U8, name="picked_plane", align_bytes=64)
+        def dealt(tile):
+            return tile[:].rearrange("p (t q r) -> p q t r", t=PACK, r=RUN)
+
+        def stationary(b, t):
+            return slice((t * PASSES + b) * P, (t * PASSES + b + 1) * P)
+
+        picked_plane = held([P, S], U8, "picked_plane")
         nc.vector.tensor_copy(picked_plane[:], tab_plane[:].indirect(offsets[:]))
-        v_plane = keep.tile([P, S], U8, name="v_plane", align_bytes=64)
-        v_codes = keep.tile([P, S], U32, name="v_codes", align_bytes=64)
+        v_codes = held([P, S], U32, "v_codes")
+        nc.vector.tensor_copy(dealt(v_codes), tab_codes[:].indirect(offsets[:]))
+        v_plane = held([P, S], U8, "v_plane")
         nc.vector.tensor_copy(
-            v_codes[:].rearrange("p (t s r) -> p s t r", t=PACK, r=RUN), tab_codes[:].indirect(offsets[:])
-        )
-        nc.vector.tensor_copy(
-            v_plane[:].bitcast(I32).rearrange("p (t s w) -> p t s w", t=PACK, w=RUN // 4),
-            picked_plane[:].bitcast(I32).rearrange("p (s t w) -> p t s w", t=PACK, w=RUN // 4),
+            v_plane[:].bitcast(I32).rearrange("p (t q w) -> p t q w", t=PACK, w=RUN // 4),
+            picked_plane[:].bitcast(I32).rearrange("p (q t w) -> p t q w", t=PACK, w=RUN // 4),
         )
 
         g_bank = y_psum.tile([P, PASSES, P], F32, name="g_bank", tag="y")
         for b in range(PASSES):
             nc.tensor.transpose(g_bank[:, b, :], g_rows[:, b * P : (b + 1) * P], ident_f32[:])
-        gain = keep.tile([P, PASSES * PACK], F32, name="gain")
-        nc.scalar.copy(gain[:].rearrange("p (b t) -> p b t", t=PACK), g_bank[:, :, :PACK])
+        gain = held([P, PASSES, PACK], F32, "gain")
+        nc.scalar.copy(gain[:], g_bank[:, :, :PACK])
 
-        x_codes = keep.tile([P, M], U32, name="x_codes", align_bytes=64)
-        x_plane = keep.tile([P, M], U8, name="x_plane", align_bytes=64)
+        x_codes = {}
+        x_plane = held([P, M], U8, "x_plane")
         x_bf = {}
 
-        def round_x(k):
-            x_bf[k] = keep.tile([P, CHUNK * PACK], BF16, name=f"x_bf{k}", tag=TAG.get(f"x_bf{k}", f"x_bf{k}"), align_bytes=64)
+        def round_x(k, after=None):
+            lo, hi = CHUNKS[k]
+            x_bf[k] = held([P, (hi - lo) * PACK], BF16, f"x_bf{k}", after)
             nc.scalar.copy(
                 x_bf[k][:].rearrange("p (c e i) -> p c i e", e=2, i=PACK),
-                x_raw[k].rearrange("p i (c e) -> p c i e", e=2),
+                x_raw[k][:].rearrange("p i (c e) -> p c i e", e=2),
             )
 
-        def quantize_x(k):
-            cols = slice(k * CHUNK, (k + 1) * CHUNK)
-            nc.vector.quantize_mx(out=x_codes[:, cols].bitcast(FP8X4), scales=x_plane[:, cols], in_=x_bf[k][:])
+        def quantize_x(k, after=None):
+            lo, hi = CHUNKS[k]
+            codes = held([P, hi - lo], U32, f"x_codes{k}", after)
+            nc.vector.quantize_mx(out=codes[:].bitcast(FP8X4), scales=x_plane[:, lo:hi], in_=x_bf[k][:])
+            for m0 in range(lo, hi, BANK_M):
+                x_codes[m0] = codes[:, m0 - lo : m0 - lo + BANK_M]
 
-        wd_codes = keep.tile([P, PACK, PASSES * P], U32, name="wd_codes", align_bytes=64)
-        wd_plane = keep.tile([P, PACK, PASSES * P], U8, name="wd_plane", align_bytes=64)
-        wd_bf = [keep.tile([P, 2, PASSES, P, PACK], BF16, name=f"wd_bf{n}", align_bytes=64) for n in range(2)]
+        wd_codes = held([P, PACK, PASSES * P], U32, "wd_codes")
+        wd_plane = held([P, PACK, PASSES * P], U8, "wd_plane")
+        wd_bf = [held([P, 2, PASSES, P, PACK], BF16, f"wd_bf{pair}") for pair in range(2)]
+        pair_words = held([P, T], U32, "pair_words")
 
-        def gather_wd(s):
-            picked = keep.tile([P, S], BF16, name=f"picked{s}", tag=TAG.get(f"picked{s}", f"picked{s}"), align_bytes=64)
-            nc.vector.tensor_copy(
-                picked[:].rearrange("p (t s r) -> p s t r", t=PACK, r=RUN), wd_raw[s][:].indirect(offsets[:])
-            )
+        def gather_wd_rows(s, after=None):
+            picked = held([P, S], BF16, f"picked{s}", after)
+            nc.vector.tensor_copy(dealt(picked), wd_raw[s][:].indirect(offsets[:]))
             turned = y_psum.tile([P, PASSES, PACK, P], BF16, name="turned", tag="y")
             for b in range(PASSES):
                 for t in range(PACK):
-                    c0 = (t * PASSES + b) * P
-                    nc.tensor.transpose(turned[:, b, t, :], picked[:, c0 : c0 + P], ident_bf[:])
+                    nc.tensor.transpose(turned[:, b, t, :], picked[:, stationary(b, t)], ident_bf[:])
             nc.scalar.copy(wd_bf[1][:, s - 2, :, :, :], turned[:].rearrange("p b t n -> p b n t"))
 
-        pair_words = keep.tile([P, T], U32, name="pair_words", align_bytes=64)
-
-        def round_pair(n):
+        def round_wd_pair_half(half):
+            cols = slice(half * T // 2, (half + 1) * T // 2)
             nc.scalar.copy(
-                pair_words[:, n * T // 2 : (n + 1) * T // 2].bitcast(BF16).rearrange("p (c e) -> p c e", e=2),
-                pair_raw[n][:].rearrange("p e c -> p c e"),
+                pair_words[:, cols].bitcast(BF16).rearrange("p (c e) -> p c e", e=2),
+                pair_raw[half][:].rearrange("p e c -> p c e"),
             )
 
-        def gather_pair():
-            picked = keep.tile([P, S], U32, name="pair_picked", tag=TAG.get("pair_picked", "pair_picked"), align_bytes=64)
-            nc.vector.tensor_copy(
-                picked[:].rearrange("p (t s r) -> p s t r", t=PACK, r=RUN), pair_words[:].indirect(offsets[:])
-            )
+        def gather_wd_pair(after=None):
+            picked = held([P, S], U32, "pair_picked", after)
+            nc.vector.tensor_copy(dealt(picked), pair_words[:].indirect(offsets[:]))
             for b in range(PASSES):
                 turned = y_psum.tile([P, PACK, P], F32, name="turned_pair", tag="y")
                 for t in range(PACK):
-                    c0 = (t * PASSES + b) * P
-                    nc.tensor.transpose(turned[:, t, :], picked[:, c0 : c0 + P].bitcast(F32), ident_f32[:])
+                    nc.tensor.transpose(turned[:, t, :], picked[:, stationary(b, t)].bitcast(F32), ident_f32[:])
                 nc.scalar.copy(
-                    wd_bf[0][:, :, b, :, :],
-                    turned[:].bitcast(BF16).rearrange("p t (n e) -> p e n t", e=2),
+                    wd_bf[0][:, :, b, :, :], turned[:].bitcast(BF16).rearrange("p t (n e) -> p e n t", e=2)
                 )
 
         def quantize_wd(pair):
+            rows = slice(2 * pair, 2 * pair + 2)
             nc.vector.quantize_mx(
-                out=wd_codes[:, 2 * pair : 2 * pair + 2, :].rearrange("p s c -> p (s c)").bitcast(FP8X4),
-                scales=wd_plane[:, 2 * pair : 2 * pair + 2, :].rearrange("p s c -> p (s c)"),
+                out=wd_codes[:, rows, :].rearrange("p s c -> p (s c)").bitcast(FP8X4),
+                scales=wd_plane[:, rows, :].rearrange("p s c -> p (s c)"),
                 in_=wd_bf[pair][:].rearrange("p s b n t -> p (s b n t)"),
             )
 
-        w4 = {}
-
-        def deal_w4():
-            w4_codes = keep.tile([P, PACK, P, 2], U8, name="w4_codes", tag=TAG.get("w4_codes", "w4_codes"), align_bytes=64)
-            w4_plane = keep.tile([P, PACK, P], U8, name="w4_plane", tag=TAG.get("w4_plane", "w4_plane"), align_bytes=64)
-            w4["codes"] = w4_codes
-            w4["plane"] = w4_plane
-            nc.vector.tensor_copy(w4_codes[:], w4_raw[:].rearrange("p (n s e) -> p s n e", s=PACK, e=2))
-            nc.vector.tensor_copy(w4_plane[:], w4_plane_raw[:].rearrange("p (n s) -> p s n", s=PACK))
+        def deal_w4(a1, a2):
+            codes = held([P, PACK, 2 * P], U8, "w4_codes", a1)
+            plane = held([P, PACK, P], U8, "w4_plane", a2)
+            nc.vector.tensor_copy(codes[:].bitcast(U16), w4_raw[:].bitcast(U16).rearrange("p (n s) -> p s n", s=PACK))
+            nc.vector.tensor_copy(plane[:], w4_plane_raw[:].rearrange("p (n s) -> p s n", s=PACK))
+            return codes, plane
 
         a_banks = {}
         lifted = {}
         gated = {}
         h_bf = {}
-        h_codes = {}
-        h_plane = {}
+        h_codes = [held([P, M], U32, f"h_codes{b}") for b in range(PASSES)]
+        h_plane = [held([P, M], U8, f"h_plane{b}") for b in range(PASSES)]
 
-        def project(u):
-            k, b = divmod(u, PASSES)
-            if k in LIFT:
-                if b == 0:
-                    both = keep.tile([P, PASSES, PACK, CHUNK], F32, name=f"lifted{k}", tag=LIFT[k], align_bytes=64)
-                    lifted[u], lifted[u + 1] = both[:, 0, :, :], both[:, 1, :, :]
-            else:
-                lifted[u] = ring.tile([P, PACK, CHUNK], F32, name="lifted")
-            for half in range(CHUNK // BANK_M):
+        def project(k, b, into=None):
+            lo, hi = CHUNKS[k]
+            lifted[k, b] = ring.tile([P, PACK, hi - lo], F32, name="lifted")[:] if into is None else into
+            for m0 in range(lo, hi, BANK_M):
                 bank = a_psum.tile([P, PACK, BANK_M], F32, name="a_bank")
-                a_banks[u, half] = bank
-                cols = slice(k * CHUNK + half * BANK_M, k * CHUNK + (half + 1) * BANK_M)
+                a_banks[b, m0] = bank
+                cols = slice(m0, m0 + BANK_M)
                 for t in range(PACK):
-                    c0 = (t * PASSES + b) * P
                     nc.tensor.matmul_mx(
                         out=bank[:, t, :],
-                        lhsT=v_codes[:, c0 : c0 + P].bitcast(FP8X4),
-                        lhsT_scale=v_plane[:, c0 : c0 + P],
-                        rhs=x_codes[:, cols].bitcast(FP8X4),
+                        lhsT=v_codes[:, stationary(b, t)].bitcast(FP8X4),
+                        lhsT_scale=v_plane[:, stationary(b, t)],
+                        rhs=x_codes[m0].bitcast(FP8X4),
                         rhs_scale=x_plane[:, cols],
                         start=True,
                         stop=True,
                     )
-                nc.scalar.activation(
-                    lifted[u][:, :, half * BANK_M : (half + 1) * BANK_M], bank[:], ACT.Relu, bias=3.0
-                )
+                nc.scalar.activation(lifted[k, b][:, :, m0 - lo : m0 - lo + BANK_M], bank[:], ACT.Relu, bias=3.0)
 
-        def gate(u):
-            b = u % PASSES
-            if f"gated{u}" in TAG:
-                gated[u] = keep.tile([P, PACK, CHUNK], F32, name=f"gated{u}", tag=TAG[f"gated{u}"], align_bytes=64)
-            else:
-                gated[u] = ring.tile([P, PACK, CHUNK], F32, name="gated")
+        def gate(k, b, into=None):
+            lo, hi = CHUNKS[k]
+            gated[k, b] = ring.tile([P, PACK, hi - lo], F32, name="gated")[:] if into is None else into
             for t in range(PACK):
-                col = b * PACK + t
                 nc.vector.tensor_scalar(
-                    gated[u][:, t, :], lifted[u][:, t, :], 6.0, gain[:, col : col + 1], ALU.min, ALU.mult
+                    gated[k, b][:, t, :], lifted[k, b][:, t, :], 6.0, gain[:, b, t : t + 1], ALU.min, ALU.mult
                 )
 
-        def swish(u, *halves):
-            if u not in h_bf:
-                if u < 2:
-                    h_bf[u] = keep.tile([P, CHUNK * PACK], BF16, name=f"h_first{u}", align_bytes=64)
-                else:
-                    h_bf[u] = ring.tile([P, CHUNK * PACK], BF16, name="h_bf", align_bytes=64)
-            for half in halves or range(CHUNK // BANK_M):
-                lo = half * BANK_M
+        def swish(k, b, lo, hi):
+            base, end = CHUNKS[k]
+            if lo == base:
+                h_bf[k, b] = held([P, (end - base) * PACK], BF16, f"h_bf{k}{b}")
+            for m0 in range(lo, hi, BANK_M):
+                c0 = m0 - base
                 nc.vector.tensor_tensor(
-                    h_bf[u][:, lo * PACK : (lo + BANK_M) * PACK].rearrange("p (c e t) -> p c t e", e=2, t=PACK),
-                    a_banks[u, half][:].rearrange("p t (c e) -> p c t e", e=2),
-                    gated[u][:, :, lo : lo + BANK_M].rearrange("p t (c e) -> p c t e", e=2),
+                    h_bf[k, b][:, c0 * PACK : (c0 + BANK_M) * PACK].rearrange("p (c e t) -> p c t e", e=2, t=PACK),
+                    a_banks[b, m0][:].rearrange("p t (c e) -> p c t e", e=2),
+                    gated[k, b][:, :, c0 : c0 + BANK_M].rearrange("p t (c e) -> p c t e", e=2),
                     ALU.mult,
                 )
 
-        def quantize_h(u, lo=0, hi=CHUNK):
-            if lo == 0:
-                h_codes[u] = keep.tile([P, CHUNK], U32, name=f"h_codes{u}", align_bytes=64)
-                h_plane[u] = keep.tile([P, CHUNK], U8, name=f"h_plane{u}", align_bytes=64)
+        def quantize_h(k, b, lo, hi):
+            base = CHUNKS[k][0]
             nc.vector.quantize_mx(
-                out=h_codes[u][:, lo:hi].bitcast(FP8X4),
-                scales=h_plane[u][:, lo:hi],
-                in_=h_bf[u][:, lo * PACK : hi * PACK],
+                out=h_codes[b][:, lo:hi].bitcast(FP8X4),
+                scales=h_plane[b][:, lo:hi],
+                in_=h_bf[k, b][:, (lo - base) * PACK : (hi - base) * PACK],
             )
 
-        y_codes = keep.tile([P, M], U32, name="y_codes", align_bytes=64)
-        y_plane = keep.tile([P, M], U8, name="y_plane", align_bytes=64)
-        y_view = out_0.rearrange("(p s) m -> p s m", s=PACK)
-        y_words = out_1[0].rearrange("p m t -> p (m t)")
-        y_bf = {}
-
-        y_f32 = {}
+        y_f32 = [held([P, PACK, STRIP], F32, f"y_f32_{n}") for n in range(M // STRIP)]
+        y_bf = held([P, M, PACK], BF16, "y_bf")
+        y_codes = held([P, M], U32, "y_codes")
+        y_plane = held([P, M], U8, "y_plane")
+        y_rows = out_0.rearrange("(p s) m -> p s m", s=PACK)
+        y_words = out_1[0].rearrange("p m s -> p (m s)")
         y_banks = {}
 
-        def down(k, half):
-            if half == 0:
-                y_f32[k] = ring.tile([P, PACK, CHUNK], F32, name="y_f32")
-                y_bf[k] = ring.tile([P, CHUNK, PACK], BF16, name="y_bf", align_bytes=64)
-            lo = half * BANK_M
+        def down(m0):
             bank = y_psum.tile([P, PACK, BANK_M], F32, name="y_bank", tag="y")
-            y_banks[k, half] = bank
-            cols = slice(k * CHUNK + lo, k * CHUNK + lo + BANK_M)
+            y_banks[m0] = bank
+            cols = slice(m0, m0 + BANK_M)
             for s in range(PACK):
                 nc.tensor.matmul_mx(
                     out=bank[:, s, :],
-                    lhsT=w4["codes"][:, s, :, :].rearrange("p n e -> p (n e)").bitcast(FP4X4),
-                    lhsT_scale=w4["plane"][:, s, :],
-                    rhs=x_codes[:, cols].bitcast(FP8X4),
+                    lhsT=w4_codes[:, s, :].bitcast(FP4X4),
+                    lhsT_scale=w4_plane[:, s, :],
+                    rhs=x_codes[m0].bitcast(FP8X4),
                     rhs_scale=x_plane[:, cols],
                     start=(s == 0),
                     stop=False,
                 )
             for b in range(PASSES):
-                u = k * PASSES + b
                 for s in range(PACK):
                     nc.tensor.matmul_mx(
                         out=bank[:, s, :],
                         lhsT=wd_codes[:, s, b * P : (b + 1) * P].bitcast(FP8X4),
                         lhsT_scale=wd_plane[:, s, b * P : (b + 1) * P],
-                        rhs=h_codes[u][:, lo : lo + BANK_M].bitcast(FP8X4),
-                        rhs_scale=h_plane[u][:, lo : lo + BANK_M],
+                        rhs=h_codes[b][:, cols].bitcast(FP8X4),
+                        rhs_scale=h_plane[b][:, cols],
                         start=False,
                         stop=(b == PASSES - 1 and s == PACK - 1),
                     )
-            nc.scalar.copy(y_bf[k][:, lo : lo + BANK_M, :], bank[:].rearrange("p s m -> p m s"))
+            nc.scalar.copy(y_bf[:, cols, :], bank[:].rearrange("p s m -> p m s"))
 
-        def copy_y(k, half, copy):
-            lo = half * BANK_M
-            copy(y_f32[k][:, :, lo : lo + BANK_M], y_banks[k, half][:])
+        def copy_y(m0, copy):
+            c0 = m0 % STRIP
+            copy(y_f32[m0 // STRIP][:, :, c0 : c0 + BANK_M], y_banks[m0][:])
 
-        def store_y(k, lo=0, hi=CHUNK):
-            nc.sync.dma_start(y_view[:, :, k * CHUNK + lo : k * CHUNK + hi], y_f32[k][:, :, lo:hi])
+        def store_y(lo, hi, queue):
+            c0 = lo % STRIP
+            queue.dma_start(y_rows[:, :, lo:hi], y_f32[lo // STRIP][:, :, c0 : c0 + hi - lo])
 
-        def quantize_y(k, lo=0, hi=CHUNK):
-            cols = slice(k * CHUNK + lo, k * CHUNK + hi)
+        def down_strip(lo):
+            for m0 in range(lo, lo + STRIP, BANK_M):
+                down(m0)
+                copy_y(m0, nc.scalar.copy)
+            store_y(lo, lo + STRIP, nc.sync)
+
+        def quantize_y(lo, hi):
             nc.vector.quantize_mx(
-                out=y_codes[:, cols].bitcast(FP8X4),
-                scales=y_plane[:, cols],
-                in_=y_bf[k][:, lo:hi, :].rearrange("p m s -> p (m s)"),
-            )
-            nc.sync.dma_start(
-                y_words[:, cols.start * PACK : cols.stop * PACK].bitcast(I32), y_codes[:, cols].bitcast(I32)
+                out=y_codes[:, lo:hi].bitcast(FP8X4),
+                scales=y_plane[:, lo:hi],
+                in_=y_bf[:, lo:hi, :].rearrange("p m s -> p (m s)"),
             )
 
-        def down_whole(k):
-            for half in range(CHUNK // BANK_M):
-                down(k, half)
-                copy_y(k, half, nc.scalar.copy)
-            store_y(k)
+        def store_words(lo, hi):
+            nc.sync.dma_start(y_words[:, lo * PACK : hi * PACK].bitcast(I32), y_codes[:, lo:hi].bitcast(I32))
 
         round_x(0)
         quantize_x(0)
-        round_pair(0)
-        project(0)
-        project(1)
-        gather_wd(2)
-        round_pair(1)
-        gate(0)
-        swish(0)
-        round_x(1)
-        gate(1)
-        quantize_h(0)
-        swish(1)
-        quantize_x(1)
-        gather_pair()
-        project(2)
-        project(3)
-        quantize_h(1)
-        gather_wd(3)
-        round_x(2)
-        gate(2)
-        quantize_wd(0)
-        quantize_x(2)
-        deal_w4()
+        round_wd_pair_half(0)
+        first_lifted = held([P, PASSES, PACK, STRIP], F32, "first_lifted", "pair_raw0")
+        project(0, 0, first_lifted[:, 0, :, :])
+        project(0, 1, first_lifted[:, 1, :, :])
+        gather_wd_rows(2)
+        round_wd_pair_half(1)
+        first_gated = held([P, PASSES, PACK, STRIP], F32, "first_gated", "wd_raw2")
+        gate(0, 0, first_gated[:, 0, :, :])
+        swish(0, 0, 0, 256)
+        round_x(1, "picked2")
+        gate(0, 1, first_gated[:, 1, :, :])
+        quantize_h(0, 0, 0, 256)
+        swish(0, 1, 0, 256)
+        gather_wd_rows(3, "h_bf00")
+        quantize_x(1, "wd_raw3")
+        project(1, 0)
+        gather_wd_pair("picked2")
+        quantize_h(0, 1, 0, 256)
+        project(1, 1)
+        round_x(2, "x_raw1")
+        w4_codes, w4_plane = deal_w4("pair_words", "h_bf01")
+        gate(1, 0)
         quantize_wd(1)
-        round_x(3)
-        units = CHUNKS * PASSES
-        for u in range(2, units - 1):
-            k, b = divmod(u, PASSES)
-            if u + 2 < units:
-                project(u + 2)
-            if b == 0:
-                down_whole(k - 1)
-            swish(u)
-            if u == 3:
-                quantize_x(3)
-            gate(u + 1)
-            quantize_h(u)
-            if b == 1:
-                quantize_y(k - 1)
-        last = CHUNKS - 1
-        swish(units - 1, 0)
-        quantize_y(last - 1)
-        quantize_h(units - 1, 0, BANK_M)
-        down(last, 0)
-        swish(units - 1, 1)
-        quantize_h(units - 1, BANK_M, CHUNK)
-        down(last, 1)
-        quantize_y(last, 0, BANK_M)
-        copy_y(last, 0, nc.vector.tensor_copy)
-        store_y(last, 0, BANK_M)
-        quantize_y(last, BANK_M, CHUNK)
-        copy_y(last, 1, nc.scalar.copy)
-        store_y(last, BANK_M, CHUNK)
-        for q in range(4):
-            queue = nc.sync if q % 2 == 0 else nc.scalar
+        quantize_wd(0)
+        swish(1, 0, 256, 768)
+        down_strip(0)
+        quantize_x(2)
+        project(2, 0)
+        gate(1, 1)
+        quantize_h(1, 0, 256, 768)
+        project(2, 1)
+        swish(1, 1, 256, 512)
+        quantize_y(0, 256)
+        store_words(0, 256)
+        quantize_h(1, 1, 256, 512)
+        down_strip(256)
+        swish(1, 1, 512, 768)
+        gate(2, 0)
+        quantize_h(1, 1, 512, 768)
+        down_strip(512)
+        swish(2, 0, 768, 1024)
+        gate(2, 1)
+        quantize_h(2, 0, 768, 1024)
+        swish(2, 1, 768, 896)
+        quantize_y(256, 512)
+        quantize_h(2, 1, 768, 896)
+        down(768)
+        swish(2, 1, 896, 1024)
+        quantize_h(2, 1, 896, 1024)
+        down(896)
+        quantize_y(512, 768)
+        store_words(256, 768)
+        copy_y(768, nc.vector.tensor_copy)
+        store_y(768, 896, nc.sync)
+        quantize_y(768, 1024)
+        store_words(768, 1024)
+        copy_y(896, nc.scalar.copy)
+        store_y(896, 1024, nc.scalar)
+        for q in range(QUADRANTS):
+            queue = nc.sync if q < QUADRANTS // 2 else nc.scalar
             queue.dma_start(
                 out_2[0, 4 * q : 4 * q + 4, :].bitcast(I32), y_plane[32 * q : 32 * q + 4, :].bitcast(I32)
             )

@@ -46,10 +46,12 @@ def tile_list_listed_hardswish_bottleneck_kernel(
                     plane[32 * q : 32 * q + 4, :].bitcast(I32), scale_rows[4 * q : 4 * q + 4, :].bitcast(I32)
                 )
 
-        tab_codes = held([P, T], U32, "tab_codes")
-        nc.sync.dma_start(tab_codes[:].bitcast(I32), tab_words[0].rearrange("p c i -> p (c i)").bitcast(I32))
         offsets = keep.tile([P, S // 16], U16, name="offsets")
         nc.sync.dma_start(offsets[:], offs)
+        w4_raw = held([P, 2 * N], U8, "w4_raw")
+        nc.sync.dma_start(w4_raw[:].bitcast(I32), w4_words[0].bitcast(I32))
+        tab_codes = held([P, T], U32, "tab_codes")
+        nc.sync.dma_start(tab_codes[:].bitcast(I32), tab_words[0].rearrange("p c i -> p (c i)").bitcast(I32))
 
         tab_plane = held([P, T], U8, "tab_plane")
         nc.vector.memset(tab_plane[:].bitcast(I32), 0)
@@ -58,18 +60,9 @@ def tile_list_listed_hardswish_bottleneck_kernel(
         x_rows = x.rearrange("(p i) m -> p i m", i=PACK)
         x_raw = {}
 
-        def load_x(k):
-            lo, hi = CHUNKS[k]
-            x_raw[k] = held([P, PACK, hi - lo], F32, f"x_raw{k}")
-            nc.sync.dma_start(x_raw[k][:], x_rows[:, :, lo:hi])
-
-        load_x(0)
-
-        g_rows = held([P, PASSES * P], F32, "g_rows")
-        nc.vector.memset(g_rows[:], 0.0)
-        nc.sync.dma_start(
-            g_rows[:PACK, :].rearrange("t (q r) -> t q r", r=RUN), g.rearrange("(q t r) -> t q r", t=PACK, r=RUN)
-        )
+        def load_x(n):
+            x_raw[n] = held([P, PACK, STRIP], F32, f"x_raw{n}")
+            nc.sync.dma_start(x_raw[n][:], x_rows[:, :, n * STRIP : (n + 1) * STRIP])
 
         wd_rows = wdT.rearrange("(p s) c -> p s c", s=PACK)
         pair_raw = {}
@@ -83,21 +76,22 @@ def tile_list_listed_hardswish_bottleneck_kernel(
             wd_raw[s] = held([P, T], F32, f"wd_raw{s}")
             nc.sync.dma_start(wd_raw[s][:], wd_rows[:, s, :])
 
-        w4_raw = held([P, 2 * N], U8, "w4_raw")
-        w4_plane_raw = held([P, N], U8, "w4_plane_raw")
-
-        def load_w4():
-            nc.sync.dma_start(w4_raw[:].bitcast(I32), w4_words[0].bitcast(I32))
-            nc.gpsimd.memset(w4_plane_raw[:].bitcast(I32), 0)
-            load_plane(w4_plane_raw, w4_scales[0])
-
-        load_wd_pair_half(0)
-        load_wd_rows(2)
-        load_wd_pair_half(1)
+        load_x(0)
+        g_rows = held([P, PASSES * P], F32, "g_rows")
+        nc.gpsimd.memset(g_rows[:], 0.0)
+        nc.sync.dma_start(
+            g_rows[:PACK, :].rearrange("t (q r) -> t q r", r=RUN), g.rearrange("(q t r) -> t q r", t=PACK, r=RUN)
+        )
         load_x(1)
-        load_wd_rows(3)
         load_x(2)
-        load_w4()
+        load_wd_rows(2)
+        load_wd_pair_half(0)
+        load_wd_pair_half(1)
+        load_wd_rows(3)
+        w4_plane_raw = held([P, N], U8, "w4_plane_raw")
+        nc.gpsimd.memset(w4_plane_raw[:].bitcast(I32), 0)
+        load_plane(w4_plane_raw, w4_scales[0])
+        load_x(3)
 
         ident_f32 = held([P, P], F32, "ident_f32")
         make_identity(nc, ident_f32[:])
@@ -110,45 +104,51 @@ def tile_list_listed_hardswish_bottleneck_kernel(
         def stationary(b, t):
             return slice((t * PASSES + b) * P, (t * PASSES + b + 1) * P)
 
-        picked_plane = held([P, S], U8, "picked_plane")
-        nc.vector.tensor_copy(picked_plane[:], tab_plane[:].indirect(offsets[:]))
+        w4_codes = held([P, PACK, 2 * P], U8, "w4_codes")
+        nc.vector.tensor_copy(
+            w4_codes[:].bitcast(U16), w4_raw[:].bitcast(U16).rearrange("p (n s) -> p s n", s=PACK)
+        )
         v_codes = held([P, S], U32, "v_codes")
         nc.vector.tensor_copy(dealt(v_codes), tab_codes[:].indirect(offsets[:]))
+        picked_plane = held([P, S], U8, "picked_plane", "tab_codes")
+        nc.vector.tensor_copy(picked_plane[:], tab_plane[:].indirect(offsets[:]))
         v_plane = held([P, S], U8, "v_plane")
         nc.vector.tensor_copy(
             v_plane[:].bitcast(I32).rearrange("p (t q w) -> p t q w", t=PACK, w=RUN // 4),
             picked_plane[:].bitcast(I32).rearrange("p (q t w) -> p t q w", t=PACK, w=RUN // 4),
         )
 
-        g_bank = y_psum.tile([P, PASSES, P], F32, name="g_bank", tag="y")
-        for b in range(PASSES):
-            nc.tensor.transpose(g_bank[:, b, :], g_rows[:, b * P : (b + 1) * P], ident_f32[:])
         gain = held([P, PASSES, PACK], F32, "gain")
-        nc.scalar.copy(gain[:], g_bank[:, :, :PACK])
+
+        def turn_gain():
+            g_bank = y_psum.tile([P, PASSES, P], F32, name="g_bank", tag="y")
+            for b in range(PASSES):
+                nc.tensor.transpose(g_bank[:, b, :], g_rows[:, b * P : (b + 1) * P], ident_f32[:])
+            nc.scalar.copy(gain[:], g_bank[:, :, :PACK])
 
         x_codes = {}
         x_plane = held([P, M], U8, "x_plane")
         x_bf = {}
 
-        def round_x(k, after=None):
-            lo, hi = CHUNKS[k]
-            x_bf[k] = held([P, (hi - lo) * PACK], BF16, f"x_bf{k}", after)
-            nc.scalar.copy(
-                x_bf[k][:].rearrange("p (c e i) -> p c i e", e=2, i=PACK),
-                x_raw[k][:].rearrange("p i (c e) -> p c i e", e=2),
+        def round_x(n, copy, after=None):
+            x_bf[n] = held([P, STRIP * PACK], BF16, f"x_bf{n}", after)
+            copy(
+                x_bf[n][:].rearrange("p (c e i) -> p c i e", e=2, i=PACK),
+                x_raw[n][:].rearrange("p i (c e) -> p c i e", e=2),
             )
 
-        def quantize_x(k, after=None):
-            lo, hi = CHUNKS[k]
-            codes = held([P, hi - lo], U32, f"x_codes{k}", after)
-            nc.vector.quantize_mx(out=codes[:].bitcast(FP8X4), scales=x_plane[:, lo:hi], in_=x_bf[k][:])
-            for m0 in range(lo, hi, BANK_M):
-                x_codes[m0] = codes[:, m0 - lo : m0 - lo + BANK_M]
+        def quantize_x(n, after=None):
+            lo = n * STRIP
+            codes = held([P, STRIP], U32, f"x_codes{n}", after)
+            nc.vector.quantize_mx(out=codes[:].bitcast(FP8X4), scales=x_plane[:, lo : lo + STRIP], in_=x_bf[n][:])
+            for c0 in range(0, STRIP, BANK_M):
+                x_codes[lo + c0] = codes[:, c0 : c0 + BANK_M]
 
         wd_codes = held([P, PACK, PASSES * P], U32, "wd_codes")
         wd_plane = held([P, PACK, PASSES * P], U8, "wd_plane")
-        wd_bf = [held([P, 2, PASSES, P, PACK], BF16, f"wd_bf{pair}") for pair in range(2)]
-        pair_words = held([P, T], U32, "pair_words")
+        wd_bf = {}
+        turned_rows = {}
+        pair_words = {}
 
         def gather_wd_rows(s, after=None):
             picked = held([P, S], BF16, f"picked{s}", after)
@@ -157,18 +157,26 @@ def tile_list_listed_hardswish_bottleneck_kernel(
             for b in range(PASSES):
                 for t in range(PACK):
                     nc.tensor.transpose(turned[:, b, t, :], picked[:, stationary(b, t)], ident_bf[:])
-            nc.scalar.copy(wd_bf[1][:, s - 2, :, :, :], turned[:].rearrange("p b t n -> p b n t"))
+            turned_rows[s] = turned
 
-        def round_wd_pair_half(half):
+        def copy_wd_rows(s):
+            if s == 2:
+                wd_bf[1] = held([P, 2, PASSES, P, PACK], BF16, "wd_bf1", "pair_raw0")
+            nc.scalar.copy(wd_bf[1][:, s - 2, :, :, :], turned_rows[s][:].rearrange("p b t n -> p b n t"))
+
+        def round_wd_pair_half(half, after=None):
             cols = slice(half * T // 2, (half + 1) * T // 2)
+            if half == 0:
+                pair_words[0] = held([P, T], U32, "pair_words", after)
             nc.scalar.copy(
-                pair_words[:, cols].bitcast(BF16).rearrange("p (c e) -> p c e", e=2),
+                pair_words[0][:, cols].bitcast(BF16).rearrange("p (c e) -> p c e", e=2),
                 pair_raw[half][:].rearrange("p e c -> p c e"),
             )
 
         def gather_wd_pair(after=None):
             picked = held([P, S], U32, "pair_picked", after)
-            nc.vector.tensor_copy(dealt(picked), pair_words[:].indirect(offsets[:]))
+            wd_bf[0] = held([P, 2, PASSES, P, PACK], BF16, "wd_bf0")
+            nc.vector.tensor_copy(dealt(picked), pair_words[0][:].indirect(offsets[:]))
             for b in range(PASSES):
                 turned = y_psum.tile([P, PACK, P], F32, name="turned_pair", tag="y")
                 for t in range(PACK):
@@ -185,12 +193,10 @@ def tile_list_listed_hardswish_bottleneck_kernel(
                 in_=wd_bf[pair][:].rearrange("p s b n t -> p (s b n t)"),
             )
 
-        def deal_w4(a1, a2):
-            codes = held([P, PACK, 2 * P], U8, "w4_codes", a1)
-            plane = held([P, PACK, P], U8, "w4_plane", a2)
-            nc.vector.tensor_copy(codes[:].bitcast(U16), w4_raw[:].bitcast(U16).rearrange("p (n s) -> p s n", s=PACK))
+        def deal_w4_plane(after):
+            plane = held([P, PACK, P], U8, "w4_plane", after)
             nc.vector.tensor_copy(plane[:], w4_plane_raw[:].rearrange("p (n s) -> p s n", s=PACK))
-            return codes, plane
+            return plane
 
         a_banks = {}
         lifted = {}
@@ -199,10 +205,11 @@ def tile_list_listed_hardswish_bottleneck_kernel(
         h_codes = [held([P, M], U32, f"h_codes{b}") for b in range(PASSES)]
         h_plane = [held([P, M], U8, f"h_plane{b}") for b in range(PASSES)]
 
-        def project(k, b, into=None):
+        def project(k, b, first=None, end=None, into=None):
             lo, hi = CHUNKS[k]
-            lifted[k, b] = ring.tile([P, PACK, hi - lo], F32, name="lifted")[:] if into is None else into
-            for m0 in range(lo, hi, BANK_M):
+            if first is None or first == lo:
+                lifted[k, b] = ring.tile([P, PACK, hi - lo], F32, name="lifted")[:] if into is None else into
+            for m0 in range(first or lo, end or hi, BANK_M):
                 bank = a_psum.tile([P, PACK, BANK_M], F32, name="a_bank")
                 a_banks[b, m0] = bank
                 cols = slice(m0, m0 + BANK_M)
@@ -306,38 +313,44 @@ def tile_list_listed_hardswish_bottleneck_kernel(
         def store_words(lo, hi):
             nc.sync.dma_start(y_words[:, lo * PACK : hi * PACK].bitcast(I32), y_codes[:, lo:hi].bitcast(I32))
 
-        round_x(0)
+        round_x(0, nc.scalar.copy)
         quantize_x(0)
-        round_wd_pair_half(0)
-        first_lifted = held([P, PASSES, PACK, STRIP], F32, "first_lifted", "pair_raw0")
-        project(0, 0, first_lifted[:, 0, :, :])
-        project(0, 1, first_lifted[:, 1, :, :])
-        gather_wd_rows(2)
-        round_wd_pair_half(1)
+        round_x(1, nc.scalar.copy)
+        round_x(2, nc.scalar.copy)
+        turn_gain()
+        project(0, 0)
+        project(0, 1)
+        gather_wd_rows(2, "tab_codes")
         first_gated = held([P, PASSES, PACK, STRIP], F32, "first_gated", "wd_raw2")
         gate(0, 0, first_gated[:, 0, :, :])
-        swish(0, 0, 0, 256)
-        round_x(1, "picked2")
         gate(0, 1, first_gated[:, 1, :, :])
-        quantize_h(0, 0, 0, 256)
+        round_wd_pair_half(0)
+        round_wd_pair_half(1)
+        swish(0, 0, 0, 256)
         swish(0, 1, 0, 256)
-        gather_wd_rows(3, "h_bf00")
-        quantize_x(1, "wd_raw3")
-        project(1, 0)
-        gather_wd_pair("picked2")
+        quantize_h(0, 0, 0, 256)
+        quantize_x(1, "tab_codes")
         quantize_h(0, 1, 0, 256)
-        project(1, 1)
-        round_x(2, "x_raw1")
-        w4_codes, w4_plane = deal_w4("pair_words", "h_bf01")
+        quantize_x(2, "h_bf00")
+        copy_wd_rows(2)
+        middle_lifted = held([P, PACK, 2 * STRIP], F32, "middle_lifted", "pair_raw1")
+        project(1, 0, into=middle_lifted[:])
+        gather_wd_rows(3, "h_bf01")
+        copy_wd_rows(3)
+        gather_wd_pair("wd_raw3")
         gate(1, 0)
         quantize_wd(1)
+        w4_plane = deal_w4_plane("wd_raw2")
+        swish(1, 0, 256, 512)
         quantize_wd(0)
-        swish(1, 0, 256, 768)
+        project(1, 1)
+        swish(1, 0, 512, 768)
+        round_x(3, nc.vector.tensor_copy, "h_bf01")
         down_strip(0)
-        quantize_x(2)
+        quantize_h(1, 0, 256, 768)
+        quantize_x(3)
         project(2, 0)
         gate(1, 1)
-        quantize_h(1, 0, 256, 768)
         project(2, 1)
         swish(1, 1, 256, 512)
         quantize_y(0, 256)

@@ -46,12 +46,12 @@ def tile_list_listed_hardswish_bottleneck_kernel(
                     plane[32 * q : 32 * q + 4, :].bitcast(I32), scale_rows[4 * q : 4 * q + 4, :].bitcast(I32)
                 )
 
+        tab_codes = held([P, T], U32, "tab_codes")
+        nc.sync.dma_start(tab_codes[:].bitcast(I32), tab_words[0].rearrange("p c i -> p (c i)").bitcast(I32))
         offsets = keep.tile([P, S // 16], U16, name="offsets")
         nc.sync.dma_start(offsets[:], offs)
         w4_raw = held([P, 2 * N], U8, "w4_raw")
         nc.sync.dma_start(w4_raw[:].bitcast(I32), w4_words[0].bitcast(I32))
-        tab_codes = held([P, T], U32, "tab_codes")
-        nc.sync.dma_start(tab_codes[:].bitcast(I32), tab_words[0].rearrange("p c i -> p (c i)").bitcast(I32))
 
         tab_plane = held([P, T], U8, "tab_plane")
         nc.vector.memset(tab_plane[:].bitcast(I32), 0)
@@ -65,18 +65,16 @@ def tile_list_listed_hardswish_bottleneck_kernel(
             nc.sync.dma_start(x_raw[n][:], x_rows[:, :, n * STRIP : (n + 1) * STRIP])
 
         wd_rows = wdT.rearrange("(p s) c -> p s c", s=PACK)
-        pair_raw = {}
         wd_raw = {}
 
-        def load_wd_pair_half(half):
-            pair_raw[half] = held([P, 2, T // 2], F32, f"pair_raw{half}")
-            nc.sync.dma_start(pair_raw[half][:], wd_rows[:, 0:2, half * T // 2 : (half + 1) * T // 2])
-
-        def load_wd_rows(s):
-            wd_raw[s] = held([P, T], F32, f"wd_raw{s}")
-            nc.sync.dma_start(wd_raw[s][:], wd_rows[:, s, :])
+        def load_wd(pair, half):
+            wd_raw[pair, half] = held([P, 2, T // 2], F32, f"wd_raw{pair}{half}")
+            nc.sync.dma_start(
+                wd_raw[pair, half][:], wd_rows[:, 2 * pair : 2 * pair + 2, half * T // 2 : (half + 1) * T // 2]
+            )
 
         load_x(0)
+        load_wd(0, 0)
         g_rows = held([P, PASSES * P], F32, "g_rows")
         nc.gpsimd.memset(g_rows[:], 0.0)
         nc.sync.dma_start(
@@ -84,19 +82,16 @@ def tile_list_listed_hardswish_bottleneck_kernel(
         )
         load_x(1)
         load_x(2)
-        load_wd_rows(2)
-        load_wd_pair_half(0)
-        load_wd_pair_half(1)
-        load_wd_rows(3)
+        load_wd(0, 1)
+        load_wd(1, 0)
+        load_wd(1, 1)
         w4_plane_raw = held([P, N], U8, "w4_plane_raw")
         nc.gpsimd.memset(w4_plane_raw[:].bitcast(I32), 0)
         load_plane(w4_plane_raw, w4_scales[0])
         load_x(3)
 
-        ident_f32 = held([P, P], F32, "ident_f32")
-        make_identity(nc, ident_f32[:])
-        ident_bf = held([P, P], BF16, "ident_bf")
-        make_identity(nc, ident_bf[:])
+        ident = held([P, P], F32, "ident")
+        make_identity(nc, ident[:])
 
         def dealt(tile):
             return tile[:].rearrange("p (t q r) -> p q t r", t=PACK, r=RUN)
@@ -104,10 +99,6 @@ def tile_list_listed_hardswish_bottleneck_kernel(
         def stationary(b, t):
             return slice((t * PASSES + b) * P, (t * PASSES + b + 1) * P)
 
-        w4_codes = held([P, PACK, 2 * P], U8, "w4_codes")
-        nc.vector.tensor_copy(
-            w4_codes[:].bitcast(U16), w4_raw[:].bitcast(U16).rearrange("p (n s) -> p s n", s=PACK)
-        )
         v_codes = held([P, S], U32, "v_codes")
         nc.vector.tensor_copy(dealt(v_codes), tab_codes[:].indirect(offsets[:]))
         picked_plane = held([P, S], U8, "picked_plane", "tab_codes")
@@ -123,66 +114,53 @@ def tile_list_listed_hardswish_bottleneck_kernel(
         def turn_gain():
             g_bank = y_psum.tile([P, PASSES, P], F32, name="g_bank", tag="y")
             for b in range(PASSES):
-                nc.tensor.transpose(g_bank[:, b, :], g_rows[:, b * P : (b + 1) * P], ident_f32[:])
+                nc.tensor.transpose(g_bank[:, b, :], g_rows[:, b * P : (b + 1) * P], ident[:])
             nc.scalar.copy(gain[:], g_bank[:, :, :PACK])
 
         x_codes = {}
         x_plane = held([P, M], U8, "x_plane")
         x_bf = {}
 
-        def round_x(n, copy, after=None):
-            x_bf[n] = held([P, STRIP * PACK], BF16, f"x_bf{n}", after)
-            copy(
-                x_bf[n][:].rearrange("p (c e i) -> p c i e", e=2, i=PACK),
-                x_raw[n][:].rearrange("p i (c e) -> p c i e", e=2),
-            )
+        def round_x(k, copy, after=None):
+            lo, hi = CHUNKS[k]
+            x_bf[k] = held([P, (hi - lo) * PACK], BF16, f"x_bf{k}", after)
+            for m0 in range(lo, hi, STRIP):
+                copy(
+                    x_bf[k][:, (m0 - lo) * PACK : (m0 - lo + STRIP) * PACK].rearrange(
+                        "p (c e i) -> p c i e", e=2, i=PACK
+                    ),
+                    x_raw[m0 // STRIP][:].rearrange("p i (c e) -> p c i e", e=2),
+                )
 
-        def quantize_x(n, after=None):
-            lo = n * STRIP
-            codes = held([P, STRIP], U32, f"x_codes{n}", after)
-            nc.vector.quantize_mx(out=codes[:].bitcast(FP8X4), scales=x_plane[:, lo : lo + STRIP], in_=x_bf[n][:])
-            for c0 in range(0, STRIP, BANK_M):
-                x_codes[lo + c0] = codes[:, c0 : c0 + BANK_M]
+        def quantize_x(k, after=None):
+            lo, hi = CHUNKS[k]
+            codes = held([P, hi - lo], U32, f"x_codes{k}", after)
+            nc.vector.quantize_mx(out=codes[:].bitcast(FP8X4), scales=x_plane[:, lo:hi], in_=x_bf[k][:])
+            for m0 in range(lo, hi, BANK_M):
+                x_codes[m0] = codes[:, m0 - lo : m0 - lo + BANK_M]
 
         wd_codes = held([P, PACK, PASSES * P], U32, "wd_codes")
         wd_plane = held([P, PACK, PASSES * P], U8, "wd_plane")
         wd_bf = {}
-        turned_rows = {}
-        pair_words = {}
+        pair_words = [held([P, T], U32, f"pair_words{pair}") for pair in range(2)]
 
-        def gather_wd_rows(s, after=None):
-            picked = held([P, S], BF16, f"picked{s}", after)
-            nc.vector.tensor_copy(dealt(picked), wd_raw[s][:].indirect(offsets[:]))
-            turned = y_psum.tile([P, PASSES, PACK, P], BF16, name="turned", tag="y")
-            for b in range(PASSES):
-                for t in range(PACK):
-                    nc.tensor.transpose(turned[:, b, t, :], picked[:, stationary(b, t)], ident_bf[:])
-            turned_rows[s] = turned
-
-        def copy_wd_rows(s):
-            if s == 2:
-                wd_bf[1] = held([P, 2, PASSES, P, PACK], BF16, "wd_bf1", "pair_raw0")
-            nc.scalar.copy(wd_bf[1][:, s - 2, :, :, :], turned_rows[s][:].rearrange("p b t n -> p b n t"))
-
-        def round_wd_pair_half(half, after=None):
+        def round_wd(pair, half):
             cols = slice(half * T // 2, (half + 1) * T // 2)
-            if half == 0:
-                pair_words[0] = held([P, T], U32, "pair_words", after)
             nc.scalar.copy(
-                pair_words[0][:, cols].bitcast(BF16).rearrange("p (c e) -> p c e", e=2),
-                pair_raw[half][:].rearrange("p e c -> p c e"),
+                pair_words[pair][:, cols].bitcast(BF16).rearrange("p (c e) -> p c e", e=2),
+                wd_raw[pair, half][:].rearrange("p e c -> p c e"),
             )
 
-        def gather_wd_pair(after=None):
-            picked = held([P, S], U32, "pair_picked", after)
-            wd_bf[0] = held([P, 2, PASSES, P, PACK], BF16, "wd_bf0")
-            nc.vector.tensor_copy(dealt(picked), pair_words[0][:].indirect(offsets[:]))
+        def gather_wd(pair, after, turned_after=None):
+            picked = held([P, S], U32, f"picked_pairs{pair}", after)
+            wd_bf[pair] = held([P, 2, PASSES, P, PACK], BF16, f"wd_bf{pair}", turned_after)
+            nc.vector.tensor_copy(dealt(picked), pair_words[pair][:].indirect(offsets[:]))
             for b in range(PASSES):
-                turned = y_psum.tile([P, PACK, P], F32, name="turned_pair", tag="y")
+                turned = y_psum.tile([P, PACK, P], F32, name="turned", tag="y")
                 for t in range(PACK):
-                    nc.tensor.transpose(turned[:, t, :], picked[:, stationary(b, t)].bitcast(F32), ident_f32[:])
+                    nc.tensor.transpose(turned[:, t, :], picked[:, stationary(b, t)].bitcast(F32), ident[:])
                 nc.scalar.copy(
-                    wd_bf[0][:, :, b, :, :], turned[:].bitcast(BF16).rearrange("p t (n e) -> p e n t", e=2)
+                    wd_bf[pair][:, :, b, :, :], turned[:].bitcast(BF16).rearrange("p t (n e) -> p e n t", e=2)
                 )
 
         def quantize_wd(pair):
@@ -192,6 +170,11 @@ def tile_list_listed_hardswish_bottleneck_kernel(
                 scales=wd_plane[:, rows, :].rearrange("p s c -> p (s c)"),
                 in_=wd_bf[pair][:].rearrange("p s b n t -> p (s b n t)"),
             )
+
+        def deal_w4_codes(after):
+            codes = held([P, PACK, 2 * P], U8, "w4_codes", after)
+            nc.vector.tensor_copy(codes[:].bitcast(U16), w4_raw[:].bitcast(U16).rearrange("p (n s) -> p s n", s=PACK))
+            return codes
 
         def deal_w4_plane(after):
             plane = held([P, PACK, P], U8, "w4_plane", after)
@@ -233,10 +216,10 @@ def tile_list_listed_hardswish_bottleneck_kernel(
                     gated[k, b][:, t, :], lifted[k, b][:, t, :], 6.0, gain[:, b, t : t + 1], ALU.min, ALU.mult
                 )
 
-        def swish(k, b, lo, hi):
+        def swish(k, b, lo, hi, after=None):
             base, end = CHUNKS[k]
             if lo == base:
-                h_bf[k, b] = held([P, (end - base) * PACK], BF16, f"h_bf{k}{b}")
+                h_bf[k, b] = held([P, (end - base) * PACK], BF16, f"h_bf{k}{b}", after)
             for m0 in range(lo, hi, BANK_M):
                 c0 = m0 - base
                 nc.vector.tensor_tensor(
@@ -315,40 +298,40 @@ def tile_list_listed_hardswish_bottleneck_kernel(
 
         round_x(0, nc.scalar.copy)
         quantize_x(0)
-        round_x(1, nc.scalar.copy)
-        round_x(2, nc.scalar.copy)
-        turn_gain()
+        round_wd(0, 0)
         project(0, 0)
+        turn_gain()
         project(0, 1)
-        gather_wd_rows(2, "tab_codes")
-        first_gated = held([P, PASSES, PACK, STRIP], F32, "first_gated", "wd_raw2")
+        w4_codes = deal_w4_codes("tab_codes")
+        round_x(1, nc.vector.tensor_copy, "w4_raw")
+        quantize_x(1)
+        round_wd(0, 1)
+        round_wd(1, 0)
+        round_wd(1, 1)
+        first_gated = held([P, PASSES, PACK, STRIP], F32, "first_gated", "x_raw2")
         gate(0, 0, first_gated[:, 0, :, :])
         gate(0, 1, first_gated[:, 1, :, :])
-        round_wd_pair_half(0)
-        round_wd_pair_half(1)
         swish(0, 0, 0, 256)
         swish(0, 1, 0, 256)
         quantize_h(0, 0, 0, 256)
-        quantize_x(1, "tab_codes")
         quantize_h(0, 1, 0, 256)
-        quantize_x(2, "h_bf00")
-        copy_wd_rows(2)
-        middle_lifted = held([P, PACK, 2 * STRIP], F32, "middle_lifted", "pair_raw1")
+        middle_lifted = held([P, PACK, 2 * STRIP], F32, "middle_lifted", "wd_raw10")
         project(1, 0, into=middle_lifted[:])
-        gather_wd_rows(3, "h_bf01")
-        copy_wd_rows(3)
-        gather_wd_pair("wd_raw3")
-        gate(1, 0)
-        quantize_wd(1)
-        w4_plane = deal_w4_plane("wd_raw2")
-        swish(1, 0, 256, 512)
+        gather_wd(0, "h_bf01", "wd_raw11")
+        gather_wd(1, "pair_words0")
+        middle_gated = held([P, PACK, 2 * STRIP], F32, "middle_gated", "pair_words1")
+        gate(1, 0, middle_gated[:])
         quantize_wd(0)
-        project(1, 1)
+        w4_plane = deal_w4_plane("wd_raw11")
+        swish(1, 0, 256, 512)
+        quantize_wd(1)
+        late_lifted = held([P, PACK, 2 * STRIP], F32, "late_lifted", "pair_words0")
+        project(1, 1, into=late_lifted[:])
         swish(1, 0, 512, 768)
-        round_x(3, nc.vector.tensor_copy, "h_bf01")
+        round_x(2, nc.scalar.copy, "wd_bf1")
         down_strip(0)
         quantize_h(1, 0, 256, 768)
-        quantize_x(3)
+        quantize_x(2)
         project(2, 0)
         gate(1, 1)
         project(2, 1)
@@ -365,13 +348,12 @@ def tile_list_listed_hardswish_bottleneck_kernel(
         gate(2, 1)
         quantize_h(2, 0, 768, 1024)
         swish(2, 1, 768, 896)
-        quantize_y(256, 512)
         quantize_h(2, 1, 768, 896)
         down(768)
         swish(2, 1, 896, 1024)
         quantize_h(2, 1, 896, 1024)
         down(896)
-        quantize_y(512, 768)
+        quantize_y(256, 768)
         store_words(256, 768)
         copy_y(768, nc.vector.tensor_copy)
         store_y(768, 896, nc.sync)

@@ -121,6 +121,18 @@ def tile_list_listed_hardswish_bottleneck_kernel(
         x_plane = held([P, M], U8, "x_plane")
         x_bf = {}
 
+        def round_last_x(after):
+            k = len(CHUNKS) - 1
+            x_bf[k] = held([P, STRIP * PACK], BF16, f"x_bf{k}", after)
+            nc.gpsimd.tensor_scalar(
+                x_bf[k][:].rearrange("p (c i) -> p c i", i=PACK),
+                x_raw[M // STRIP - 1][:].rearrange("p i c -> p c i"),
+                1.0,
+                0.0,
+                ALU.mult,
+                ALU.add,
+            )
+
         def round_x(k, copy, after=None):
             lo, hi = CHUNKS[k]
             x_bf[k] = held([P, (hi - lo) * PACK], BF16, f"x_bf{k}", after)
@@ -315,6 +327,7 @@ def tile_list_listed_hardswish_bottleneck_kernel(
         swish(0, 1, 0, 256)
         quantize_h(0, 0, 0, 256)
         quantize_h(0, 1, 0, 256)
+        round_last_x("h_bf00")
         middle_lifted = held([P, PACK, 2 * STRIP], F32, "middle_lifted", "wd_raw10")
         project(1, 0, into=middle_lifted[:])
         gather_wd(0, "h_bf01", "wd_raw11")
@@ -328,10 +341,9 @@ def tile_list_listed_hardswish_bottleneck_kernel(
         late_lifted = held([P, PACK, 2 * STRIP], F32, "late_lifted", "pair_words0")
         project(1, 1, into=late_lifted[:])
         swish(1, 0, 512, 768)
-        round_x(2, nc.scalar.copy, "wd_bf1")
         down_strip(0)
         quantize_h(1, 0, 256, 768)
-        quantize_x(2)
+        quantize_x(2, "wd_bf1")
         project(2, 0)
         gate(1, 1)
         project(2, 1)

@@ -80,9 +80,9 @@ def tile_list_listed_hardswish_bottleneck_kernel(
         nc.sync.dma_start(
             g_rows[:PACK, :].rearrange("t (q r) -> t q r", r=RUN), g.rearrange("(q t r) -> t q r", t=PACK, r=RUN)
         )
+        load_wd(0, 1)
         load_x(1)
         load_x(2)
-        load_wd(0, 1)
         load_wd(1, 0)
         load_wd(1, 1)
         w4_plane_raw = held([P, N], U8, "w4_plane_raw")
@@ -93,14 +93,14 @@ def tile_list_listed_hardswish_bottleneck_kernel(
         ident = held([P, P], F32, "ident")
         make_identity(nc, ident[:])
 
-        def dealt(tile):
-            return tile[:].rearrange("p (t q r) -> p q t r", t=PACK, r=RUN)
+        def dealt(words):
+            return words.rearrange("p (t q r) -> p q t r", t=PACK, r=RUN)
 
         def stationary(b, t):
             return slice((t * PASSES + b) * P, (t * PASSES + b + 1) * P)
 
         v_codes = held([P, S], U32, "v_codes")
-        nc.vector.tensor_copy(dealt(v_codes), tab_codes[:].indirect(offsets[:]))
+        nc.vector.tensor_copy(dealt(v_codes[:]), tab_codes[:].indirect(offsets[:]))
         picked_plane = held([P, S], U8, "picked_plane", "tab_codes")
         nc.vector.tensor_copy(picked_plane[:], tab_plane[:].indirect(offsets[:]))
         v_plane = held([P, S], U8, "v_plane")
@@ -121,33 +121,30 @@ def tile_list_listed_hardswish_bottleneck_kernel(
         x_plane = held([P, M], U8, "x_plane")
         x_bf = {}
 
-        def round_last_x(after):
-            k = len(CHUNKS) - 1
-            x_bf[k] = held([P, STRIP * PACK], BF16, f"x_bf{k}", after)
-            nc.gpsimd.tensor_scalar(
-                x_bf[k][:].rearrange("p (c i) -> p c i", i=PACK),
-                x_raw[M // STRIP - 1][:].rearrange("p i c -> p c i"),
-                1.0,
-                0.0,
-                ALU.mult,
-                ALU.add,
+        def round_first_x():
+            x_bf[0] = held([P, STRIP * PACK], BF16, "x_bf0")[:]
+            nc.scalar.copy(
+                x_bf[0].rearrange("p (c e i) -> p c i e", e=2, i=PACK),
+                x_raw[0][:].rearrange("p i (c e) -> p c i e", e=2),
             )
 
-        def round_x(k, copy, after=None):
+        def round_later_x(k, into):
             lo, hi = CHUNKS[k]
-            x_bf[k] = held([P, (hi - lo) * PACK], BF16, f"x_bf{k}", after)
+            x_bf[k] = into
             for m0 in range(lo, hi, STRIP):
-                copy(
-                    x_bf[k][:, (m0 - lo) * PACK : (m0 - lo + STRIP) * PACK].rearrange(
-                        "p (c e i) -> p c i e", e=2, i=PACK
-                    ),
-                    x_raw[m0 // STRIP][:].rearrange("p i (c e) -> p c i e", e=2),
+                nc.gpsimd.tensor_scalar(
+                    into[:, (m0 - lo) * PACK : (m0 - lo + STRIP) * PACK].rearrange("p (c i) -> p c i", i=PACK),
+                    x_raw[m0 // STRIP][:].rearrange("p i c -> p c i"),
+                    1.0,
+                    0.0,
+                    ALU.mult,
+                    ALU.add,
                 )
 
         def quantize_x(k, after=None):
             lo, hi = CHUNKS[k]
             codes = held([P, hi - lo], U32, f"x_codes{k}", after)
-            nc.vector.quantize_mx(out=codes[:].bitcast(FP8X4), scales=x_plane[:, lo:hi], in_=x_bf[k][:])
+            nc.vector.quantize_mx(out=codes[:].bitcast(FP8X4), scales=x_plane[:, lo:hi], in_=x_bf[k])
             for m0 in range(lo, hi, BANK_M):
                 x_codes[m0] = codes[:, m0 - lo : m0 - lo + BANK_M]
 
@@ -156,23 +153,29 @@ def tile_list_listed_hardswish_bottleneck_kernel(
         wd_bf = {}
         pair_words = [held([P, T], U32, f"pair_words{pair}") for pair in range(2)]
 
-        def round_wd(pair, half):
+        def round_wd(pair, half, copy):
             cols = slice(half * T // 2, (half + 1) * T // 2)
-            nc.scalar.copy(
+            copy(
                 pair_words[pair][:, cols].bitcast(BF16).rearrange("p (c e) -> p c e", e=2),
                 wd_raw[pair, half][:].rearrange("p e c -> p c e"),
             )
 
-        def gather_wd(pair, after, turned_after=None):
-            picked = held([P, S], U32, f"picked_pairs{pair}", after)
-            wd_bf[pair] = held([P, 2, PASSES, P, PACK], BF16, f"wd_bf{pair}", turned_after)
+        def gather_wd(pair, picked):
             nc.vector.tensor_copy(dealt(picked), pair_words[pair][:].indirect(offsets[:]))
+            turned = []
             for b in range(PASSES):
-                turned = y_psum.tile([P, PACK, P], F32, name="turned", tag="y")
+                bank = y_psum.tile([P, PACK, P], F32, name="turned", tag="y")
+                turned.append(bank)
                 for t in range(PACK):
-                    nc.tensor.transpose(turned[:, t, :], picked[:, stationary(b, t)].bitcast(F32), ident[:])
+                    nc.tensor.transpose(bank[:, t, :], picked[:, stationary(b, t)].bitcast(F32), ident[:])
+            return turned
+
+        def copy_turned(pair, turned, into):
+            wd_bf[pair] = into
+            laid = into.rearrange("p (e b n t) -> p e b n t", e=2, b=PASSES, t=PACK)
+            for b in range(PASSES):
                 nc.scalar.copy(
-                    wd_bf[pair][:, :, b, :, :], turned[:].bitcast(BF16).rearrange("p t (n e) -> p e n t", e=2)
+                    laid[:, :, b, :, :], turned[b][:].bitcast(BF16).rearrange("p t (n e) -> p e n t", e=2)
                 )
 
         def quantize_wd(pair):
@@ -180,7 +183,7 @@ def tile_list_listed_hardswish_bottleneck_kernel(
             nc.vector.quantize_mx(
                 out=wd_codes[:, rows, :].rearrange("p s c -> p (s c)").bitcast(FP8X4),
                 scales=wd_plane[:, rows, :].rearrange("p s c -> p (s c)"),
-                in_=wd_bf[pair][:].rearrange("p s b n t -> p (s b n t)"),
+                in_=wd_bf[pair],
             )
 
         def deal_w4_codes(after):
@@ -308,37 +311,44 @@ def tile_list_listed_hardswish_bottleneck_kernel(
         def store_words(lo, hi):
             nc.sync.dma_start(y_words[:, lo * PACK : hi * PACK].bitcast(I32), y_codes[:, lo:hi].bitcast(I32))
 
-        round_x(0, nc.scalar.copy)
+        round_first_x()
         quantize_x(0)
-        round_wd(0, 0)
-        project(0, 0)
+        round_wd(0, 0, nc.scalar.copy)
+        first_lifted = held([P, PACK, STRIP], F32, "first_lifted")
+        project(0, 0, into=first_lifted[:])
         turn_gain()
         project(0, 1)
         w4_codes = deal_w4_codes("tab_codes")
-        round_x(1, nc.vector.tensor_copy, "w4_raw")
-        quantize_x(1)
-        round_wd(0, 1)
-        round_wd(1, 0)
-        round_wd(1, 1)
-        first_gated = held([P, PASSES, PACK, STRIP], F32, "first_gated", "x_raw2")
-        gate(0, 0, first_gated[:, 0, :, :])
-        gate(0, 1, first_gated[:, 1, :, :])
+        round_wd(0, 1, nc.vector.tensor_copy)
+        round_wd(1, 0, nc.scalar.copy)
+        round_wd(1, 1, nc.scalar.copy)
+        first_gated = held([P, PACK, STRIP], F32, "first_gated", "wd_raw01")
+        gate(0, 0, first_gated[:])
+        after_first_gate = held([P, 2 * S], U32, "after_first_gate", "first_lifted")
+        round_later_x(1, after_first_gate[:, S:].bitcast(BF16))
+        first_turned = gather_wd(0, after_first_gate[:, :S])
         swish(0, 0, 0, 256)
+        second_gated = held([P, PACK, STRIP], F32, "second_gated", "x_raw2")
+        gate(0, 1, second_gated[:])
+        quantize_x(1)
         swish(0, 1, 0, 256)
         quantize_h(0, 0, 0, 256)
         quantize_h(0, 1, 0, 256)
-        round_last_x("h_bf00")
-        middle_lifted = held([P, PACK, 2 * STRIP], F32, "middle_lifted", "wd_raw10")
-        project(1, 0, into=middle_lifted[:])
-        gather_wd(0, "h_bf01", "wd_raw11")
-        gather_wd(1, "pair_words0")
+        last_x_bf = held([P, STRIP * PACK], BF16, "last_x_bf", "h_bf01")
+        round_later_x(2, last_x_bf[:])
+        after_last_cast = held([P, 3 * S], F32, "after_last_cast", "wd_raw11")
+        project(1, 0, into=after_last_cast[:, : 2 * S].rearrange("p (t c) -> p t c", t=PACK))
+        copy_turned(0, first_turned, after_last_cast[:, 2 * S :].bitcast(BF16))
+        second_picked = held([P, S], U32, "second_picked")
+        second_wd_bf = held([P, 2 * S], BF16, "wd_bf1")
+        copy_turned(1, gather_wd(1, second_picked[:]), second_wd_bf[:])
         middle_gated = held([P, PACK, 2 * STRIP], F32, "middle_gated", "pair_words1")
         gate(1, 0, middle_gated[:])
         quantize_wd(0)
         w4_plane = deal_w4_plane("wd_raw11")
         swish(1, 0, 256, 512)
         quantize_wd(1)
-        late_lifted = held([P, PACK, 2 * STRIP], F32, "late_lifted", "pair_words0")
+        late_lifted = held([P, PACK, 2 * STRIP], F32, "late_lifted", "second_picked")
         project(1, 1, into=late_lifted[:])
         swish(1, 0, 512, 768)
         down_strip(0)

@@ -24,7 +24,9 @@ PASSES = S // (P * PACK)
 QUADRANTS = 4
 BANK_M = 128
 STRIP = 256
-CHUNKS = ((0, 256), (256, 768), (768, 1024))
+HALF = T // 2
+KIB = 1024
+WIDTH = {F32: 4, BF16: 2, U32: 4, U8: 1}
 
 
 def tile_list_listed_hardswish_bottleneck_kernel(
@@ -32,13 +34,31 @@ def tile_list_listed_hardswish_bottleneck_kernel(
 ):
     nc = tc.nc
     with ExitStack() as ctx:
+        lists = ctx.enter_context(tc.tile_pool(name="lists", bufs=1))
         keep = ctx.enter_context(tc.tile_pool(name="keep", bufs=1))
-        ring = ctx.enter_context(tc.tile_pool(name="ring", bufs=3))
         a_psum = ctx.enter_context(tc.psum_pool(name="a_psum", bufs=6))
         y_psum = ctx.enter_context(tc.psum_pool(name="y_psum", bufs=2))
 
-        def held(shape, dtype, name, after=None):
-            return keep.tile(shape, dtype, name=name, tag=after or name, align_bytes=64)
+        places = {"top": 0}
+
+        def reserve(name, size):
+            places[name] = places["top"]
+            places["top"] = places["top"] + (size + 63) // 64 * 64
+
+        reserve("window", 16 * KIB)
+        moved = {"wd_plane": ("window", 0), "h_plane1": ("window", KIB)}
+
+        def held(shape, dtype, name, on=None, skip=0):
+            if name in moved:
+                on, skip = moved[name]
+            if on is None:
+                size = WIDTH[dtype]
+                for extent in shape[1:]:
+                    size = size * extent
+                reserve(name, size)
+            else:
+                places[name] = places[on] + skip
+            return keep.tile(shape, dtype, name=name, align_bytes=64, offset=places[name])
 
         def load_plane(plane, scale_rows):
             for q in range(QUADRANTS):
@@ -48,7 +68,7 @@ def tile_list_listed_hardswish_bottleneck_kernel(
 
         tab_codes = held([P, T], U32, "tab_codes")
         nc.sync.dma_start(tab_codes[:].bitcast(I32), tab_words[0].rearrange("p c i -> p (c i)").bitcast(I32))
-        offsets = keep.tile([P, S // 16], U16, name="offsets")
+        offsets = lists.tile([P, S // 16], U16, name="offsets")
         nc.sync.dma_start(offsets[:], offs)
         w4_raw = held([P, 2 * N], U8, "w4_raw")
         nc.sync.dma_start(w4_raw[:].bitcast(I32), w4_words[0].bitcast(I32))
@@ -68,27 +88,32 @@ def tile_list_listed_hardswish_bottleneck_kernel(
         wd_raw = {}
 
         def load_wd(pair, half):
-            wd_raw[pair, half] = held([P, 2, T // 2], F32, f"wd_raw{pair}{half}")
+            wd_raw[pair, half] = held([P, 2, HALF], F32, f"wd_raw{pair}{half}")
             nc.sync.dma_start(
-                wd_raw[pair, half][:], wd_rows[:, 2 * pair : 2 * pair + 2, half * T // 2 : (half + 1) * T // 2]
+                wd_raw[pair, half][:], wd_rows[:, 2 * pair : 2 * pair + 2, half * HALF : (half + 1) * HALF]
             )
 
-        load_x(0)
-        load_wd(0, 0)
         g_rows = held([P, PASSES * P], F32, "g_rows")
         nc.gpsimd.memset(g_rows[:], 0.0)
-        nc.sync.dma_start(
-            g_rows[:PACK, :].rearrange("t (q r) -> t q r", r=RUN), g.rearrange("(q t r) -> t q r", t=PACK, r=RUN)
-        )
-        load_wd(0, 1)
-        load_x(1)
-        load_x(2)
-        load_wd(1, 0)
-        load_wd(1, 1)
+
+        def load_g():
+            nc.sync.dma_start(
+                g_rows[:PACK, :].rearrange("t (q r) -> t q r", r=RUN), g.rearrange("(q t r) -> t q r", t=PACK, r=RUN)
+            )
+
         w4_plane_raw = held([P, N], U8, "w4_plane_raw")
         nc.gpsimd.memset(w4_plane_raw[:].bitcast(I32), 0)
-        load_plane(w4_plane_raw, w4_scales[0])
+
+        load_x(0)
+        load_x(1)
+        load_g()
+        load_x(2)
+        load_wd(0, 0)
+        load_wd(0, 1)
+        load_wd(1, 0)
+        load_wd(1, 1)
         load_x(3)
+        load_plane(w4_plane_raw, w4_scales[0])
 
         ident = held([P, P], F32, "ident")
         make_identity(nc, ident[:])
@@ -96,18 +121,27 @@ def tile_list_listed_hardswish_bottleneck_kernel(
         def dealt(words):
             return words.rearrange("p (t q r) -> p q t r", t=PACK, r=RUN)
 
-        def stationary(b, t):
-            return slice((t * PASSES + b) * P, (t * PASSES + b + 1) * P)
+        def listed(b):
+            return offsets[:, b * P * PACK // 16 : (b + 1) * P * PACK // 16]
 
-        v_codes = held([P, S], U32, "v_codes")
-        nc.vector.tensor_copy(dealt(v_codes[:]), tab_codes[:].indirect(offsets[:]))
-        picked_plane = held([P, S], U8, "picked_plane", "tab_codes")
-        nc.vector.tensor_copy(picked_plane[:], tab_plane[:].indirect(offsets[:]))
-        v_plane = held([P, S], U8, "v_plane")
-        nc.vector.tensor_copy(
-            v_plane[:].bitcast(I32).rearrange("p (t q w) -> p t q w", t=PACK, w=RUN // 4),
-            picked_plane[:].bitcast(I32).rearrange("p (q t w) -> p t q w", t=PACK, w=RUN // 4),
-        )
+        v_codes = {}
+        picked_plane = {}
+        v_plane = {}
+
+        def gather_codes(b, on=None, skip=0):
+            v_codes[b] = held([P, PACK * P], U32, f"v_codes{b}", on, skip)
+            nc.vector.tensor_copy(dealt(v_codes[b][:]), tab_codes[:].indirect(listed(b)))
+
+        def gather_plane(b, on=None, skip=0):
+            picked_plane[b] = held([P, PACK * P], U8, f"picked_plane{b}", on, skip)
+            nc.vector.tensor_copy(picked_plane[b][:], tab_plane[:].indirect(listed(b)))
+
+        def deal_plane(b, on=None, skip=0):
+            v_plane[b] = held([P, PACK * P], U8, f"v_plane{b}", on, skip)
+            nc.vector.tensor_copy(
+                v_plane[b][:].bitcast(I32).rearrange("p (t q w) -> p t q w", t=PACK, w=RUN // 4),
+                picked_plane[b][:].bitcast(I32).rearrange("p (q t w) -> p t q w", t=PACK, w=RUN // 4),
+            )
 
         gain = held([P, PASSES, PACK], F32, "gain")
 
@@ -117,82 +151,68 @@ def tile_list_listed_hardswish_bottleneck_kernel(
                 nc.tensor.transpose(g_bank[:, b, :], g_rows[:, b * P : (b + 1) * P], ident[:])
             nc.scalar.copy(gain[:], g_bank[:, :, :PACK])
 
+        def pool_round(into, values):
+            nc.gpsimd.tensor_scalar(into, values, 1.0, 0.0, ALU.mult, ALU.add)
+
         x_codes = {}
         x_plane = held([P, M], U8, "x_plane")
-        x_bf = {}
 
-        def round_first_x():
-            x_bf[0] = held([P, STRIP * PACK], BF16, "x_bf0")[:]
+        def round_x_scalar(n, into):
             nc.scalar.copy(
-                x_bf[0].rearrange("p (c e i) -> p c i e", e=2, i=PACK),
-                x_raw[0][:].rearrange("p i (c e) -> p c i e", e=2),
+                into.rearrange("p (c e i) -> p c i e", e=2, i=PACK), x_raw[n][:].rearrange("p i (c e) -> p c i e", e=2)
             )
 
-        def round_later_x(k, into):
-            lo, hi = CHUNKS[k]
-            x_bf[k] = into
-            for m0 in range(lo, hi, STRIP):
-                nc.gpsimd.tensor_scalar(
-                    into[:, (m0 - lo) * PACK : (m0 - lo + STRIP) * PACK].rearrange("p (c i) -> p c i", i=PACK),
-                    x_raw[m0 // STRIP][:].rearrange("p i c -> p c i"),
-                    1.0,
-                    0.0,
-                    ALU.mult,
-                    ALU.add,
-                )
+        def round_x_pool(n, into):
+            pool_round(into.rearrange("p (c i) -> p c i", i=PACK), x_raw[n][:].rearrange("p i c -> p c i"))
 
-        def quantize_x(k, after=None):
-            lo, hi = CHUNKS[k]
-            codes = held([P, hi - lo], U32, f"x_codes{k}", after)
-            nc.vector.quantize_mx(out=codes[:].bitcast(FP8X4), scales=x_plane[:, lo:hi], in_=x_bf[k])
+        def quantize_x(lo, hi, x_bf, on=None, skip=0):
+            codes = held([P, hi - lo], U32, f"x_codes{lo}", on, skip)
+            nc.vector.quantize_mx(out=codes[:].bitcast(FP8X4), scales=x_plane[:, lo:hi], in_=x_bf)
             for m0 in range(lo, hi, BANK_M):
                 x_codes[m0] = codes[:, m0 - lo : m0 - lo + BANK_M]
 
         wd_codes = held([P, PACK, PASSES * P], U32, "wd_codes")
         wd_plane = held([P, PACK, PASSES * P], U8, "wd_plane")
         wd_bf = {}
-        pair_words = [held([P, T], U32, f"pair_words{pair}") for pair in range(2)]
+        pair_words = {}
 
-        def round_wd(pair, half, copy):
-            cols = slice(half * T // 2, (half + 1) * T // 2)
+        def round_wd(pair, lo, hi, copy):
+            half = lo // HALF
             copy(
-                pair_words[pair][:, cols].bitcast(BF16).rearrange("p (c e) -> p c e", e=2),
-                wd_raw[pair, half][:].rearrange("p e c -> p c e"),
+                pair_words[pair][:, lo:hi].bitcast(BF16).rearrange("p (c e) -> p c e", e=2),
+                wd_raw[pair, half][:, :, lo - half * HALF : hi - half * HALF].rearrange("p e c -> p c e"),
             )
 
-        def gather_wd(pair, picked):
-            nc.vector.tensor_copy(dealt(picked), pair_words[pair][:].indirect(offsets[:]))
-            turned = []
-            for b in range(PASSES):
-                bank = y_psum.tile([P, PACK, P], F32, name="turned", tag="y")
-                turned.append(bank)
-                for t in range(PACK):
-                    nc.tensor.transpose(bank[:, t, :], picked[:, stationary(b, t)].bitcast(F32), ident[:])
-            return turned
+        turned = {}
 
-        def copy_turned(pair, turned, into):
-            wd_bf[pair] = into
-            laid = into.rearrange("p (e b n t) -> p e b n t", e=2, b=PASSES, t=PACK)
-            for b in range(PASSES):
-                nc.scalar.copy(
-                    laid[:, :, b, :, :], turned[b][:].bitcast(BF16).rearrange("p t (n e) -> p e n t", e=2)
-                )
+        def gather_wd(pair, b, on=None, skip=0):
+            picked = held([P, PACK * P], U32, f"picked{pair}{b}", on, skip)
+            nc.vector.tensor_copy(dealt(picked[:]), pair_words[pair][:].indirect(listed(b)))
+            turned[pair, b] = y_psum.tile([P, PACK, P], F32, name="turned", tag="y")
+            for t in range(PACK):
+                nc.tensor.transpose(turned[pair, b][:, t, :], picked[:, t * P : (t + 1) * P].bitcast(F32), ident[:])
+
+        def copy_turned(pair, b):
+            if b == 0:
+                wd_bf[pair] = held([P, 2 * S], BF16, f"wd_bf{pair}")
+            laid = wd_bf[pair][:].rearrange("p (e b n t) -> p e b n t", e=2, b=PASSES, t=PACK)
+            nc.scalar.copy(laid[:, :, b, :, :], turned[pair, b][:].bitcast(BF16).rearrange("p t (n e) -> p e n t", e=2))
 
         def quantize_wd(pair):
             rows = slice(2 * pair, 2 * pair + 2)
             nc.vector.quantize_mx(
                 out=wd_codes[:, rows, :].rearrange("p s c -> p (s c)").bitcast(FP8X4),
                 scales=wd_plane[:, rows, :].rearrange("p s c -> p (s c)"),
-                in_=wd_bf[pair],
+                in_=wd_bf[pair][:],
             )
 
-        def deal_w4_codes(after):
-            codes = held([P, PACK, 2 * P], U8, "w4_codes", after)
+        def deal_w4_codes(on=None, skip=0):
+            codes = held([P, PACK, 2 * P], U8, "w4_codes", on, skip)
             nc.vector.tensor_copy(codes[:].bitcast(U16), w4_raw[:].bitcast(U16).rearrange("p (n s) -> p s n", s=PACK))
             return codes
 
-        def deal_w4_plane(after):
-            plane = held([P, PACK, P], U8, "w4_plane", after)
+        def deal_w4_plane(on=None, skip=0):
+            plane = held([P, PACK, P], U8, "w4_plane", on, skip)
             nc.vector.tensor_copy(plane[:], w4_plane_raw[:].rearrange("p (n s) -> p s n", s=PACK))
             return plane
 
@@ -203,53 +223,50 @@ def tile_list_listed_hardswish_bottleneck_kernel(
         h_codes = [held([P, M], U32, f"h_codes{b}") for b in range(PASSES)]
         h_plane = [held([P, M], U8, f"h_plane{b}") for b in range(PASSES)]
 
-        def project(k, b, first=None, end=None, into=None):
-            lo, hi = CHUNKS[k]
-            if first is None or first == lo:
-                lifted[k, b] = ring.tile([P, PACK, hi - lo], F32, name="lifted")[:] if into is None else into
+        def project(unit, first=None, end=None, on=None, skip=0):
+            b, lo, hi = unit
+            if unit not in lifted:
+                lifted[unit] = held([P, PACK, hi - lo], F32, f"lifted{b}_{lo}", on, skip)
             for m0 in range(first or lo, end or hi, BANK_M):
                 bank = a_psum.tile([P, PACK, BANK_M], F32, name="a_bank")
                 a_banks[b, m0] = bank
-                cols = slice(m0, m0 + BANK_M)
                 for t in range(PACK):
                     nc.tensor.matmul_mx(
                         out=bank[:, t, :],
-                        lhsT=v_codes[:, stationary(b, t)].bitcast(FP8X4),
-                        lhsT_scale=v_plane[:, stationary(b, t)],
+                        lhsT=v_codes[b][:, t * P : (t + 1) * P].bitcast(FP8X4),
+                        lhsT_scale=v_plane[b][:, t * P : (t + 1) * P],
                         rhs=x_codes[m0].bitcast(FP8X4),
-                        rhs_scale=x_plane[:, cols],
+                        rhs_scale=x_plane[:, m0 : m0 + BANK_M],
                         start=True,
                         stop=True,
                     )
-                nc.scalar.activation(lifted[k, b][:, :, m0 - lo : m0 - lo + BANK_M], bank[:], ACT.Relu, bias=3.0)
+                nc.scalar.activation(lifted[unit][:, :, m0 - lo : m0 - lo + BANK_M], bank[:], ACT.Relu, bias=3.0)
 
-        def gate(k, b, into=None):
-            lo, hi = CHUNKS[k]
-            gated[k, b] = ring.tile([P, PACK, hi - lo], F32, name="gated")[:] if into is None else into
+        def gate(unit, on=None, skip=0):
+            b, lo, hi = unit
+            gated[unit] = held([P, PACK, hi - lo], F32, f"gated{b}_{lo}", on, skip)
             for t in range(PACK):
                 nc.vector.tensor_scalar(
-                    gated[k, b][:, t, :], lifted[k, b][:, t, :], 6.0, gain[:, b, t : t + 1], ALU.min, ALU.mult
+                    gated[unit][:, t, :], lifted[unit][:, t, :], 6.0, gain[:, b, t : t + 1], ALU.min, ALU.mult
                 )
 
-        def swish(k, b, lo, hi, after=None):
-            base, end = CHUNKS[k]
-            if lo == base:
-                h_bf[k, b] = held([P, (end - base) * PACK], BF16, f"h_bf{k}{b}", after)
-            for m0 in range(lo, hi, BANK_M):
-                c0 = m0 - base
+        def swish(unit, first=None, end=None, on=None, skip=0):
+            b, lo, hi = unit
+            first, end = first or lo, end or hi
+            h_bf[b, first] = held([P, (end - first) * PACK], BF16, f"h_bf{b}_{first}", on, skip)
+            for m0 in range(first, end, BANK_M):
+                c0 = m0 - lo
+                h0 = (m0 - first) * PACK
                 nc.vector.tensor_tensor(
-                    h_bf[k, b][:, c0 * PACK : (c0 + BANK_M) * PACK].rearrange("p (c e t) -> p c t e", e=2, t=PACK),
+                    h_bf[b, first][:, h0 : h0 + BANK_M * PACK].rearrange("p (c e t) -> p c t e", e=2, t=PACK),
                     a_banks[b, m0][:].rearrange("p t (c e) -> p c t e", e=2),
-                    gated[k, b][:, :, c0 : c0 + BANK_M].rearrange("p t (c e) -> p c t e", e=2),
+                    gated[unit][:, :, c0 : c0 + BANK_M].rearrange("p t (c e) -> p c t e", e=2),
                     ALU.mult,
                 )
 
-        def quantize_h(k, b, lo, hi):
-            base = CHUNKS[k][0]
+        def quantize_h(b, lo, hi):
             nc.vector.quantize_mx(
-                out=h_codes[b][:, lo:hi].bitcast(FP8X4),
-                scales=h_plane[b][:, lo:hi],
-                in_=h_bf[k, b][:, (lo - base) * PACK : (hi - base) * PACK],
+                out=h_codes[b][:, lo:hi].bitcast(FP8X4), scales=h_plane[b][:, lo:hi], in_=h_bf[b, lo][:]
             )
 
         y_f32 = [held([P, PACK, STRIP], F32, f"y_f32_{n}") for n in range(M // STRIP)]
@@ -311,72 +328,85 @@ def tile_list_listed_hardswish_bottleneck_kernel(
         def store_words(lo, hi):
             nc.sync.dma_start(y_words[:, lo * PACK : hi * PACK].bitcast(I32), y_codes[:, lo:hi].bitcast(I32))
 
-        round_first_x()
-        quantize_x(0)
-        round_wd(0, 0, nc.scalar.copy)
-        first_lifted = held([P, PACK, STRIP], F32, "first_lifted")
-        project(0, 0, into=first_lifted[:])
+        front0, front1, back0 = (0, 0, 512), (1, 0, 512), (0, 512, 1024)
+        third1, last1 = (1, 512, 768), (1, 768, 1024)
+        x_bf = [held([P, STRIP * PACK], BF16, f"x_bf{n}") for n in range(2)]
+        reserve("after_x", 6 * KIB)
+        round_x_scalar(0, x_bf[0][:])
+        round_x_scalar(1, x_bf[1][:])
         turn_gain()
-        project(0, 1)
-        w4_codes = deal_w4_codes("tab_codes")
-        round_wd(0, 1, nc.vector.tensor_copy)
-        round_wd(1, 0, nc.scalar.copy)
-        round_wd(1, 1, nc.scalar.copy)
-        first_gated = held([P, PACK, STRIP], F32, "first_gated", "wd_raw01")
-        gate(0, 0, first_gated[:])
-        after_first_gate = held([P, 2 * S], U32, "after_first_gate", "first_lifted")
-        round_later_x(1, after_first_gate[:, S:].bitcast(BF16))
-        first_turned = gather_wd(0, after_first_gate[:, :S])
-        swish(0, 0, 0, 256)
-        second_gated = held([P, PACK, STRIP], F32, "second_gated", "x_raw2")
-        gate(0, 1, second_gated[:])
-        quantize_x(1)
-        swish(0, 1, 0, 256)
-        quantize_h(0, 0, 0, 256)
-        quantize_h(0, 1, 0, 256)
-        last_x_bf = held([P, STRIP * PACK], BF16, "last_x_bf", "h_bf01")
-        round_later_x(2, last_x_bf[:])
-        after_last_cast = held([P, 3 * S], F32, "after_last_cast", "wd_raw11")
-        project(1, 0, into=after_last_cast[:, : 2 * S].rearrange("p (t c) -> p t c", t=PACK))
-        copy_turned(0, first_turned, after_last_cast[:, 2 * S :].bitcast(BF16))
-        second_picked = held([P, S], U32, "second_picked")
-        second_wd_bf = held([P, 2 * S], BF16, "wd_bf1")
-        copy_turned(1, gather_wd(1, second_picked[:]), second_wd_bf[:])
-        middle_gated = held([P, PACK, 2 * STRIP], F32, "middle_gated", "pair_words1")
-        gate(1, 0, middle_gated[:])
+        gather_codes(0)
+        gather_plane(0)
+        quantize_x(0, 256, x_bf[0][:])
+        deal_plane(0, "x_raw0")
+        project(front0, 0, 256)
+        gather_plane(1, "x_raw0", KIB)
+        quantize_x(256, 512, x_bf[1][:])
+        project(front0, 256, 512)
+        x_bf.append(held([P, STRIP * PACK], BF16, "x_bf2", "x_bf1"))
+        round_x_pool(2, x_bf[2][:])
+        gather_codes(1, "x_raw1")
+        deal_plane(1, "x_raw1", 2 * KIB)
+        w4_codes = deal_w4_codes("x_raw1", 3 * KIB)
+        quantize_x(512, 768, x_bf[2][:])
+        gate(front0, "x_bf1")
+        swish(front0)
+        project(front1, on="window", skip=7 * KIB)
+        pair_words[0] = held([P, T], U32, "pair_words0", "lifted0_0")
+        round_wd(0, 0, 768, nc.gpsimd.tensor_copy)
+        round_wd(0, 768, 1024, nc.scalar.copy)
+        round_wd(0, 1024, 1536, nc.scalar.copy)
+        round_wd(0, 1536, 2048, nc.scalar.copy)
+        project(back0, 512, 768)
+        quantize_h(0, 0, 512)
+        gate(front1)
+        gather_wd(0, 0, "window", 12 * KIB)
+        gather_wd(0, 1, "window", 14 * KIB)
+        pair_words[1] = held([P, T], U32, "pair_words1", "window")
+        round_wd(1, 0, 768, nc.gpsimd.tensor_copy)
+        round_wd(1, 768, 1024, nc.scalar.copy)
+        round_wd(1, 1024, 2048, nc.scalar.copy)
+        x_bf.append(held([P, STRIP * PACK], BF16, "x_bf3", "window", 9 * KIB))
+        round_x_pool(3, x_bf[3][:])
+        copy_turned(0, 0)
+        copy_turned(0, 1)
+        swish(front1, 0, 256)
+        quantize_x(768, 1024, x_bf[3][:])
+        project(back0, 768, 1024)
+        gather_wd(1, 0, "window", 8 * KIB)
+        copy_turned(1, 0)
+        gather_wd(1, 1, "window", 10 * KIB)
+        copy_turned(1, 1)
         quantize_wd(0)
-        w4_plane = deal_w4_plane("wd_raw11")
-        swish(1, 0, 256, 512)
+        swish(front1, 256, 512, "window", 2 * KIB)
+        project(third1)
+        w4_plane = deal_w4_plane("window", 4 * KIB)
+        quantize_h(1, 0, 256)
+        quantize_h(1, 256, 512)
         quantize_wd(1)
-        late_lifted = held([P, PACK, 2 * STRIP], F32, "late_lifted", "second_picked")
-        project(1, 1, into=late_lifted[:])
-        swish(1, 0, 512, 768)
+        gate(back0, "window", 5 * KIB)
         down_strip(0)
-        quantize_h(1, 0, 256, 768)
-        quantize_x(2, "wd_bf1")
-        project(2, 0)
-        gate(1, 1)
-        project(2, 1)
-        swish(1, 1, 256, 512)
-        quantize_y(0, 256)
-        store_words(0, 256)
-        quantize_h(1, 1, 256, 512)
+        swish(back0, 512, 768)
+        project(last1)
+        gate(third1)
+        quantize_h(0, 512, 768)
+        swish(back0, 768, 1024)
         down_strip(256)
-        swish(1, 1, 512, 768)
-        gate(2, 0)
-        quantize_h(1, 1, 512, 768)
+        swish(third1)
+        quantize_h(0, 768, 1024)
+        gate(last1)
+        quantize_h(1, 512, 768)
         down_strip(512)
-        swish(2, 0, 768, 1024)
-        gate(2, 1)
-        quantize_h(2, 0, 768, 1024)
-        swish(2, 1, 768, 896)
-        quantize_h(2, 1, 768, 896)
+        quantize_y(0, 512)
+        store_words(0, 512)
+        swish(last1, 768, 896)
+        quantize_h(1, 768, 896)
         down(768)
-        swish(2, 1, 896, 1024)
-        quantize_h(2, 1, 896, 1024)
+        swish(last1, 896, 1024)
+        quantize_h(1, 896, 1024)
         down(896)
-        quantize_y(256, 768)
-        store_words(256, 768)
+        quantize_y(512, 768)
+        store_words(512, 768)
         copy_y(768, nc.vector.tensor_copy)
         store_y(768, 896, nc.sync)
         quantize_y(768, 1024)

@@ -45,8 +45,11 @@ def tile_list_listed_hardswish_bottleneck_kernel(
             places[name] = places["top"]
             places["top"] = places["top"] + (size + 63) // 64 * 64
 
+        reserve("early", 12 * KIB)
         reserve("window", 16 * KIB)
-        moved = {"wd_plane": ("window", 0), "h_plane1": ("window", KIB)}
+        reserve("first_x", 4 * KIB)
+        reserve("last_wd", 8 * KIB)
+        moved = {"x_raw0": ("first_x", 0), "v_codes0": ("first_x", 0), "v_codes1": ("first_x", 2 * KIB), "wd_plane0": ("window", 9 * KIB), "wd_plane1": ("window", 9 * KIB + 512), "wd_raw11": ("last_wd", 0), "wd_bf0": ("last_wd", 0), "wd_bf1": ("last_wd", 4 * KIB)}
 
         def held(shape, dtype, name, on=None, skip=0):
             if name in moved:
@@ -66,16 +69,11 @@ def tile_list_listed_hardswish_bottleneck_kernel(
                     plane[32 * q : 32 * q + 4, :].bitcast(I32), scale_rows[4 * q : 4 * q + 4, :].bitcast(I32)
                 )
 
-        tab_codes = held([P, T], U32, "tab_codes")
-        nc.sync.dma_start(tab_codes[:].bitcast(I32), tab_words[0].rearrange("p c i -> p (c i)").bitcast(I32))
         offsets = lists.tile([P, S // 16], U16, name="offsets")
         nc.sync.dma_start(offsets[:], offs)
         w4_raw = held([P, 2 * N], U8, "w4_raw")
-        nc.sync.dma_start(w4_raw[:].bitcast(I32), w4_words[0].bitcast(I32))
-
         tab_plane = held([P, T], U8, "tab_plane")
         nc.vector.memset(tab_plane[:].bitcast(I32), 0)
-        load_plane(tab_plane, tab_scales[0])
 
         x_rows = x.rearrange("(p i) m -> p i m", i=PACK)
         x_raw = {}
@@ -105,13 +103,17 @@ def tile_list_listed_hardswish_bottleneck_kernel(
         nc.gpsimd.memset(w4_plane_raw[:].bitcast(I32), 0)
 
         load_x(0)
+        load_plane(tab_plane, tab_scales[0])
+        tab_codes = held([P, T], U32, "tab_codes")
+        nc.sync.dma_start(tab_codes[:].bitcast(I32), tab_words[0].rearrange("p c i -> p (c i)").bitcast(I32))
         load_x(1)
         load_g()
-        load_x(2)
+        nc.sync.dma_start(w4_raw[:].bitcast(I32), w4_words[0].bitcast(I32))
         load_wd(0, 0)
         load_wd(0, 1)
         load_wd(1, 0)
         load_wd(1, 1)
+        load_x(2)
         load_x(3)
         load_plane(w4_plane_raw, w4_scales[0])
 
@@ -124,23 +126,23 @@ def tile_list_listed_hardswish_bottleneck_kernel(
         def listed(b):
             return offsets[:, b * P * PACK // 16 : (b + 1) * P * PACK // 16]
 
-        v_codes = {}
-        picked_plane = {}
-        v_plane = {}
+        def stationary(b, t):
+            return slice((t * PASSES + b) * P, (t * PASSES + b + 1) * P)
 
-        def gather_codes(b, on=None, skip=0):
-            v_codes[b] = held([P, PACK * P], U32, f"v_codes{b}", on, skip)
+        v_codes = [held([P, PACK * P], U32, f"v_codes{b}") for b in range(PASSES)]
+        picked_plane = held([P, S], U8, "picked_plane")
+        v_plane = held([P, S], U8, "v_plane")
+
+        def gather_codes(b):
             nc.vector.tensor_copy(dealt(v_codes[b][:]), tab_codes[:].indirect(listed(b)))
 
-        def gather_plane(b, on=None, skip=0):
-            picked_plane[b] = held([P, PACK * P], U8, f"picked_plane{b}", on, skip)
-            nc.vector.tensor_copy(picked_plane[b][:], tab_plane[:].indirect(listed(b)))
+        def gather_plane():
+            nc.vector.tensor_copy(picked_plane[:], tab_plane[:].indirect(offsets[:]))
 
-        def deal_plane(b, on=None, skip=0):
-            v_plane[b] = held([P, PACK * P], U8, f"v_plane{b}", on, skip)
+        def deal_plane():
             nc.vector.tensor_copy(
-                v_plane[b][:].bitcast(I32).rearrange("p (t q w) -> p t q w", t=PACK, w=RUN // 4),
-                picked_plane[b][:].bitcast(I32).rearrange("p (q t w) -> p t q w", t=PACK, w=RUN // 4),
+                v_plane[:].bitcast(I32).rearrange("p (t q w) -> p t q w", t=PACK, w=RUN // 4),
+                picked_plane[:].bitcast(I32).rearrange("p (q t w) -> p t q w", t=PACK, w=RUN // 4),
             )
 
         gain = held([P, PASSES, PACK], F32, "gain")
@@ -171,8 +173,8 @@ def tile_list_listed_hardswish_bottleneck_kernel(
             for m0 in range(lo, hi, BANK_M):
                 x_codes[m0] = codes[:, m0 - lo : m0 - lo + BANK_M]
 
-        wd_codes = held([P, PACK, PASSES * P], U32, "wd_codes")
-        wd_plane = held([P, PACK, PASSES * P], U8, "wd_plane")
+        wd_codes = [held([P, PACK, P], U32, f"wd_codes{b}") for b in range(PASSES)]
+        wd_plane = [held([P, PACK, P], U8, f"wd_plane{b}") for b in range(PASSES)]
         wd_bf = {}
         pair_words = {}
 
@@ -193,17 +195,18 @@ def tile_list_listed_hardswish_bottleneck_kernel(
                 nc.tensor.transpose(turned[pair, b][:, t, :], picked[:, t * P : (t + 1) * P].bitcast(F32), ident[:])
 
         def copy_turned(pair, b):
-            if b == 0:
-                wd_bf[pair] = held([P, 2 * S], BF16, f"wd_bf{pair}")
-            laid = wd_bf[pair][:].rearrange("p (e b n t) -> p e b n t", e=2, b=PASSES, t=PACK)
-            nc.scalar.copy(laid[:, :, b, :, :], turned[pair, b][:].bitcast(BF16).rearrange("p t (n e) -> p e n t", e=2))
+            if pair == 0:
+                wd_bf[b] = held([P, PACK, P, PACK], BF16, f"wd_bf{b}")
+            nc.scalar.copy(
+                wd_bf[b][:, 2 * pair : 2 * pair + 2, :, :],
+                turned[pair, b][:].bitcast(BF16).rearrange("p t (n e) -> p e n t", e=2),
+            )
 
-        def quantize_wd(pair):
-            rows = slice(2 * pair, 2 * pair + 2)
+        def quantize_wd(b):
             nc.vector.quantize_mx(
-                out=wd_codes[:, rows, :].rearrange("p s c -> p (s c)").bitcast(FP8X4),
-                scales=wd_plane[:, rows, :].rearrange("p s c -> p (s c)"),
-                in_=wd_bf[pair][:],
+                out=wd_codes[b][:].rearrange("p s c -> p (s c)").bitcast(FP8X4),
+                scales=wd_plane[b][:].rearrange("p s c -> p (s c)"),
+                in_=wd_bf[b][:].rearrange("p s n t -> p (s n t)"),
             )
 
         def deal_w4_codes(on=None, skip=0):
@@ -220,8 +223,8 @@ def tile_list_listed_hardswish_bottleneck_kernel(
         lifted = {}
         gated = {}
         h_bf = {}
-        h_codes = [held([P, M], U32, f"h_codes{b}") for b in range(PASSES)]
-        h_plane = [held([P, M], U8, f"h_plane{b}") for b in range(PASSES)]
+        h_codes = {}
+        h_plane = {}
 
         def project(unit, first=None, end=None, on=None, skip=0):
             b, lo, hi = unit
@@ -234,7 +237,7 @@ def tile_list_listed_hardswish_bottleneck_kernel(
                     nc.tensor.matmul_mx(
                         out=bank[:, t, :],
                         lhsT=v_codes[b][:, t * P : (t + 1) * P].bitcast(FP8X4),
-                        lhsT_scale=v_plane[b][:, t * P : (t + 1) * P],
+                        lhsT_scale=v_plane[:, stationary(b, t)],
                         rhs=x_codes[m0].bitcast(FP8X4),
                         rhs_scale=x_plane[:, m0 : m0 + BANK_M],
                         start=True,
@@ -250,27 +253,32 @@ def tile_list_listed_hardswish_bottleneck_kernel(
                     gated[unit][:, t, :], lifted[unit][:, t, :], 6.0, gain[:, b, t : t + 1], ALU.min, ALU.mult
                 )
 
-        def swish(unit, first=None, end=None, on=None, skip=0):
+        def swish(unit, first=None, end=None, on=None, skip=0, base=None, top=None):
             b, lo, hi = unit
             first, end = first or lo, end or hi
-            h_bf[b, first] = held([P, (end - first) * PACK], BF16, f"h_bf{b}_{first}", on, skip)
+            if base is None:
+                base = first
+                h_bf[b, base] = held([P, ((top or end) - first) * PACK], BF16, f"h_bf{b}_{first}", on, skip)
             for m0 in range(first, end, BANK_M):
                 c0 = m0 - lo
-                h0 = (m0 - first) * PACK
+                h0 = (m0 - base) * PACK
                 nc.vector.tensor_tensor(
-                    h_bf[b, first][:, h0 : h0 + BANK_M * PACK].rearrange("p (c e t) -> p c t e", e=2, t=PACK),
+                    h_bf[b, base][:, h0 : h0 + BANK_M * PACK].rearrange("p (c e t) -> p c t e", e=2, t=PACK),
                     a_banks[b, m0][:].rearrange("p t (c e) -> p c t e", e=2),
                     gated[unit][:, :, c0 : c0 + BANK_M].rearrange("p t (c e) -> p c t e", e=2),
                     ALU.mult,
                 )
 
-        def quantize_h(b, lo, hi):
-            nc.vector.quantize_mx(
-                out=h_codes[b][:, lo:hi].bitcast(FP8X4), scales=h_plane[b][:, lo:hi], in_=h_bf[b, lo][:]
-            )
+        def quantize_h(b, lo, hi, on=None, skip=0):
+            codes = held([P, hi - lo], U32, f"h_codes{b}_{lo}")
+            plane = held([P, hi - lo], U8, f"h_plane{b}_{lo}", on, skip)
+            nc.vector.quantize_mx(out=codes[:].bitcast(FP8X4), scales=plane[:], in_=h_bf[b, lo][:])
+            for m0 in range(lo, hi, BANK_M):
+                h_codes[b, m0] = codes[:, m0 - lo : m0 - lo + BANK_M]
+                h_plane[b, m0] = plane[:, m0 - lo : m0 - lo + BANK_M]
 
         y_f32 = [held([P, PACK, STRIP], F32, f"y_f32_{n}") for n in range(M // STRIP)]
-        y_bf = held([P, M, PACK], BF16, "y_bf")
+        y_bf = {}
         y_codes = held([P, M], U32, "y_codes")
         y_plane = held([P, M], U8, "y_plane")
         y_rows = out_0.rearrange("(p s) m -> p s m", s=PACK)
@@ -295,14 +303,25 @@ def tile_list_listed_hardswish_bottleneck_kernel(
                 for s in range(PACK):
                     nc.tensor.matmul_mx(
                         out=bank[:, s, :],
-                        lhsT=wd_codes[:, s, b * P : (b + 1) * P].bitcast(FP8X4),
-                        lhsT_scale=wd_plane[:, s, b * P : (b + 1) * P],
-                        rhs=h_codes[b][:, cols].bitcast(FP8X4),
-                        rhs_scale=h_plane[b][:, cols],
+                        lhsT=wd_codes[b][:, s, :].bitcast(FP8X4),
+                        lhsT_scale=wd_plane[b][:, s, :],
+                        rhs=h_codes[b, m0].bitcast(FP8X4),
+                        rhs_scale=h_plane[b, m0],
                         start=False,
                         stop=(b == PASSES - 1 and s == PACK - 1),
                     )
-            nc.scalar.copy(y_bf[:, cols, :], bank[:].rearrange("p s m -> p m s"))
+
+        def hold_y_bf(lo, hi, on=None, skip=0):
+            tile = held([P, hi - lo, PACK], BF16, f"y_bf{lo}", on, skip)
+            y_bf[lo, hi] = tile
+            for m0 in range(lo, hi, BANK_M):
+                y_bf[m0] = tile[:, m0 - lo : m0 - lo + BANK_M, :]
+
+        def round_y_scalar(m0):
+            nc.scalar.copy(y_bf[m0], y_banks[m0][:].rearrange("p s m -> p m s"))
+
+        def round_y_pool(lo, hi, m0):
+            pool_round(y_bf[lo, hi][:, m0 - lo : m0 - lo + STRIP, :], y_f32[m0 // STRIP][:].rearrange("p s m -> p m s"))
 
         def copy_y(m0, copy):
             c0 = m0 % STRIP
@@ -312,9 +331,11 @@ def tile_list_listed_hardswish_bottleneck_kernel(
             c0 = lo % STRIP
             queue.dma_start(y_rows[:, :, lo:hi], y_f32[lo // STRIP][:, :, c0 : c0 + hi - lo])
 
-        def down_strip(lo):
+        def down_strip(lo, rounded):
             for m0 in range(lo, lo + STRIP, BANK_M):
                 down(m0)
+                if rounded:
+                    round_y_scalar(m0)
                 copy_y(m0, nc.scalar.copy)
             store_y(lo, lo + STRIP, nc.sync)
 
@@ -322,89 +343,91 @@ def tile_list_listed_hardswish_bottleneck_kernel(
             nc.vector.quantize_mx(
                 out=y_codes[:, lo:hi].bitcast(FP8X4),
                 scales=y_plane[:, lo:hi],
-                in_=y_bf[:, lo:hi, :].rearrange("p m s -> p (m s)"),
+                in_=y_bf[lo, hi][:].rearrange("p m s -> p (m s)"),
             )
 
         def store_words(lo, hi):
             nc.sync.dma_start(y_words[:, lo * PACK : hi * PACK].bitcast(I32), y_codes[:, lo:hi].bitcast(I32))
 
-        front0, front1, back0 = (0, 0, 512), (1, 0, 512), (0, 512, 1024)
-        third1, last1 = (1, 512, 768), (1, 768, 1024)
-        x_bf = [held([P, STRIP * PACK], BF16, f"x_bf{n}") for n in range(2)]
-        reserve("after_x", 6 * KIB)
-        round_x_scalar(0, x_bf[0][:])
-        round_x_scalar(1, x_bf[1][:])
+        first0, second0, front1 = (0, 0, 256), (0, 256, 512), (1, 0, 512)
+        back0, third1, last1 = (0, 512, 1024), (1, 512, 768), (1, 768, 1024)
+        x_bf0 = held([P, STRIP * PACK], BF16, "x_bf0")
+        round_x_scalar(0, x_bf0[:])
         turn_gain()
+        gather_plane()
+        deal_plane()
+        quantize_x(0, 256, x_bf0[:])
         gather_codes(0)
-        gather_plane(0)
-        quantize_x(0, 256, x_bf[0][:])
-        deal_plane(0, "x_raw0")
-        project(front0, 0, 256)
-        gather_plane(1, "x_raw0", KIB)
-        quantize_x(256, 512, x_bf[1][:])
-        project(front0, 256, 512)
-        x_bf.append(held([P, STRIP * PACK], BF16, "x_bf2", "x_bf1"))
-        round_x_pool(2, x_bf[2][:])
-        gather_codes(1, "x_raw1")
-        deal_plane(1, "x_raw1", 2 * KIB)
-        w4_codes = deal_w4_codes("x_raw1", 3 * KIB)
-        quantize_x(512, 768, x_bf[2][:])
-        gate(front0, "x_bf1")
-        swish(front0)
+        gather_codes(1)
+        x_bf1 = held([P, STRIP * PACK], BF16, "x_bf1", "x_bf0")
+        round_x_pool(1, x_bf1[:])
+        project(first0)
+        quantize_x(256, 512, x_bf1[:])
+        project(second0, on="early", skip=6 * KIB)
+        w4_codes = deal_w4_codes("x_bf0")
+        gate(first0)
+        gate(second0)
+        swish(first0, on="early", skip=8 * KIB, top=512)
+        swish(second0, base=0)
         project(front1, on="window", skip=7 * KIB)
-        pair_words[0] = held([P, T], U32, "pair_words0", "lifted0_0")
+        pair_words[0] = held([P, T], U32, "pair_words0", "early")
         round_wd(0, 0, 768, nc.gpsimd.tensor_copy)
         round_wd(0, 768, 1024, nc.scalar.copy)
         round_wd(0, 1024, 1536, nc.scalar.copy)
         round_wd(0, 1536, 2048, nc.scalar.copy)
-        project(back0, 512, 768)
         quantize_h(0, 0, 512)
         gate(front1)
         gather_wd(0, 0, "window", 12 * KIB)
         gather_wd(0, 1, "window", 14 * KIB)
         pair_words[1] = held([P, T], U32, "pair_words1", "window")
-        round_wd(1, 0, 768, nc.gpsimd.tensor_copy)
-        round_wd(1, 768, 1024, nc.scalar.copy)
+        round_wd(1, 0, 832, nc.gpsimd.tensor_copy)
+        round_wd(1, 832, 1024, nc.scalar.copy)
         round_wd(1, 1024, 2048, nc.scalar.copy)
-        x_bf.append(held([P, STRIP * PACK], BF16, "x_bf3", "window", 9 * KIB))
-        round_x_pool(3, x_bf[3][:])
+        back_x_bf = held([P, 2 * STRIP * PACK], BF16, "back_x_bf", "window", 8 * KIB)
+        round_x_pool(2, back_x_bf[:, : STRIP * PACK])
+        round_x_pool(3, back_x_bf[:, STRIP * PACK :])
         copy_turned(0, 0)
         copy_turned(0, 1)
-        swish(front1, 0, 256)
-        quantize_x(768, 1024, x_bf[3][:])
-        project(back0, 768, 1024)
-        gather_wd(1, 0, "window", 8 * KIB)
+        gather_wd(1, 0)
         copy_turned(1, 0)
-        gather_wd(1, 1, "window", 10 * KIB)
+        gather_wd(1, 1)
         copy_turned(1, 1)
+        swish(front1, 0, 256, "window")
+        quantize_x(512, 1024, back_x_bf[:], "window", 2 * KIB)
+        project(back0)
+        w4_plane = deal_w4_plane("window", 8 * KIB)
+        quantize_h(1, 0, 256, "window", 8 * KIB + 512)
         quantize_wd(0)
-        swish(front1, 256, 512, "window", 2 * KIB)
-        project(third1)
-        w4_plane = deal_w4_plane("window", 4 * KIB)
-        quantize_h(1, 0, 256)
-        quantize_h(1, 256, 512)
         quantize_wd(1)
-        gate(back0, "window", 5 * KIB)
-        down_strip(0)
+        swish(front1, 256, 512, "window", 10 * KIB)
+        project(third1)
+        hold_y_bf(0, 512)
+        gate(back0)
+        quantize_h(1, 256, 512)
+        down_strip(0, True)
         swish(back0, 512, 768)
         project(last1)
         gate(third1)
         quantize_h(0, 512, 768)
         swish(back0, 768, 1024)
-        down_strip(256)
+        down_strip(256, True)
         swish(third1)
         quantize_h(0, 768, 1024)
         gate(last1)
         quantize_h(1, 512, 768)
-        down_strip(512)
+        hold_y_bf(512, 768)
+        down_strip(512, True)
         quantize_y(0, 512)
         store_words(0, 512)
         swish(last1, 768, 896)
         quantize_h(1, 768, 896)
+        hold_y_bf(768, 1024)
         down(768)
+        round_y_scalar(768)
         swish(last1, 896, 1024)
         quantize_h(1, 896, 1024)
         down(896)
+        round_y_scalar(896)
         quantize_y(512, 768)
         store_words(512, 768)
         copy_y(768, nc.vector.tensor_copy)

@@ -49,6 +49,7 @@ def tile_list_listed_hardswish_bottleneck_kernel(
         reserve("window", 16 * KIB)
         reserve("first_x", 4 * KIB)
         reserve("last_wd", 8 * KIB)
+        reserve("late", 8 * KIB)
         moved = {"x_raw0": ("first_x", 0), "v_codes0": ("first_x", 0), "v_codes1": ("first_x", 2 * KIB), "wd_plane0": ("window", 9 * KIB), "wd_plane1": ("window", 9 * KIB + 512), "wd_raw11": ("last_wd", 0), "wd_bf0": ("last_wd", 0), "wd_bf1": ("last_wd", 4 * KIB)}
 
         def held(shape, dtype, name, on=None, skip=0):
@@ -285,8 +286,11 @@ def tile_list_listed_hardswish_bottleneck_kernel(
         y_words = out_1[0].rearrange("p m s -> p (m s)")
         y_banks = {}
 
-        def down(m0):
-            bank = y_psum.tile([P, PACK, BANK_M], F32, name="y_bank", tag="y")
+        def down(m0, spare=False):
+            if spare:
+                bank = a_psum.tile([P, PACK, BANK_M], F32, name="a_bank")
+            else:
+                bank = y_psum.tile([P, PACK, BANK_M], F32, name="y_bank", tag="y")
             y_banks[m0] = bank
             cols = slice(m0, m0 + BANK_M)
             for s in range(PACK):
@@ -395,41 +399,42 @@ def tile_list_listed_hardswish_bottleneck_kernel(
         swish(front1, 0, 256, "window")
         quantize_x(512, 1024, back_x_bf[:], "window", 2 * KIB)
         project(back0)
+        swish(front1, 256, 512, "window", 10 * KIB)
+        project(third1, on="late", skip=2 * KIB)
         w4_plane = deal_w4_plane("window", 8 * KIB)
         quantize_h(1, 0, 256, "window", 8 * KIB + 512)
         quantize_wd(0)
-        quantize_wd(1)
-        swish(front1, 256, 512, "window", 10 * KIB)
-        project(third1)
-        hold_y_bf(0, 512)
-        gate(back0)
         quantize_h(1, 256, 512)
-        down_strip(0, True)
-        swish(back0, 512, 768)
-        project(last1)
+        quantize_wd(1)
+        down_strip(0, False)
+        gate(back0)
         gate(third1)
-        quantize_h(0, 512, 768)
-        swish(back0, 768, 1024)
+        hold_y_bf(0, 256, "late", 2 * KIB)
+        round_y_pool(0, 256, 0)
+        swish(back0, 512, 768, "late", 4 * KIB)
+        project(last1)
+        hold_y_bf(256, 768)
         down_strip(256, True)
         swish(third1)
-        quantize_h(0, 768, 1024)
-        gate(last1)
+        quantize_h(0, 512, 768)
+        quantize_y(0, 256)
+        store_words(0, 256)
         quantize_h(1, 512, 768)
-        hold_y_bf(512, 768)
         down_strip(512, True)
-        quantize_y(0, 512)
-        store_words(0, 512)
+        swish(back0, 768, 1024, "late", 2 * KIB)
+        gate(last1)
+        quantize_h(0, 768, 1024)
         swish(last1, 768, 896)
+        swish(last1, 896, 1024)
         quantize_h(1, 768, 896)
         hold_y_bf(768, 1024)
-        down(768)
+        down(768, True)
         round_y_scalar(768)
-        swish(last1, 896, 1024)
         quantize_h(1, 896, 1024)
-        down(896)
+        down(896, True)
         round_y_scalar(896)
-        quantize_y(512, 768)
-        store_words(512, 768)
+        quantize_y(256, 768)
+        store_words(256, 768)
         copy_y(768, nc.vector.tensor_copy)
         store_y(768, 896, nc.sync)
         quantize_y(768, 1024)

@@ -278,7 +278,8 @@ def tile_list_listed_hardswish_bottleneck_kernel(
                 h_codes[b, m0] = codes[:, m0 - lo : m0 - lo + BANK_M]
                 h_plane[b, m0] = plane[:, m0 - lo : m0 - lo + BANK_M]
 
-        y_f32 = [held([P, PACK, STRIP], F32, f"y_f32_{n}") for n in range(M // STRIP)]
+        y_f32 = [held([P, PACK, STRIP], F32, f"y_f32_{n}") for n in range(M // STRIP - 1)]
+        y_last = {m0: held([P, PACK, BANK_M], F32, f"y_last{m0}") for m0 in range(M - STRIP, M, BANK_M)}
         y_bf = {}
         y_codes = held([P, M], U32, "y_codes")
         y_plane = held([P, M], U8, "y_plane")
@@ -331,6 +332,15 @@ def tile_list_listed_hardswish_bottleneck_kernel(
             c0 = m0 % STRIP
             copy(y_f32[m0 // STRIP][:, :, c0 : c0 + BANK_M], y_banks[m0][:])
 
+        def copy_store_last(m0, queue):
+            nc.scalar.copy(y_last[m0][:], y_banks[m0][:])
+            queue.dma_start(y_rows[:, :, m0 : m0 + BANK_M], y_last[m0][:])
+
+        def round_last(m0):
+            nc.vector.tensor_copy(
+                y_bf[m0].rearrange("p (c e) s -> p c s e", e=2), y_last[m0][:].rearrange("p s (c e) -> p c s e", e=2)
+            )
+
         def store_y(lo, hi, queue):
             c0 = lo % STRIP
             queue.dma_start(y_rows[:, :, lo:hi], y_f32[lo // STRIP][:, :, c0 : c0 + hi - lo])
@@ -338,10 +348,11 @@ def tile_list_listed_hardswish_bottleneck_kernel(
         def down_strip(lo, rounded):
             for m0 in range(lo, lo + STRIP, BANK_M):
                 down(m0)
+                copy_y(m0, nc.scalar.copy)
+                if m0 + BANK_M == lo + STRIP:
+                    store_y(lo, lo + STRIP, nc.sync)
                 if rounded:
                     round_y_scalar(m0)
-                copy_y(m0, nc.scalar.copy)
-            store_y(lo, lo + STRIP, nc.sync)
 
         def quantize_y(lo, hi):
             nc.vector.quantize_mx(
@@ -429,18 +440,16 @@ def tile_list_listed_hardswish_bottleneck_kernel(
         quantize_h(1, 768, 896)
         hold_y_bf(768, 1024)
         down(768, True)
-        round_y_scalar(768)
+        copy_store_last(768, nc.sync)
         quantize_h(1, 896, 1024)
         down(896, True)
-        round_y_scalar(896)
+        copy_store_last(896, nc.scalar)
         quantize_y(256, 768)
         store_words(256, 768)
-        copy_y(768, nc.vector.tensor_copy)
-        store_y(768, 896, nc.sync)
+        round_last(768)
+        round_last(896)
         quantize_y(768, 1024)
         store_words(768, 1024)
-        copy_y(896, nc.scalar.copy)
-        store_y(896, 1024, nc.scalar)
         for q in range(QUADRANTS):
             queue = nc.sync if q < QUADRANTS // 2 else nc.scalar
             queue.dma_start(

@@ -217,7 +217,7 @@ def tile_list_listed_hardswish_bottleneck_kernel(
 
         def deal_w4_plane(on=None, skip=0):
             plane = held([P, PACK, P], U8, "w4_plane", on, skip)
-            nc.vector.tensor_copy(plane[:], w4_plane_raw[:].rearrange("p (n s) -> p s n", s=PACK))
+            nc.gpsimd.tensor_copy(plane[:], w4_plane_raw[:].rearrange("p (n s) -> p s n", s=PACK))
             return plane
 
         a_banks = {}
@@ -395,8 +395,7 @@ def tile_list_listed_hardswish_bottleneck_kernel(
         gather_wd(0, 0, "window", 12 * KIB)
         gather_wd(0, 1, "window", 14 * KIB)
         pair_words[1] = held([P, T], U32, "pair_words1", "window")
-        round_wd(1, 0, 832, nc.gpsimd.tensor_copy)
-        round_wd(1, 832, 1024, nc.scalar.copy)
+        round_wd(1, 0, 1024, nc.gpsimd.tensor_copy)
         round_wd(1, 1024, 2048, nc.scalar.copy)
         back_x_bf = held([P, 2 * STRIP * PACK], BF16, "back_x_bf", "window", 8 * KIB)
         round_x_pool(2, back_x_bf[:, : STRIP * PACK])
@@ -438,7 +437,8 @@ def tile_list_listed_hardswish_bottleneck_kernel(
         swish(last1, 768, 896)
         swish(last1, 896, 1024)
         quantize_h(1, 768, 896)
-        hold_y_bf(768, 1024)
+        hold_y_bf(768, 896)
+        hold_y_bf(896, 1024)
         down(768, True)
         copy_store_last(768, nc.sync)
         quantize_h(1, 896, 1024)
@@ -448,7 +448,8 @@ def tile_list_listed_hardswish_bottleneck_kernel(
         store_words(256, 768)
         round_last(768)
         round_last(896)
-        quantize_y(768, 1024)
+        quantize_y(768, 896)
+        quantize_y(896, 1024)
         store_words(768, 1024)
         for q in range(QUADRANTS):
             queue = nc.sync if q < QUADRANTS // 2 else nc.scalar

@@ -25,8 +25,45 @@ QUADRANTS = 4
 BANK_M = 128
 STRIP = 256
 HALF = T // 2
+GROUP = 16
+POOL_COLUMNS = 896
+A_BANKS = 6
+Y_BANKS = 2
 KIB = 1024
+ALIGN = 64
 WIDTH = {F32: 4, BF16: 2, U32: 4, U8: 1}
+
+REGIONS = (("early", 12 * KIB), ("window", 16 * KIB), ("first_x", 4 * KIB), ("last_wd", 8 * KIB), ("late", 8 * KIB))
+
+TENANTS = {
+    "x_raw0": ("first_x", 0),
+    "v_codes0": ("first_x", 0),
+    "v_codes1": ("first_x", 2 * KIB),
+    "x_bf1": ("x_bf0", 0),
+    "w4_codes": ("x_bf0", 0),
+    "lifted0_256": ("early", 6 * KIB),
+    "h_bf0_0": ("early", 8 * KIB),
+    "pair_words0": ("early", 0),
+    "lifted1_0": ("window", 7 * KIB),
+    "picked00": ("window", 12 * KIB),
+    "picked01": ("window", 14 * KIB),
+    "pair_words1": ("window", 0),
+    "back_x_bf": ("window", 8 * KIB),
+    "h_bf1_0": ("window", 0),
+    "x_codes512": ("window", 2 * KIB),
+    "h_bf1_256": ("window", 10 * KIB),
+    "w4_plane": ("window", 8 * KIB),
+    "h_plane1_0": ("window", 8 * KIB + 512),
+    "wd_plane0": ("window", 9 * KIB),
+    "wd_plane1": ("window", 9 * KIB + 512),
+    "wd_raw11": ("last_wd", 0),
+    "wd_bf0": ("last_wd", 0),
+    "wd_bf1": ("last_wd", 4 * KIB),
+    "lifted1_512": ("late", 2 * KIB),
+    "y_bf0": ("late", 2 * KIB),
+    "h_bf0_512": ("late", 4 * KIB),
+    "h_bf0_768": ("late", 4 * KIB),
+}
 
 
 def tile_list_listed_hardswish_bottleneck_kernel(
@@ -36,33 +73,28 @@ def tile_list_listed_hardswish_bottleneck_kernel(
     with ExitStack() as ctx:
         lists = ctx.enter_context(tc.tile_pool(name="lists", bufs=1))
         keep = ctx.enter_context(tc.tile_pool(name="keep", bufs=1))
-        a_psum = ctx.enter_context(tc.psum_pool(name="a_psum", bufs=6))
-        y_psum = ctx.enter_context(tc.psum_pool(name="y_psum", bufs=2))
+        a_psum = ctx.enter_context(tc.psum_pool(name="a_psum", bufs=A_BANKS))
+        y_psum = ctx.enter_context(tc.psum_pool(name="y_psum", bufs=Y_BANKS))
 
         places = {"top": 0}
 
         def reserve(name, size):
             places[name] = places["top"]
-            places["top"] = places["top"] + (size + 63) // 64 * 64
+            places["top"] = places["top"] + (size + ALIGN - 1) // ALIGN * ALIGN
 
-        reserve("early", 12 * KIB)
-        reserve("window", 16 * KIB)
-        reserve("first_x", 4 * KIB)
-        reserve("last_wd", 8 * KIB)
-        reserve("late", 8 * KIB)
-        moved = {"x_raw0": ("first_x", 0), "v_codes0": ("first_x", 0), "v_codes1": ("first_x", 2 * KIB), "wd_plane0": ("window", 9 * KIB), "wd_plane1": ("window", 9 * KIB + 512), "wd_raw11": ("last_wd", 0), "wd_bf0": ("last_wd", 0), "wd_bf1": ("last_wd", 4 * KIB)}
+        for region, region_size in REGIONS:
+            reserve(region, region_size)
 
-        def held(shape, dtype, name, on=None, skip=0):
-            if name in moved:
-                on, skip = moved[name]
-            if on is None:
+        def held(shape, dtype, name):
+            if name in TENANTS:
+                host, skip = TENANTS[name]
+                places[name] = places[host] + skip
+            else:
                 size = WIDTH[dtype]
                 for extent in shape[1:]:
                     size = size * extent
                 reserve(name, size)
-            else:
-                places[name] = places[on] + skip
-            return keep.tile(shape, dtype, name=name, align_bytes=64, offset=places[name])
+            return keep.tile(shape, dtype, name=name, align_bytes=ALIGN, offset=places[name])
 
         def load_plane(plane, scale_rows):
             for q in range(QUADRANTS):
@@ -70,7 +102,7 @@ def tile_list_listed_hardswish_bottleneck_kernel(
                     plane[32 * q : 32 * q + 4, :].bitcast(I32), scale_rows[4 * q : 4 * q + 4, :].bitcast(I32)
                 )
 
-        offsets = lists.tile([P, S // 16], U16, name="offsets")
+        offsets = lists.tile([P, S // GROUP], U16, name="offsets")
         nc.sync.dma_start(offsets[:], offs)
         w4_raw = held([P, 2 * N], U8, "w4_raw")
         tab_plane = held([P, T], U8, "tab_plane")
@@ -79,9 +111,9 @@ def tile_list_listed_hardswish_bottleneck_kernel(
         x_rows = x.rearrange("(p i) m -> p i m", i=PACK)
         x_raw = {}
 
-        def load_x(n):
-            x_raw[n] = held([P, PACK, STRIP], F32, f"x_raw{n}")
-            nc.sync.dma_start(x_raw[n][:], x_rows[:, :, n * STRIP : (n + 1) * STRIP])
+        def load_x(strip):
+            x_raw[strip] = held([P, PACK, STRIP], F32, f"x_raw{strip}")
+            nc.sync.dma_start(x_raw[strip][:], x_rows[:, :, strip * STRIP : (strip + 1) * STRIP])
 
         wd_rows = wdT.rearrange("(p s) c -> p s c", s=PACK)
         wd_raw = {}
@@ -94,12 +126,6 @@ def tile_list_listed_hardswish_bottleneck_kernel(
 
         g_rows = held([P, PASSES * P], F32, "g_rows")
         nc.gpsimd.memset(g_rows[:], 0.0)
-
-        def load_g():
-            nc.sync.dma_start(
-                g_rows[:PACK, :].rearrange("t (q r) -> t q r", r=RUN), g.rearrange("(q t r) -> t q r", t=PACK, r=RUN)
-            )
-
         w4_plane_raw = held([P, N], U8, "w4_plane_raw")
         nc.gpsimd.memset(w4_plane_raw[:].bitcast(I32), 0)
 
@@ -108,12 +134,13 @@ def tile_list_listed_hardswish_bottleneck_kernel(
         tab_codes = held([P, T], U32, "tab_codes")
         nc.sync.dma_start(tab_codes[:].bitcast(I32), tab_words[0].rearrange("p c i -> p (c i)").bitcast(I32))
         load_x(1)
-        load_g()
+        nc.sync.dma_start(
+            g_rows[:PACK, :].rearrange("t (q r) -> t q r", r=RUN), g.rearrange("(q t r) -> t q r", t=PACK, r=RUN)
+        )
         nc.sync.dma_start(w4_raw[:].bitcast(I32), w4_words[0].bitcast(I32))
-        load_wd(0, 0)
-        load_wd(0, 1)
-        load_wd(1, 0)
-        load_wd(1, 1)
+        for pair in range(2):
+            for half in range(2):
+                load_wd(pair, half)
         load_x(2)
         load_x(3)
         load_plane(w4_plane_raw, w4_scales[0])
@@ -125,10 +152,7 @@ def tile_list_listed_hardswish_bottleneck_kernel(
             return words.rearrange("p (t q r) -> p q t r", t=PACK, r=RUN)
 
         def listed(b):
-            return offsets[:, b * P * PACK // 16 : (b + 1) * P * PACK // 16]
-
-        def stationary(b, t):
-            return slice((t * PASSES + b) * P, (t * PASSES + b + 1) * P)
+            return offsets[:, b * P * PACK // GROUP : (b + 1) * P * PACK // GROUP]
 
         v_codes = [held([P, PACK * P], U32, f"v_codes{b}") for b in range(PASSES)]
         picked_plane = held([P, S], U8, "picked_plane")
@@ -139,8 +163,6 @@ def tile_list_listed_hardswish_bottleneck_kernel(
 
         def gather_plane():
             nc.vector.tensor_copy(picked_plane[:], tab_plane[:].indirect(offsets[:]))
-
-        def deal_plane():
             nc.vector.tensor_copy(
                 v_plane[:].bitcast(I32).rearrange("p (t q w) -> p t q w", t=PACK, w=RUN // 4),
                 picked_plane[:].bitcast(I32).rearrange("p (q t w) -> p t q w", t=PACK, w=RUN // 4),
@@ -160,16 +182,17 @@ def tile_list_listed_hardswish_bottleneck_kernel(
         x_codes = {}
         x_plane = held([P, M], U8, "x_plane")
 
-        def round_x_scalar(n, into):
+        def round_x_scalar(strip, into):
             nc.scalar.copy(
-                into.rearrange("p (c e i) -> p c i e", e=2, i=PACK), x_raw[n][:].rearrange("p i (c e) -> p c i e", e=2)
+                into.rearrange("p (c e i) -> p c i e", e=2, i=PACK),
+                x_raw[strip][:].rearrange("p i (c e) -> p c i e", e=2),
             )
 
-        def round_x_pool(n, into):
-            pool_round(into.rearrange("p (c i) -> p c i", i=PACK), x_raw[n][:].rearrange("p i c -> p c i"))
+        def round_x_pool(strip, into):
+            pool_round(into.rearrange("p (c i) -> p c i", i=PACK), x_raw[strip][:].rearrange("p i c -> p c i"))
 
-        def quantize_x(lo, hi, x_bf, on=None, skip=0):
-            codes = held([P, hi - lo], U32, f"x_codes{lo}", on, skip)
+        def quantize_x(lo, hi, x_bf):
+            codes = held([P, hi - lo], U32, f"x_codes{lo}")
             nc.vector.quantize_mx(out=codes[:].bitcast(FP8X4), scales=x_plane[:, lo:hi], in_=x_bf)
             for m0 in range(lo, hi, BANK_M):
                 x_codes[m0] = codes[:, m0 - lo : m0 - lo + BANK_M]
@@ -178,6 +201,7 @@ def tile_list_listed_hardswish_bottleneck_kernel(
         wd_plane = [held([P, PACK, P], U8, f"wd_plane{b}") for b in range(PASSES)]
         wd_bf = {}
         pair_words = {}
+        turned = {}
 
         def round_wd(pair, lo, hi, copy):
             half = lo // HALF
@@ -186,10 +210,8 @@ def tile_list_listed_hardswish_bottleneck_kernel(
                 wd_raw[pair, half][:, :, lo - half * HALF : hi - half * HALF].rearrange("p e c -> p c e"),
             )
 
-        turned = {}
-
-        def gather_wd(pair, b, on=None, skip=0):
-            picked = held([P, PACK * P], U32, f"picked{pair}{b}", on, skip)
+        def gather_wd(pair, b):
+            picked = held([P, PACK * P], U32, f"picked{pair}{b}")
             nc.vector.tensor_copy(dealt(picked[:]), pair_words[pair][:].indirect(listed(b)))
             turned[pair, b] = y_psum.tile([P, PACK, P], F32, name="turned", tag="y")
             for t in range(PACK):
@@ -200,24 +222,24 @@ def tile_list_listed_hardswish_bottleneck_kernel(
                 wd_bf[b] = held([P, PACK, P, PACK], BF16, f"wd_bf{b}")
             nc.scalar.copy(
                 wd_bf[b][:, 2 * pair : 2 * pair + 2, :, :],
-                turned[pair, b][:].bitcast(BF16).rearrange("p t (n e) -> p e n t", e=2),
+                turned[pair, b][:].bitcast(BF16).rearrange("p t (c e) -> p e c t", e=2),
             )
 
         def quantize_wd(b):
             nc.vector.quantize_mx(
                 out=wd_codes[b][:].rearrange("p s c -> p (s c)").bitcast(FP8X4),
                 scales=wd_plane[b][:].rearrange("p s c -> p (s c)"),
-                in_=wd_bf[b][:].rearrange("p s n t -> p (s n t)"),
+                in_=wd_bf[b][:].rearrange("p s c t -> p (s c t)"),
             )
 
-        def deal_w4_codes(on=None, skip=0):
-            codes = held([P, PACK, 2 * P], U8, "w4_codes", on, skip)
-            nc.vector.tensor_copy(codes[:].bitcast(U16), w4_raw[:].bitcast(U16).rearrange("p (n s) -> p s n", s=PACK))
+        def deal_w4_codes():
+            codes = held([P, PACK, 2 * P], U8, "w4_codes")
+            nc.vector.tensor_copy(codes[:].bitcast(U16), w4_raw[:].bitcast(U16).rearrange("p (c s) -> p s c", s=PACK))
             return codes
 
-        def deal_w4_plane(on=None, skip=0):
-            plane = held([P, PACK, P], U8, "w4_plane", on, skip)
-            nc.gpsimd.tensor_copy(plane[:], w4_plane_raw[:].rearrange("p (n s) -> p s n", s=PACK))
+        def deal_w4_plane():
+            plane = held([P, PACK, P], U8, "w4_plane")
+            nc.gpsimd.tensor_copy(plane[:], w4_plane_raw[:].rearrange("p (c s) -> p s c", s=PACK))
             return plane
 
         a_banks = {}
@@ -227,18 +249,18 @@ def tile_list_listed_hardswish_bottleneck_kernel(
         h_codes = {}
         h_plane = {}
 
-        def project(unit, first=None, end=None, on=None, skip=0):
+        def project(unit):
             b, lo, hi = unit
-            if unit not in lifted:
-                lifted[unit] = held([P, PACK, hi - lo], F32, f"lifted{b}_{lo}", on, skip)
-            for m0 in range(first or lo, end or hi, BANK_M):
+            lifted[unit] = held([P, PACK, hi - lo], F32, f"lifted{b}_{lo}")
+            for m0 in range(lo, hi, BANK_M):
                 bank = a_psum.tile([P, PACK, BANK_M], F32, name="a_bank")
                 a_banks[b, m0] = bank
                 for t in range(PACK):
+                    plane0 = (t * PASSES + b) * P
                     nc.tensor.matmul_mx(
                         out=bank[:, t, :],
                         lhsT=v_codes[b][:, t * P : (t + 1) * P].bitcast(FP8X4),
-                        lhsT_scale=v_plane[:, stationary(b, t)],
+                        lhsT_scale=v_plane[:, plane0 : plane0 + P],
                         rhs=x_codes[m0].bitcast(FP8X4),
                         rhs_scale=x_plane[:, m0 : m0 + BANK_M],
                         start=True,
@@ -246,61 +268,58 @@ def tile_list_listed_hardswish_bottleneck_kernel(
                     )
                 nc.scalar.activation(lifted[unit][:, :, m0 - lo : m0 - lo + BANK_M], bank[:], ACT.Relu, bias=3.0)
 
-        def gate(unit, on=None, skip=0):
+        def gate(unit):
             b, lo, hi = unit
-            gated[unit] = held([P, PACK, hi - lo], F32, f"gated{b}_{lo}", on, skip)
+            gated[unit] = held([P, PACK, hi - lo], F32, f"gated{b}_{lo}")
             for t in range(PACK):
                 nc.vector.tensor_scalar(
                     gated[unit][:, t, :], lifted[unit][:, t, :], 6.0, gain[:, b, t : t + 1], ALU.min, ALU.mult
                 )
 
-        def swish(unit, first=None, end=None, on=None, skip=0, base=None, top=None):
+        def hold_h(b, lo, hi):
+            h_bf[b, lo] = held([P, (hi - lo) * PACK], BF16, f"h_bf{b}_{lo}")
+
+        def swish(unit, first, end, tile_lo):
             b, lo, hi = unit
-            first, end = first or lo, end or hi
-            if base is None:
-                base = first
-                h_bf[b, base] = held([P, ((top or end) - first) * PACK], BF16, f"h_bf{b}_{first}", on, skip)
             for m0 in range(first, end, BANK_M):
                 c0 = m0 - lo
-                h0 = (m0 - base) * PACK
+                h0 = (m0 - tile_lo) * PACK
                 nc.vector.tensor_tensor(
-                    h_bf[b, base][:, h0 : h0 + BANK_M * PACK].rearrange("p (c e t) -> p c t e", e=2, t=PACK),
+                    h_bf[b, tile_lo][:, h0 : h0 + BANK_M * PACK].rearrange("p (c e t) -> p c t e", e=2, t=PACK),
                     a_banks[b, m0][:].rearrange("p t (c e) -> p c t e", e=2),
                     gated[unit][:, :, c0 : c0 + BANK_M].rearrange("p t (c e) -> p c t e", e=2),
                     ALU.mult,
                 )
 
-        def quantize_h(b, lo, hi, on=None, skip=0):
+        def swish_tile(unit, first, end):
+            hold_h(unit[0], first, end)
+            swish(unit, first, end, first)
+
+        def quantize_h(b, lo, hi):
             codes = held([P, hi - lo], U32, f"h_codes{b}_{lo}")
-            plane = held([P, hi - lo], U8, f"h_plane{b}_{lo}", on, skip)
+            plane = held([P, hi - lo], U8, f"h_plane{b}_{lo}")
             nc.vector.quantize_mx(out=codes[:].bitcast(FP8X4), scales=plane[:], in_=h_bf[b, lo][:])
             for m0 in range(lo, hi, BANK_M):
                 h_codes[b, m0] = codes[:, m0 - lo : m0 - lo + BANK_M]
                 h_plane[b, m0] = plane[:, m0 - lo : m0 - lo + BANK_M]
 
-        y_f32 = [held([P, PACK, STRIP], F32, f"y_f32_{n}") for n in range(M // STRIP - 1)]
+        y_f32 = [held([P, PACK, STRIP], F32, f"y_f32_{strip}") for strip in range(M // STRIP - 1)]
         y_last = {m0: held([P, PACK, BANK_M], F32, f"y_last{m0}") for m0 in range(M - STRIP, M, BANK_M)}
         y_bf = {}
+        y_bf_bank = {}
         y_codes = held([P, M], U32, "y_codes")
         y_plane = held([P, M], U8, "y_plane")
         y_rows = out_0.rearrange("(p s) m -> p s m", s=PACK)
         y_words = out_1[0].rearrange("p m s -> p (m s)")
-        y_banks = {}
 
-        def down(m0, spare=False):
-            if spare:
-                bank = a_psum.tile([P, PACK, BANK_M], F32, name="a_bank")
-            else:
-                bank = y_psum.tile([P, PACK, BANK_M], F32, name="y_bank", tag="y")
-            y_banks[m0] = bank
-            cols = slice(m0, m0 + BANK_M)
+        def down(m0, bank):
             for s in range(PACK):
                 nc.tensor.matmul_mx(
                     out=bank[:, s, :],
                     lhsT=w4_codes[:, s, :].bitcast(FP4X4),
                     lhsT_scale=w4_plane[:, s, :],
                     rhs=x_codes[m0].bitcast(FP8X4),
-                    rhs_scale=x_plane[:, cols],
+                    rhs_scale=x_plane[:, m0 : m0 + BANK_M],
                     start=(s == 0),
                     stop=False,
                 )
@@ -316,138 +335,132 @@ def tile_list_listed_hardswish_bottleneck_kernel(
                         stop=(b == PASSES - 1 and s == PACK - 1),
                     )
 
-        def hold_y_bf(lo, hi, on=None, skip=0):
-            tile = held([P, hi - lo, PACK], BF16, f"y_bf{lo}", on, skip)
-            y_bf[lo, hi] = tile
+        def hold_y(lo, hi):
+            y_bf[lo] = held([P, hi - lo, PACK], BF16, f"y_bf{lo}")
             for m0 in range(lo, hi, BANK_M):
-                y_bf[m0] = tile[:, m0 - lo : m0 - lo + BANK_M, :]
+                y_bf_bank[m0] = y_bf[lo][:, m0 - lo : m0 - lo + BANK_M, :]
 
-        def round_y_scalar(m0):
-            nc.scalar.copy(y_bf[m0], y_banks[m0][:].rearrange("p s m -> p m s"))
+        def down_strip(lo, rounded_end):
+            values = y_f32[lo // STRIP]
+            for m0 in range(lo, lo + STRIP, BANK_M):
+                bank = y_psum.tile([P, PACK, BANK_M], F32, name="y_bank", tag="y")
+                down(m0, bank)
+                nc.scalar.copy(values[:, :, m0 - lo : m0 - lo + BANK_M], bank[:])
+                if m0 + BANK_M == lo + STRIP:
+                    nc.sync.dma_start(y_rows[:, :, lo : lo + STRIP], values[:])
+                if m0 < rounded_end:
+                    nc.scalar.copy(y_bf_bank[m0], bank[:].rearrange("p s m -> p m s"))
 
-        def round_y_pool(lo, hi, m0):
-            pool_round(y_bf[lo, hi][:, m0 - lo : m0 - lo + STRIP, :], y_f32[m0 // STRIP][:].rearrange("p s m -> p m s"))
-
-        def copy_y(m0, copy):
-            c0 = m0 % STRIP
-            copy(y_f32[m0 // STRIP][:, :, c0 : c0 + BANK_M], y_banks[m0][:])
-
-        def copy_store_last(m0, queue):
-            nc.scalar.copy(y_last[m0][:], y_banks[m0][:])
+        def down_last(m0, queue):
+            bank = a_psum.tile([P, PACK, BANK_M], F32, name="a_bank")
+            down(m0, bank)
+            nc.scalar.copy(y_last[m0][:], bank[:])
             queue.dma_start(y_rows[:, :, m0 : m0 + BANK_M], y_last[m0][:])
 
-        def round_last(m0):
+        def round_y_vector(m0, values):
             nc.vector.tensor_copy(
-                y_bf[m0].rearrange("p (c e) s -> p c s e", e=2), y_last[m0][:].rearrange("p s (c e) -> p c s e", e=2)
+                y_bf_bank[m0].rearrange("p (c e) s -> p c s e", e=2), values.rearrange("p s (c e) -> p c s e", e=2)
             )
-
-        def store_y(lo, hi, queue):
-            c0 = lo % STRIP
-            queue.dma_start(y_rows[:, :, lo:hi], y_f32[lo // STRIP][:, :, c0 : c0 + hi - lo])
-
-        def down_strip(lo, rounded):
-            for m0 in range(lo, lo + STRIP, BANK_M):
-                down(m0)
-                copy_y(m0, nc.scalar.copy)
-                if m0 + BANK_M == lo + STRIP:
-                    store_y(lo, lo + STRIP, nc.sync)
-                if rounded:
-                    round_y_scalar(m0)
 
         def quantize_y(lo, hi):
             nc.vector.quantize_mx(
                 out=y_codes[:, lo:hi].bitcast(FP8X4),
                 scales=y_plane[:, lo:hi],
-                in_=y_bf[lo, hi][:].rearrange("p m s -> p (m s)"),
+                in_=y_bf[lo][:].rearrange("p m s -> p (m s)"),
             )
 
         def store_words(lo, hi):
             nc.sync.dma_start(y_words[:, lo * PACK : hi * PACK].bitcast(I32), y_codes[:, lo:hi].bitcast(I32))
 
-        first0, second0, front1 = (0, 0, 256), (0, 256, 512), (1, 0, 512)
-        back0, third1, last1 = (0, 512, 1024), (1, 512, 768), (1, 768, 1024)
+        first, second, third = (0, 0, 256), (0, 256, 512), (1, 0, 512)
+        fourth, fifth, sixth = (0, 512, 1024), (1, 512, 768), (1, 768, 1024)
+
         x_bf0 = held([P, STRIP * PACK], BF16, "x_bf0")
         round_x_scalar(0, x_bf0[:])
         turn_gain()
         gather_plane()
-        deal_plane()
         quantize_x(0, 256, x_bf0[:])
         gather_codes(0)
         gather_codes(1)
-        x_bf1 = held([P, STRIP * PACK], BF16, "x_bf1", "x_bf0")
+        x_bf1 = held([P, STRIP * PACK], BF16, "x_bf1")
         round_x_pool(1, x_bf1[:])
-        project(first0)
+        project(first)
         quantize_x(256, 512, x_bf1[:])
-        project(second0, on="early", skip=6 * KIB)
-        w4_codes = deal_w4_codes("x_bf0")
-        gate(first0)
-        gate(second0)
-        swish(first0, on="early", skip=8 * KIB, top=512)
-        swish(second0, base=0)
-        project(front1, on="window", skip=7 * KIB)
-        pair_words[0] = held([P, T], U32, "pair_words0", "early")
-        round_wd(0, 0, 768, nc.gpsimd.tensor_copy)
-        round_wd(0, 768, 1024, nc.scalar.copy)
-        round_wd(0, 1024, 1536, nc.scalar.copy)
-        round_wd(0, 1536, 2048, nc.scalar.copy)
+        project(second)
+        w4_codes = deal_w4_codes()
+        gate(first)
+        gate(second)
+        hold_h(0, 0, 512)
+        swish(first, 0, 256, 0)
+        swish(second, 256, 512, 0)
+        project(third)
+
+        pair_words[0] = held([P, T], U32, "pair_words0")
+        round_wd(0, 0, POOL_COLUMNS, nc.gpsimd.tensor_copy)
+        round_wd(0, POOL_COLUMNS, HALF, nc.scalar.copy)
+        round_wd(0, HALF, HALF + HALF // 2, nc.scalar.copy)
+        round_wd(0, HALF + HALF // 2, T, nc.scalar.copy)
         quantize_h(0, 0, 512)
-        gate(front1)
-        gather_wd(0, 0, "window", 12 * KIB)
-        gather_wd(0, 1, "window", 14 * KIB)
-        pair_words[1] = held([P, T], U32, "pair_words1", "window")
-        round_wd(1, 0, 1024, nc.gpsimd.tensor_copy)
-        round_wd(1, 1024, 2048, nc.scalar.copy)
-        back_x_bf = held([P, 2 * STRIP * PACK], BF16, "back_x_bf", "window", 8 * KIB)
+        gate(third)
+        gather_wd(0, 0)
+        gather_wd(0, 1)
+        pair_words[1] = held([P, T], U32, "pair_words1")
+        round_wd(1, 0, HALF, nc.gpsimd.tensor_copy)
+        round_wd(1, HALF, T, nc.scalar.copy)
+        back_x_bf = held([P, 2 * STRIP * PACK], BF16, "back_x_bf")
         round_x_pool(2, back_x_bf[:, : STRIP * PACK])
         round_x_pool(3, back_x_bf[:, STRIP * PACK :])
         copy_turned(0, 0)
         copy_turned(0, 1)
-        gather_wd(1, 0)
-        copy_turned(1, 0)
-        gather_wd(1, 1)
-        copy_turned(1, 1)
-        swish(front1, 0, 256, "window")
-        quantize_x(512, 1024, back_x_bf[:], "window", 2 * KIB)
-        project(back0)
-        swish(front1, 256, 512, "window", 10 * KIB)
-        project(third1, on="late", skip=2 * KIB)
-        w4_plane = deal_w4_plane("window", 8 * KIB)
-        quantize_h(1, 0, 256, "window", 8 * KIB + 512)
+        for b in range(PASSES):
+            gather_wd(1, b)
+            copy_turned(1, b)
+        swish_tile(third, 0, 256)
+        quantize_x(512, 1024, back_x_bf[:])
+        project(fourth)
+        swish_tile(third, 256, 512)
+        project(fifth)
+        w4_plane = deal_w4_plane()
+        quantize_h(1, 0, 256)
         quantize_wd(0)
         quantize_h(1, 256, 512)
         quantize_wd(1)
-        down_strip(0, False)
-        gate(back0)
-        gate(third1)
-        hold_y_bf(0, 256, "late", 2 * KIB)
-        round_y_pool(0, 256, 0)
-        swish(back0, 512, 768, "late", 4 * KIB)
-        project(last1)
-        hold_y_bf(256, 768)
-        down_strip(256, True)
-        swish(third1)
+
+        down_strip(0, 0)
+        gate(fourth)
+        gate(fifth)
+        hold_y(0, 256)
+        pool_round(y_bf[0][:], y_f32[0][:].rearrange("p s m -> p m s"))
+        swish_tile(fourth, 512, 768)
+        project(sixth)
+        hold_y(256, 512)
+        down_strip(256, 512)
+        swish_tile(fifth, 512, 768)
         quantize_h(0, 512, 768)
+        quantize_h(1, 512, 768)
+        hold_y(512, 768)
+        down_strip(512, 640)
+        swish_tile(fourth, 768, 1024)
+        gate(sixth)
+        quantize_h(0, 768, 1024)
+
+        swish_tile(sixth, 768, 896)
         quantize_y(0, 256)
         store_words(0, 256)
-        quantize_h(1, 512, 768)
-        down_strip(512, True)
-        swish(back0, 768, 1024, "late", 2 * KIB)
-        gate(last1)
-        quantize_h(0, 768, 1024)
-        swish(last1, 768, 896)
-        swish(last1, 896, 1024)
         quantize_h(1, 768, 896)
-        hold_y_bf(768, 896)
-        hold_y_bf(896, 1024)
-        down(768, True)
-        copy_store_last(768, nc.sync)
+        hold_y(768, 896)
+        hold_y(896, 1024)
+        down_last(768, nc.sync)
+        swish_tile(sixth, 896, 1024)
+        quantize_y(256, 512)
+        store_words(256, 512)
         quantize_h(1, 896, 1024)
-        down(896, True)
-        copy_store_last(896, nc.scalar)
-        quantize_y(256, 768)
-        store_words(256, 768)
-        round_last(768)
-        round_last(896)
+        down_last(896, nc.scalar)
+        round_y_vector(640, y_f32[2][:, :, BANK_M:])
+        round_y_vector(768, y_last[768][:])
+        quantize_y(512, 768)
+        store_words(512, 768)
+        round_y_vector(896, y_last[896][:])
         quantize_y(768, 896)
         quantize_y(896, 1024)
         store_words(768, 1024)

@@ -26,14 +26,21 @@ BANK_M = 128
 STRIP = 256
 HALF = T // 2
 GROUP = 16
-POOL_COLUMNS = 896
-A_BANKS = 6
-Y_BANKS = 2
+POOL_FIRST = 768
+POOL_LAST = 256
+BANK_BYTES = 2048
 KIB = 1024
 ALIGN = 64
 WIDTH = {F32: 4, BF16: 2, U32: 4, U8: 1}
 
-REGIONS = (("early", 12 * KIB), ("window", 16 * KIB), ("first_x", 4 * KIB), ("last_wd", 8 * KIB), ("late", 8 * KIB))
+A_BANK = {(0, 0): 0, (0, 128): 1, (0, 256): 2, (0, 384): 3, (1, 0): 4, (1, 128): 5, (1, 256): 6, (1, 384): 7,
+          (0, 512): 0, (0, 640): 1, (1, 512): 2, (1, 640): 3, (0, 768): 0, (0, 896): 1, (1, 768): 4, (1, 896): 5}
+TURN_BANK = {(0, 0): 4, (0, 1): 5, (1, 0): 6, (1, 1): 7}
+Y_BANK = {0: 2, 128: 3, 256: 6, 384: 7, 512: 2, 640: 3, 768: 0, 896: 1}
+GAIN_BANK = 7
+
+REGIONS = (("first_x", 4 * KIB), ("second", 6 * KIB), ("third", 8 * KIB), ("fifth", 11 * KIB),
+           ("last_wd", 11 * KIB), ("seventh", 5 * KIB))
 
 TENANTS = {
     "x_raw0": ("first_x", 0),
@@ -41,28 +48,24 @@ TENANTS = {
     "v_codes1": ("first_x", 2 * KIB),
     "x_bf1": ("x_bf0", 0),
     "w4_codes": ("x_bf0", 0),
-    "lifted0_256": ("early", 6 * KIB),
-    "h_bf0_0": ("early", 8 * KIB),
-    "pair_words0": ("early", 0),
-    "lifted1_0": ("window", 7 * KIB),
-    "picked00": ("window", 12 * KIB),
-    "picked01": ("window", 14 * KIB),
-    "pair_words1": ("window", 0),
-    "back_x_bf": ("window", 8 * KIB),
-    "h_bf1_0": ("window", 0),
-    "x_codes512": ("window", 2 * KIB),
-    "h_bf1_256": ("window", 10 * KIB),
-    "w4_plane": ("window", 8 * KIB),
-    "h_plane1_0": ("window", 8 * KIB + 512),
-    "wd_plane0": ("window", 9 * KIB),
-    "wd_plane1": ("window", 9 * KIB + 512),
-    "wd_raw11": ("last_wd", 0),
+    "lifted0_256": ("second", 1 * KIB),
+    "x_bf2": ("second", 0),
+    "h_bf0_0": ("second", 2 * KIB),
+    "lifted1_0": ("third", 0),
+    "pair_words0": ("third", 0),
+    "h_bf0_512": ("wd_raw01", 0),
+    "lifted1_512": ("fifth", 7 * KIB),
+    "pair_words1": ("fifth", 0),
+    "x_bf3": ("fifth", 8 * KIB),
+    "w4_plane": ("fifth", 10 * KIB),
+    "wd_raw11": ("last_wd", 3 * KIB),
     "wd_bf0": ("last_wd", 0),
-    "wd_bf1": ("last_wd", 4 * KIB),
-    "lifted1_512": ("late", 2 * KIB),
-    "y_bf0": ("late", 2 * KIB),
-    "h_bf0_512": ("late", 4 * KIB),
-    "h_bf0_768": ("late", 4 * KIB),
+    "h_bf1_512": ("last_wd", 4 * KIB),
+    "h_codes0_512": ("last_wd", 6 * KIB),
+    "wd_bf1": ("last_wd", 7 * KIB),
+    "lifted1_768": ("seventh", 0),
+    "y_bf0": ("seventh", 0),
+    "h_bf0_768": ("seventh", 3 * KIB),
 }
 
 
@@ -73,8 +76,10 @@ def tile_list_listed_hardswish_bottleneck_kernel(
     with ExitStack() as ctx:
         lists = ctx.enter_context(tc.tile_pool(name="lists", bufs=1))
         keep = ctx.enter_context(tc.tile_pool(name="keep", bufs=1))
-        a_psum = ctx.enter_context(tc.psum_pool(name="a_psum", bufs=A_BANKS))
-        y_psum = ctx.enter_context(tc.psum_pool(name="y_psum", bufs=Y_BANKS))
+        psum = ctx.enter_context(tc.psum_pool(name="psum", bufs=1))
+
+        def banked(shape, name, bank):
+            return psum.tile(shape, F32, name=name, offset=bank * BANK_BYTES)
 
         places = {"top": 0}
 
@@ -138,10 +143,10 @@ def tile_list_listed_hardswish_bottleneck_kernel(
             g_rows[:PACK, :].rearrange("t (q r) -> t q r", r=RUN), g.rearrange("(q t r) -> t q r", t=PACK, r=RUN)
         )
         nc.sync.dma_start(w4_raw[:].bitcast(I32), w4_words[0].bitcast(I32))
+        load_x(2)
         for pair in range(2):
             for half in range(2):
                 load_wd(pair, half)
-        load_x(2)
         load_x(3)
         load_plane(w4_plane_raw, w4_scales[0])
 
@@ -171,7 +176,7 @@ def tile_list_listed_hardswish_bottleneck_kernel(
         gain = held([P, PASSES, PACK], F32, "gain")
 
         def turn_gain():
-            g_bank = y_psum.tile([P, PASSES, P], F32, name="g_bank", tag="y")
+            g_bank = banked([P, PASSES, P], "g_bank", GAIN_BANK)
             for b in range(PASSES):
                 nc.tensor.transpose(g_bank[:, b, :], g_rows[:, b * P : (b + 1) * P], ident[:])
             nc.scalar.copy(gain[:], g_bank[:, :, :PACK])
@@ -213,7 +218,7 @@ def tile_list_listed_hardswish_bottleneck_kernel(
         def gather_wd(pair, b):
             picked = held([P, PACK * P], U32, f"picked{pair}{b}")
             nc.vector.tensor_copy(dealt(picked[:]), pair_words[pair][:].indirect(listed(b)))
-            turned[pair, b] = y_psum.tile([P, PACK, P], F32, name="turned", tag="y")
+            turned[pair, b] = banked([P, PACK, P], f"turned{pair}{b}", TURN_BANK[pair, b])
             for t in range(PACK):
                 nc.tensor.transpose(turned[pair, b][:, t, :], picked[:, t * P : (t + 1) * P].bitcast(F32), ident[:])
 
@@ -253,7 +258,7 @@ def tile_list_listed_hardswish_bottleneck_kernel(
             b, lo, hi = unit
             lifted[unit] = held([P, PACK, hi - lo], F32, f"lifted{b}_{lo}")
             for m0 in range(lo, hi, BANK_M):
-                bank = a_psum.tile([P, PACK, BANK_M], F32, name="a_bank")
+                bank = banked([P, PACK, BANK_M], f"a_bank{b}_{m0}", A_BANK[b, m0])
                 a_banks[b, m0] = bank
                 for t in range(PACK):
                     plane0 = (t * PASSES + b) * P
@@ -340,26 +345,30 @@ def tile_list_listed_hardswish_bottleneck_kernel(
             for m0 in range(lo, hi, BANK_M):
                 y_bf_bank[m0] = y_bf[lo][:, m0 - lo : m0 - lo + BANK_M, :]
 
-        def down_strip(lo, rounded_end):
+        y_banks = {}
+
+        def round_y_scalar(m0):
+            nc.scalar.copy(y_bf_bank[m0], y_banks[m0][:].rearrange("p s m -> p m s"))
+
+        def down_strip(lo, rounded):
             values = y_f32[lo // STRIP]
             for m0 in range(lo, lo + STRIP, BANK_M):
-                bank = y_psum.tile([P, PACK, BANK_M], F32, name="y_bank", tag="y")
-                down(m0, bank)
-                nc.scalar.copy(values[:, :, m0 - lo : m0 - lo + BANK_M], bank[:])
-                if m0 + BANK_M == lo + STRIP:
-                    nc.sync.dma_start(y_rows[:, :, lo : lo + STRIP], values[:])
-                if m0 < rounded_end:
-                    nc.scalar.copy(y_bf_bank[m0], bank[:].rearrange("p s m -> p m s"))
+                y_banks[m0] = banked([P, PACK, BANK_M], f"y_bank{m0}", Y_BANK[m0])
+                down(m0, y_banks[m0])
+                nc.scalar.copy(values[:, :, m0 - lo : m0 - lo + BANK_M], y_banks[m0][:])
+            nc.sync.dma_start(y_rows[:, :, lo : lo + STRIP], values[:])
+            for m0 in rounded:
+                round_y_scalar(m0)
 
         def down_last(m0, queue):
-            bank = a_psum.tile([P, PACK, BANK_M], F32, name="a_bank")
+            bank = banked([P, PACK, BANK_M], f"y_bank{m0}", Y_BANK[m0])
             down(m0, bank)
             nc.scalar.copy(y_last[m0][:], bank[:])
             queue.dma_start(y_rows[:, :, m0 : m0 + BANK_M], y_last[m0][:])
 
-        def round_y_vector(m0, values):
+        def round_y_vector(into, values):
             nc.vector.tensor_copy(
-                y_bf_bank[m0].rearrange("p (c e) s -> p c s e", e=2), values.rearrange("p s (c e) -> p c s e", e=2)
+                into.rearrange("p (c e) s -> p c s e", e=2), values.rearrange("p s (c e) -> p c s e", e=2)
             )
 
         def quantize_y(lo, hi):
@@ -373,96 +382,97 @@ def tile_list_listed_hardswish_bottleneck_kernel(
             nc.sync.dma_start(y_words[:, lo * PACK : hi * PACK].bitcast(I32), y_codes[:, lo:hi].bitcast(I32))
 
         first, second, third = (0, 0, 256), (0, 256, 512), (1, 0, 512)
-        fourth, fifth, sixth = (0, 512, 1024), (1, 512, 768), (1, 768, 1024)
+        fourth, fifth, sixth, seventh = (0, 512, 768), (1, 512, 768), (0, 768, 1024), (1, 768, 1024)
+        x_bf = {}
 
-        x_bf0 = held([P, STRIP * PACK], BF16, "x_bf0")
-        round_x_scalar(0, x_bf0[:])
+        def round_x(strip, rounder):
+            x_bf[strip] = held([P, STRIP * PACK], BF16, f"x_bf{strip}")
+            rounder(strip, x_bf[strip][:])
+
+        def quantize_strip(strip):
+            quantize_x(strip * STRIP, (strip + 1) * STRIP, x_bf[strip][:])
+
+        round_x(0, round_x_scalar)
         turn_gain()
         gather_plane()
-        quantize_x(0, 256, x_bf0[:])
+        quantize_strip(0)
         gather_codes(0)
         gather_codes(1)
-        x_bf1 = held([P, STRIP * PACK], BF16, "x_bf1")
-        round_x_pool(1, x_bf1[:])
+        round_x(1, round_x_pool)
         project(first)
-        quantize_x(256, 512, x_bf1[:])
+        quantize_strip(1)
         project(second)
+        project(third)
         w4_codes = deal_w4_codes()
         gate(first)
         gate(second)
+        round_x(2, round_x_pool)
         hold_h(0, 0, 512)
         swish(first, 0, 256, 0)
         swish(second, 256, 512, 0)
-        project(third)
-
-        pair_words[0] = held([P, T], U32, "pair_words0")
-        round_wd(0, 0, POOL_COLUMNS, nc.gpsimd.tensor_copy)
-        round_wd(0, POOL_COLUMNS, HALF, nc.scalar.copy)
-        round_wd(0, HALF, HALF + HALF // 2, nc.scalar.copy)
-        round_wd(0, HALF + HALF // 2, T, nc.scalar.copy)
+        quantize_strip(2)
+        project(fourth)
+        project(fifth)
         quantize_h(0, 0, 512)
         gate(third)
-        gather_wd(0, 0)
-        gather_wd(0, 1)
+        pair_words[0] = held([P, T], U32, "pair_words0")
+        round_wd(0, 0, POOL_FIRST, nc.gpsimd.tensor_copy)
+        round_wd(0, POOL_FIRST, HALF, nc.scalar.copy)
+        round_wd(0, HALF, T, nc.scalar.copy)
+        swish_tile(third, 0, 512)
+        gate(fourth)
+        quantize_h(1, 0, 512)
+        gate(fifth)
+
         pair_words[1] = held([P, T], U32, "pair_words1")
         round_wd(1, 0, HALF, nc.gpsimd.tensor_copy)
-        round_wd(1, HALF, T, nc.scalar.copy)
-        back_x_bf = held([P, 2 * STRIP * PACK], BF16, "back_x_bf")
-        round_x_pool(2, back_x_bf[:, : STRIP * PACK])
-        round_x_pool(3, back_x_bf[:, STRIP * PACK :])
+        round_wd(1, HALF, HALF + POOL_LAST, nc.gpsimd.tensor_copy)
+        round_wd(1, HALF + POOL_LAST, T, nc.scalar.copy)
+        round_x(3, round_x_pool)
+        w4_plane = deal_w4_plane()
+        gather_wd(0, 0)
+        gather_wd(0, 1)
         copy_turned(0, 0)
         copy_turned(0, 1)
+        swish_tile(fourth, 512, 768)
         for b in range(PASSES):
             gather_wd(1, b)
             copy_turned(1, b)
-        swish_tile(third, 0, 256)
-        quantize_x(512, 1024, back_x_bf[:])
-        project(fourth)
-        swish_tile(third, 256, 512)
-        project(fifth)
-        w4_plane = deal_w4_plane()
-        quantize_h(1, 0, 256)
+        quantize_strip(3)
+        project(sixth)
+        project(seventh)
+        swish_tile(fifth, 512, 768)
         quantize_wd(0)
-        quantize_h(1, 256, 512)
+        quantize_h(0, 512, 768)
         quantize_wd(1)
+        quantize_h(1, 512, 768)
 
-        down_strip(0, 0)
-        gate(fourth)
-        gate(fifth)
+        down_strip(0, ())
+        gate(sixth)
+        gate(seventh)
+        down_strip(256, ())
         hold_y(0, 256)
         pool_round(y_bf[0][:], y_f32[0][:].rearrange("p s m -> p m s"))
-        swish_tile(fourth, 512, 768)
-        project(sixth)
-        hold_y(256, 512)
-        down_strip(256, 512)
-        swish_tile(fifth, 512, 768)
-        quantize_h(0, 512, 768)
-        quantize_h(1, 512, 768)
-        hold_y(512, 768)
-        down_strip(512, 640)
-        swish_tile(fourth, 768, 1024)
-        gate(sixth)
+        hold_y(256, 768)
+        down_strip(512, (384, 512))
+        swish_tile(sixth, 768, 1024)
+        swish_tile(seventh, 768, 896)
+        swish_tile(seventh, 896, 1024)
         quantize_h(0, 768, 1024)
-
-        swish_tile(sixth, 768, 896)
+        quantize_h(1, 768, 896)
+        quantize_h(1, 896, 1024)
+        hold_y(768, 1024)
+        down_last(768, nc.sync)
+        down_last(896, nc.scalar)
         quantize_y(0, 256)
         store_words(0, 256)
-        quantize_h(1, 768, 896)
-        hold_y(768, 896)
-        hold_y(896, 1024)
-        down_last(768, nc.sync)
-        swish_tile(sixth, 896, 1024)
-        quantize_y(256, 512)
-        store_words(256, 512)
-        quantize_h(1, 896, 1024)
-        down_last(896, nc.scalar)
-        round_y_vector(640, y_f32[2][:, :, BANK_M:])
-        round_y_vector(768, y_last[768][:])
-        quantize_y(512, 768)
-        store_words(512, 768)
-        round_y_vector(896, y_last[896][:])
-        quantize_y(768, 896)
-        quantize_y(896, 1024)
+        round_y_vector(y_bf_bank[256], y_f32[1][:, :, :BANK_M])
+        round_y_vector(y_bf_bank[640], y_f32[2][:, :, BANK_M:])
+        round_y_vector(y_bf_bank[768], y_last[768][:])
+        quantize_y(256, 768)
+        store_words(256, 768)
+        round_y_vector(y_bf_bank[896], y_last[896][:])
+        quantize_y(768, 1024)
         store_words(768, 1024)
         for q in range(QUADRANTS):
             queue = nc.sync if q < QUADRANTS // 2 else nc.scalar

@@ -26,21 +26,20 @@ BANK_M = 128
 STRIP = 256
 HALF = T // 2
 GROUP = 16
-POOL_FIRST = 768
-POOL_LAST = 256
+POOL_COLUMNS = 896
+WD_LOADS = {"00": (0, 0, HALF), "01": (0, HALF, T), "10": (1, 0, HALF), "11": (1, HALF, T)}
 BANK_BYTES = 2048
+A_BANK = {(0, 0): 0, (0, 128): 1, (0, 256): 2, (0, 384): 3, (1, 0): 4, (1, 128): 5, (1, 256): 6, (1, 384): 7,
+          (0, 512): 0, (0, 640): 1, (1, 512): 4, (1, 640): 5, (0, 768): 2, (0, 896): 3, (1, 768): 0, (1, 896): 1}
+TURN_BANK = {(0, 0): 2, (0, 1): 3, (1, 0): 2, (1, 1): 3}
+Y_BANK = {0: 6, 256: 6, 512: 4, 768: 2, 896: 3}
+GAIN_BANK = 7
 KIB = 1024
 ALIGN = 64
 WIDTH = {F32: 4, BF16: 2, U32: 4, U8: 1}
 
-A_BANK = {(0, 0): 0, (0, 128): 1, (0, 256): 2, (0, 384): 3, (1, 0): 4, (1, 128): 5, (1, 256): 6, (1, 384): 7,
-          (0, 512): 0, (0, 640): 1, (1, 512): 2, (1, 640): 3, (0, 768): 0, (0, 896): 1, (1, 768): 4, (1, 896): 5}
-TURN_BANK = {(0, 0): 4, (0, 1): 5, (1, 0): 6, (1, 1): 7}
-Y_BANK = {0: 2, 128: 3, 256: 6, 384: 7, 512: 2, 640: 3, 768: 0, 896: 1}
-GAIN_BANK = 7
-
-REGIONS = (("first_x", 4 * KIB), ("second", 6 * KIB), ("third", 8 * KIB), ("fifth", 11 * KIB),
-           ("last_wd", 11 * KIB), ("seventh", 5 * KIB))
+REGIONS = (("early", 12 * KIB), ("first_x", 4 * KIB), ("third_x", 8 * KIB),
+           ("last_x", 7 * KIB), ("last_wd", 16 * KIB), ("last_pick", 4 * KIB))
 
 TENANTS = {
     "x_raw0": ("first_x", 0),
@@ -48,24 +47,30 @@ TENANTS = {
     "v_codes1": ("first_x", 2 * KIB),
     "x_bf1": ("x_bf0", 0),
     "w4_codes": ("x_bf0", 0),
-    "lifted0_256": ("second", 1 * KIB),
-    "x_bf2": ("second", 0),
-    "h_bf0_0": ("second", 2 * KIB),
-    "lifted1_0": ("third", 0),
-    "pair_words0": ("third", 0),
-    "h_bf0_512": ("wd_raw01", 0),
-    "lifted1_512": ("fifth", 7 * KIB),
-    "pair_words1": ("fifth", 0),
-    "x_bf3": ("fifth", 8 * KIB),
-    "w4_plane": ("fifth", 10 * KIB),
-    "wd_raw11": ("last_wd", 3 * KIB),
-    "wd_bf0": ("last_wd", 0),
-    "h_bf1_512": ("last_wd", 4 * KIB),
-    "h_codes0_512": ("last_wd", 6 * KIB),
-    "wd_bf1": ("last_wd", 7 * KIB),
-    "lifted1_768": ("seventh", 0),
-    "y_bf0": ("seventh", 0),
-    "h_bf0_768": ("seventh", 3 * KIB),
+    "lifted0_256": ("early", 6 * KIB),
+    "h_bf0_0": ("early", 8 * KIB),
+    "pair_words0": ("early", 0),
+    "x_raw2": ("third_x", 1 * KIB),
+    "picked00": ("third_x", 0),
+    "picked01": ("third_x", 2 * KIB),
+    "h_bf1_0": ("third_x", 4 * KIB),
+    "w4_plane": ("x_bf2", 0),
+    "x_bf3": ("lifted1_0", 0),
+    "x_raw3": ("last_x", 3 * KIB),
+    "h_codes1_0": ("last_x", 3 * KIB),
+    "h_codes1_256": ("last_x", 4 * KIB),
+    "wd_raw11": ("last_wd", 5 * KIB),
+    "lifted0_512": ("last_wd", 12 * KIB),
+    "picked11": ("last_pick", 0),
+    "lifted1_512": ("last_pick", 0),
+    "h_bf1_256": ("wd_raw10", 0),
+    "gated0_512": ("wd_raw10", 2 * KIB),
+    "wd_bf0": ("last_wd", 3 * KIB),
+    "wd_bf1": ("last_wd", 8 * KIB),
+    "x_codes768": ("last_wd", 3 * KIB),
+    "h_bf0_512": ("last_wd", 8 * KIB),
+    "h_bf1_512": ("last_wd", 10 * KIB),
+    "y_bf0": ("lifted1_768", 0),
 }
 
 
@@ -123,11 +128,10 @@ def tile_list_listed_hardswish_bottleneck_kernel(
         wd_rows = wdT.rearrange("(p s) c -> p s c", s=PACK)
         wd_raw = {}
 
-        def load_wd(pair, half):
-            wd_raw[pair, half] = held([P, 2, HALF], F32, f"wd_raw{pair}{half}")
-            nc.sync.dma_start(
-                wd_raw[pair, half][:], wd_rows[:, 2 * pair : 2 * pair + 2, half * HALF : (half + 1) * HALF]
-            )
+        def load_wd(piece):
+            pair, lo, hi = WD_LOADS[piece]
+            wd_raw[piece] = held([P, 2, hi - lo], F32, f"wd_raw{piece}")
+            nc.sync.dma_start(wd_raw[piece][:], wd_rows[:, 2 * pair : 2 * pair + 2, lo:hi])
 
         g_rows = held([P, PASSES * P], F32, "g_rows")
         nc.gpsimd.memset(g_rows[:], 0.0)
@@ -143,12 +147,13 @@ def tile_list_listed_hardswish_bottleneck_kernel(
             g_rows[:PACK, :].rearrange("t (q r) -> t q r", r=RUN), g.rearrange("(q t r) -> t q r", t=PACK, r=RUN)
         )
         nc.sync.dma_start(w4_raw[:].bitcast(I32), w4_words[0].bitcast(I32))
+        load_wd("00")
+        load_wd("01")
         load_x(2)
-        for pair in range(2):
-            for half in range(2):
-                load_wd(pair, half)
-        load_x(3)
         load_plane(w4_plane_raw, w4_scales[0])
+        load_wd("10")
+        load_wd("11")
+        load_x(3)
 
         ident = held([P, P], F32, "ident")
         make_identity(nc, ident[:])
@@ -181,10 +186,20 @@ def tile_list_listed_hardswish_bottleneck_kernel(
                 nc.tensor.transpose(g_bank[:, b, :], g_rows[:, b * P : (b + 1) * P], ident[:])
             nc.scalar.copy(gain[:], g_bank[:, :, :PACK])
 
+        gain_shift = held([P, PACK], F32, "gain_shift")
+        gain_upper = held([P, PACK], F32, "gain_upper")
+        gain_lower = held([P, PACK], F32, "gain_lower")
+
+        def bound_gain(b):
+            nc.gpsimd.tensor_scalar(gain_shift[:], gain[:, b, :], 3.0, 0.0, ALU.mult, ALU.add)
+            nc.gpsimd.tensor_scalar(gain_upper[:], gain[:, b, :], 6.0, 0.0, ALU.mult, ALU.max)
+            nc.gpsimd.tensor_scalar(gain_lower[:], gain[:, b, :], 6.0, 0.0, ALU.mult, ALU.min)
+
         def pool_round(into, values):
             nc.gpsimd.tensor_scalar(into, values, 1.0, 0.0, ALU.mult, ALU.add)
 
         x_codes = {}
+        x_strip = {}
         x_plane = held([P, M], U8, "x_plane")
 
         def round_x_scalar(strip, into):
@@ -201,6 +216,8 @@ def tile_list_listed_hardswish_bottleneck_kernel(
             nc.vector.quantize_mx(out=codes[:].bitcast(FP8X4), scales=x_plane[:, lo:hi], in_=x_bf)
             for m0 in range(lo, hi, BANK_M):
                 x_codes[m0] = codes[:, m0 - lo : m0 - lo + BANK_M]
+            for m0 in range(lo, hi, STRIP):
+                x_strip[m0] = codes[:, m0 - lo : m0 - lo + STRIP]
 
         wd_codes = [held([P, PACK, P], U32, f"wd_codes{b}") for b in range(PASSES)]
         wd_plane = [held([P, PACK, P], U8, f"wd_plane{b}") for b in range(PASSES)]
@@ -208,11 +225,11 @@ def tile_list_listed_hardswish_bottleneck_kernel(
         pair_words = {}
         turned = {}
 
-        def round_wd(pair, lo, hi, copy):
-            half = lo // HALF
+        def round_wd(piece, lo, hi, copy):
+            pair, first_column, end_column = WD_LOADS[piece]
             copy(
                 pair_words[pair][:, lo:hi].bitcast(BF16).rearrange("p (c e) -> p c e", e=2),
-                wd_raw[pair, half][:, :, lo - half * HALF : hi - half * HALF].rearrange("p e c -> p c e"),
+                wd_raw[piece][:, :, lo - first_column : hi - first_column].rearrange("p e c -> p c e"),
             )
 
         def gather_wd(pair, b):
@@ -253,8 +270,39 @@ def tile_list_listed_hardswish_bottleneck_kernel(
         h_bf = {}
         h_codes = {}
         h_plane = {}
+        h_strip = {}
 
-        def project(unit):
+        def lift(unit, m0):
+            b, lo, hi = unit
+            nc.scalar.activation(
+                lifted[unit][:, :, m0 - lo : m0 - lo + BANK_M], a_banks[b, m0][:], ACT.Relu, bias=3.0
+            )
+
+        def lift_gained(unit, m0):
+            b, lo, hi = unit
+            for t in range(PACK):
+                nc.scalar.activation(
+                    lifted[unit][:, t, m0 - lo : m0 - lo + BANK_M],
+                    a_banks[b, m0][:, t, :],
+                    ACT.Identity,
+                    bias=gain_shift[:, t : t + 1],
+                    scale=gain[:, b, t : t + 1],
+                )
+
+        def gate_pool(unit):
+            b, lo, hi = unit
+            gated[unit] = held([P, PACK, hi - lo], F32, f"gated{b}_{lo}")
+            for t in range(PACK):
+                nc.gpsimd.tensor_scalar(
+                    gated[unit][:, t, :],
+                    lifted[unit][:, t, :],
+                    gain_upper[:, t : t + 1],
+                    gain_lower[:, t : t + 1],
+                    ALU.min,
+                    ALU.max,
+                )
+
+        def project(unit, lifter):
             b, lo, hi = unit
             lifted[unit] = held([P, PACK, hi - lo], F32, f"lifted{b}_{lo}")
             for m0 in range(lo, hi, BANK_M):
@@ -271,7 +319,7 @@ def tile_list_listed_hardswish_bottleneck_kernel(
                         start=True,
                         stop=True,
                     )
-                nc.scalar.activation(lifted[unit][:, :, m0 - lo : m0 - lo + BANK_M], bank[:], ACT.Relu, bias=3.0)
+                lifter(unit, m0)
 
         def gate(unit):
             b, lo, hi = unit
@@ -307,6 +355,8 @@ def tile_list_listed_hardswish_bottleneck_kernel(
             for m0 in range(lo, hi, BANK_M):
                 h_codes[b, m0] = codes[:, m0 - lo : m0 - lo + BANK_M]
                 h_plane[b, m0] = plane[:, m0 - lo : m0 - lo + BANK_M]
+            for m0 in range(lo, hi - STRIP + 1, STRIP):
+                h_strip[b, m0] = (codes[:, m0 - lo : m0 - lo + STRIP], plane[:, m0 - lo : m0 - lo + STRIP])
 
         y_f32 = [held([P, PACK, STRIP], F32, f"y_f32_{strip}") for strip in range(M // STRIP - 1)]
         y_last = {m0: held([P, PACK, BANK_M], F32, f"y_last{m0}") for m0 in range(M - STRIP, M, BANK_M)}
@@ -345,20 +395,38 @@ def tile_list_listed_hardswish_bottleneck_kernel(
             for m0 in range(lo, hi, BANK_M):
                 y_bf_bank[m0] = y_bf[lo][:, m0 - lo : m0 - lo + BANK_M, :]
 
-        y_banks = {}
-
-        def round_y_scalar(m0):
-            nc.scalar.copy(y_bf_bank[m0], y_banks[m0][:].rearrange("p s m -> p m s"))
-
-        def down_strip(lo, rounded):
+        def down_strip(lo, rounded_end):
             values = y_f32[lo // STRIP]
-            for m0 in range(lo, lo + STRIP, BANK_M):
-                y_banks[m0] = banked([P, PACK, BANK_M], f"y_bank{m0}", Y_BANK[m0])
-                down(m0, y_banks[m0])
-                nc.scalar.copy(values[:, :, m0 - lo : m0 - lo + BANK_M], y_banks[m0][:])
+            banks = [banked([P, 2, STRIP], f"y_bank{lo}_{pair}", Y_BANK[lo] + pair) for pair in range(2)]
+            for s in range(PACK):
+                nc.tensor.matmul_mx(
+                    out=banks[s // 2][:, s % 2, :],
+                    lhsT=w4_codes[:, s, :].bitcast(FP4X4),
+                    lhsT_scale=w4_plane[:, s, :],
+                    rhs=x_strip[lo].bitcast(FP8X4),
+                    rhs_scale=x_plane[:, lo : lo + STRIP],
+                    start=(s % 2 == 0),
+                    stop=False,
+                )
+            for b in range(PASSES):
+                for s in range(PACK):
+                    nc.tensor.matmul_mx(
+                        out=banks[s // 2][:, s % 2, :],
+                        lhsT=wd_codes[b][:, s, :].bitcast(FP8X4),
+                        lhsT_scale=wd_plane[b][:, s, :],
+                        rhs=h_strip[b, lo][0].bitcast(FP8X4),
+                        rhs_scale=h_strip[b, lo][1],
+                        start=False,
+                        stop=(b == PASSES - 1 and s % 2 == 1),
+                    )
+            for pair in range(2):
+                nc.scalar.copy(values[:, 2 * pair : 2 * pair + 2, :], banks[pair][:])
             nc.sync.dma_start(y_rows[:, :, lo : lo + STRIP], values[:])
-            for m0 in rounded:
-                round_y_scalar(m0)
+            if rounded_end > lo:
+                nc.scalar.copy(
+                    y_bf[lo][:, : rounded_end - lo, :].rearrange("p (c e) s -> p c s e", e=2),
+                    values[:, :, : rounded_end - lo].rearrange("p s (c e) -> p c s e", e=2),
+                )
 
         def down_last(m0, queue):
             bank = banked([P, PACK, BANK_M], f"y_bank{m0}", Y_BANK[m0])
@@ -366,9 +434,9 @@ def tile_list_listed_hardswish_bottleneck_kernel(
             nc.scalar.copy(y_last[m0][:], bank[:])
             queue.dma_start(y_rows[:, :, m0 : m0 + BANK_M], y_last[m0][:])
 
-        def round_y_vector(into, values):
+        def round_y_vector(m0, values):
             nc.vector.tensor_copy(
-                into.rearrange("p (c e) s -> p c s e", e=2), values.rearrange("p s (c e) -> p c s e", e=2)
+                y_bf_bank[m0].rearrange("p (c e) s -> p c s e", e=2), values.rearrange("p s (c e) -> p c s e", e=2)
             )
 
         def quantize_y(lo, hi):
@@ -383,96 +451,100 @@ def tile_list_listed_hardswish_bottleneck_kernel(
 
         first, second, third = (0, 0, 256), (0, 256, 512), (1, 0, 512)
         fourth, fifth, sixth, seventh = (0, 512, 768), (1, 512, 768), (0, 768, 1024), (1, 768, 1024)
-        x_bf = {}
 
-        def round_x(strip, rounder):
-            x_bf[strip] = held([P, STRIP * PACK], BF16, f"x_bf{strip}")
-            rounder(strip, x_bf[strip][:])
-
-        def quantize_strip(strip):
-            quantize_x(strip * STRIP, (strip + 1) * STRIP, x_bf[strip][:])
-
-        round_x(0, round_x_scalar)
+        x_bf0 = held([P, STRIP * PACK], BF16, "x_bf0")
+        round_x_scalar(0, x_bf0[:])
         turn_gain()
         gather_plane()
-        quantize_strip(0)
+        quantize_x(0, 256, x_bf0[:])
         gather_codes(0)
         gather_codes(1)
-        round_x(1, round_x_pool)
-        project(first)
-        quantize_strip(1)
-        project(second)
-        project(third)
+        x_bf1 = held([P, STRIP * PACK], BF16, "x_bf1")
+        round_x_pool(1, x_bf1[:])
+        bound_gain(fourth[0])
+        project(first, lift)
+        quantize_x(256, 512, x_bf1[:])
+        project(second, lift)
+        project(third, lift)
         w4_codes = deal_w4_codes()
         gate(first)
         gate(second)
-        round_x(2, round_x_pool)
         hold_h(0, 0, 512)
         swish(first, 0, 256, 0)
         swish(second, 256, 512, 0)
-        quantize_strip(2)
-        project(fourth)
-        project(fifth)
+
+        pair_words[0] = held([P, T], U32, "pair_words0")
+        round_wd("00", 0, POOL_COLUMNS, nc.gpsimd.tensor_copy)
+        round_wd("00", POOL_COLUMNS, HALF, nc.scalar.copy)
+        round_wd("01", HALF, T, nc.scalar.copy)
+        x_bf2 = held([P, STRIP * PACK], BF16, "x_bf2")
+        round_x_scalar(2, x_bf2[:])
         quantize_h(0, 0, 512)
         gate(third)
-        pair_words[0] = held([P, T], U32, "pair_words0")
-        round_wd(0, 0, POOL_FIRST, nc.gpsimd.tensor_copy)
-        round_wd(0, POOL_FIRST, HALF, nc.scalar.copy)
-        round_wd(0, HALF, T, nc.scalar.copy)
-        swish_tile(third, 0, 512)
-        gate(fourth)
-        quantize_h(1, 0, 512)
-        gate(fifth)
-
-        pair_words[1] = held([P, T], U32, "pair_words1")
-        round_wd(1, 0, HALF, nc.gpsimd.tensor_copy)
-        round_wd(1, HALF, HALF + POOL_LAST, nc.gpsimd.tensor_copy)
-        round_wd(1, HALF + POOL_LAST, T, nc.scalar.copy)
-        round_x(3, round_x_pool)
+        quantize_x(512, 768, x_bf2[:])
+        project(fourth, lift_gained)
         w4_plane = deal_w4_plane()
+        pair_words[1] = held([P, T], U32, "pair_words1")
+        round_wd("10", 0, POOL_COLUMNS, nc.gpsimd.tensor_copy)
+        round_wd("10", POOL_COLUMNS, HALF, nc.scalar.copy)
+        round_wd("11", HALF, T, nc.scalar.copy)
+        gate_pool(fourth)
+        x_bf3 = held([P, STRIP * PACK], BF16, "x_bf3")
+        round_x_pool(3, x_bf3[:])
         gather_wd(0, 0)
         gather_wd(0, 1)
         copy_turned(0, 0)
         copy_turned(0, 1)
-        swish_tile(fourth, 512, 768)
+        swish_tile(third, 0, 256)
         for b in range(PASSES):
             gather_wd(1, b)
             copy_turned(1, b)
-        quantize_strip(3)
-        project(sixth)
-        project(seventh)
-        swish_tile(fifth, 512, 768)
+        project(fifth, lift)
+        swish_tile(third, 256, 512)
+        quantize_h(1, 0, 256)
         quantize_wd(0)
-        quantize_h(0, 512, 768)
         quantize_wd(1)
-        quantize_h(1, 512, 768)
+        quantize_x(768, 1024, x_bf3[:])
 
-        down_strip(0, ())
+        down_strip(0, 0)
+        project(sixth, lift)
+        quantize_h(1, 256, 512)
+        gate(fifth)
+        swish_tile(fourth, 512, 768)
+        project(seventh, lift)
+        down_strip(256, 256)
+        swish_tile(fifth, 512, 768)
+        quantize_h(0, 512, 768)
         gate(sixth)
+        quantize_h(1, 512, 768)
         gate(seventh)
-        down_strip(256, ())
-        hold_y(0, 256)
-        pool_round(y_bf[0][:], y_f32[0][:].rearrange("p s m -> p m s"))
-        hold_y(256, 768)
-        down_strip(512, (384, 512))
+        hold_y(0, 512)
+        pool_round(y_bf[0][:, :STRIP, :], y_f32[0][:].rearrange("p s m -> p m s"))
+        nc.scalar.copy(
+            y_bf[0][:, STRIP:, :].rearrange("p (c e) s -> p c s e", e=2),
+            y_f32[1][:].rearrange("p s (c e) -> p c s e", e=2),
+        )
+        hold_y(512, 768)
+        down_strip(512, 640)
         swish_tile(sixth, 768, 1024)
         swish_tile(seventh, 768, 896)
-        swish_tile(seventh, 896, 1024)
         quantize_h(0, 768, 1024)
         quantize_h(1, 768, 896)
-        quantize_h(1, 896, 1024)
-        hold_y(768, 1024)
+        hold_y(768, 896)
+        hold_y(896, 1024)
         down_last(768, nc.sync)
+        swish_tile(seventh, 896, 1024)
+        round_y_vector(640, y_f32[2][:, :, BANK_M:])
+        quantize_h(1, 896, 1024)
         down_last(896, nc.scalar)
-        quantize_y(0, 256)
-        store_words(0, 256)
-        round_y_vector(y_bf_bank[256], y_f32[1][:, :, :BANK_M])
-        round_y_vector(y_bf_bank[640], y_f32[2][:, :, BANK_M:])
-        round_y_vector(y_bf_bank[768], y_last[768][:])
-        quantize_y(256, 768)
-        store_words(256, 768)
-        round_y_vector(y_bf_bank[896], y_last[896][:])
-        quantize_y(768, 1024)
+        quantize_y(0, 512)
+        store_words(0, 512)
+        round_y_vector(768, y_last[768][:])
+        quantize_y(512, 768)
+        store_words(512, 768)
+        round_y_vector(896, y_last[896][:])
+        quantize_y(768, 896)
+        quantize_y(896, 1024)
         store_words(768, 1024)
         for q in range(QUADRANTS):
             queue = nc.sync if q < QUADRANTS // 2 else nc.scalar

@@ -27,9 +27,12 @@ STRIP = 256
 HALF = T // 2
 GROUP = 16
 POOL_COLUMNS = 896
-WD_LOADS = {"00": (0, 0, HALF), "01": (0, HALF, T), "10": (1, 0, HALF), "11": (1, HALF, T)}
+POOL_LAST = 448
+MID_LAST = (HALF + T - POOL_LAST) // 2
+WD_LOADS = {"00": (0, 0, HALF), "01": (0, HALF, T), "10": (1, 0, HALF), "11": (1, HALF, MID_LAST),
+            "12": (1, MID_LAST, T - POOL_LAST), "13": (1, T - POOL_LAST, T)}
 BANK_BYTES = 2048
-A_BANK = {(0, 0): 0, (0, 128): 1, (0, 256): 2, (0, 384): 3, (1, 0): 4, (1, 128): 5, (1, 256): 6, (1, 384): 7,
+A_BANK = {(0, 0): 0, (0, 128): 1, (1, 0): 2, (1, 128): 3, (0, 256): 4, (0, 384): 5, (1, 256): 6, (1, 384): 7,
           (0, 512): 0, (0, 640): 1, (1, 512): 4, (1, 640): 5, (0, 768): 2, (0, 896): 3, (1, 768): 0, (1, 896): 1}
 TURN_BANK = {(0, 0): 2, (0, 1): 3, (1, 0): 2, (1, 1): 3}
 Y_BANK = {0: 6, 256: 6, 512: 4, 768: 2, 896: 3}
@@ -38,8 +41,7 @@ KIB = 1024
 ALIGN = 64
 WIDTH = {F32: 4, BF16: 2, U32: 4, U8: 1}
 
-REGIONS = (("early", 12 * KIB), ("first_x", 4 * KIB), ("third_x", 8 * KIB),
-           ("last_x", 7 * KIB), ("last_wd", 16 * KIB), ("last_pick", 4 * KIB))
+REGIONS = (("early", 12 * KIB), ("first_x", 4 * KIB), ("third_x", 8 * KIB), ("last_wd", 22 * KIB), ("last_pick", 4 * KIB), ("last_x", 7 * KIB))
 
 TENANTS = {
     "x_raw0": ("first_x", 0),
@@ -47,30 +49,30 @@ TENANTS = {
     "v_codes1": ("first_x", 2 * KIB),
     "x_bf1": ("x_bf0", 0),
     "w4_codes": ("x_bf0", 0),
-    "lifted0_256": ("early", 6 * KIB),
-    "h_bf0_0": ("early", 8 * KIB),
+    "lifted1_0": ("early", 6 * KIB),
+    "h_bf0": ("early", 8 * KIB),
     "pair_words0": ("early", 0),
     "x_raw2": ("third_x", 1 * KIB),
     "picked00": ("third_x", 0),
     "picked01": ("third_x", 2 * KIB),
-    "h_bf1_0": ("third_x", 4 * KIB),
+    "h_bf256": ("third_x", 4 * KIB),
     "w4_plane": ("x_bf2", 0),
-    "x_bf3": ("lifted1_0", 0),
+    "x_bf3": ("lifted1_256", 0),
     "x_raw3": ("last_x", 3 * KIB),
-    "h_codes1_0": ("last_x", 3 * KIB),
-    "h_codes1_256": ("last_x", 4 * KIB),
-    "wd_raw11": ("last_wd", 5 * KIB),
-    "lifted0_512": ("last_wd", 12 * KIB),
-    "picked11": ("last_pick", 0),
-    "lifted1_512": ("last_pick", 0),
-    "h_bf1_256": ("wd_raw10", 0),
-    "gated0_512": ("wd_raw10", 2 * KIB),
+    "gated0_512": ("last_x", 0),
+    "h_codes256": ("last_x", 4 * KIB),
+    "wd_raw11": ("last_wd", 6 * KIB),
+    "wd_raw12": ("last_wd", 15 * KIB),
     "wd_bf0": ("last_wd", 3 * KIB),
-    "wd_bf1": ("last_wd", 8 * KIB),
-    "x_codes768": ("last_wd", 3 * KIB),
-    "h_bf0_512": ("last_wd", 8 * KIB),
-    "h_bf1_512": ("last_wd", 10 * KIB),
-    "y_bf0": ("lifted1_768", 0),
+    "lifted0_512": ("last_wd", 7 * KIB),
+    "lifted1_512": ("last_wd", 12 * KIB),
+    "wd_bf1": ("last_wd", 16 * KIB),
+    "gated1_512": ("last_wd", 0),
+    "h_bf512": ("last_wd", 16 * KIB),
+    "picked11": ("last_pick", 0),
+    "lifted0_768": ("last_pick", 0),
+    "gated0_768": ("lifted1_512", 0),
+    "y_bf0": ("h_bf512", 0),
 }
 
 
@@ -153,6 +155,8 @@ def tile_list_listed_hardswish_bottleneck_kernel(
         load_plane(w4_plane_raw, w4_scales[0])
         load_wd("10")
         load_wd("11")
+        load_wd("12")
+        load_wd("13")
         load_x(3)
 
         ident = held([P, P], F32, "ident")
@@ -191,9 +195,9 @@ def tile_list_listed_hardswish_bottleneck_kernel(
         gain_lower = held([P, PACK], F32, "gain_lower")
 
         def bound_gain(b):
-            nc.gpsimd.tensor_scalar(gain_shift[:], gain[:, b, :], 3.0, 0.0, ALU.mult, ALU.add)
-            nc.gpsimd.tensor_scalar(gain_upper[:], gain[:, b, :], 6.0, 0.0, ALU.mult, ALU.max)
-            nc.gpsimd.tensor_scalar(gain_lower[:], gain[:, b, :], 6.0, 0.0, ALU.mult, ALU.min)
+            nc.vector.tensor_scalar(gain_shift[:], gain[:, b, :], 3.0, 0.0, ALU.mult, ALU.add)
+            nc.vector.tensor_scalar(gain_upper[:], gain[:, b, :], 6.0, 0.0, ALU.mult, ALU.max)
+            nc.vector.tensor_scalar(gain_lower[:], gain[:, b, :], 6.0, 0.0, ALU.mult, ALU.min)
 
         def pool_round(into, values):
             nc.gpsimd.tensor_scalar(into, values, 1.0, 0.0, ALU.mult, ALU.add)
@@ -268,9 +272,8 @@ def tile_list_listed_hardswish_bottleneck_kernel(
         lifted = {}
         gated = {}
         h_bf = {}
-        h_codes = {}
-        h_plane = {}
-        h_strip = {}
+        h_bank = {}
+        h_operand = {}
 
         def lift(unit, m0):
             b, lo, hi = unit
@@ -329,34 +332,36 @@ def tile_list_listed_hardswish_bottleneck_kernel(
                     gated[unit][:, t, :], lifted[unit][:, t, :], 6.0, gain[:, b, t : t + 1], ALU.min, ALU.mult
                 )
 
-        def hold_h(b, lo, hi):
-            h_bf[b, lo] = held([P, (hi - lo) * PACK], BF16, f"h_bf{b}_{lo}")
+        def hold_h(name, pieces):
+            tile = held([P, sum(hi - lo for b, lo, hi in pieces) * PACK], BF16, f"h_bf{name}")
+            h_bf[name] = (tile, pieces)
+            column = 0
+            for b, lo, hi in pieces:
+                for m0 in range(lo, hi, BANK_M):
+                    h_bank[b, m0] = tile[:, column * PACK : (column + BANK_M) * PACK]
+                    column = column + BANK_M
 
-        def swish(unit, first, end, tile_lo):
+        def swish(unit, first, end):
             b, lo, hi = unit
             for m0 in range(first, end, BANK_M):
                 c0 = m0 - lo
-                h0 = (m0 - tile_lo) * PACK
                 nc.vector.tensor_tensor(
-                    h_bf[b, tile_lo][:, h0 : h0 + BANK_M * PACK].rearrange("p (c e t) -> p c t e", e=2, t=PACK),
+                    h_bank[b, m0].rearrange("p (c e t) -> p c t e", e=2, t=PACK),
                     a_banks[b, m0][:].rearrange("p t (c e) -> p c t e", e=2),
                     gated[unit][:, :, c0 : c0 + BANK_M].rearrange("p t (c e) -> p c t e", e=2),
                     ALU.mult,
                 )
 
-        def swish_tile(unit, first, end):
-            hold_h(unit[0], first, end)
-            swish(unit, first, end, first)
-
-        def quantize_h(b, lo, hi):
-            codes = held([P, hi - lo], U32, f"h_codes{b}_{lo}")
-            plane = held([P, hi - lo], U8, f"h_plane{b}_{lo}")
-            nc.vector.quantize_mx(out=codes[:].bitcast(FP8X4), scales=plane[:], in_=h_bf[b, lo][:])
-            for m0 in range(lo, hi, BANK_M):
-                h_codes[b, m0] = codes[:, m0 - lo : m0 - lo + BANK_M]
-                h_plane[b, m0] = plane[:, m0 - lo : m0 - lo + BANK_M]
-            for m0 in range(lo, hi - STRIP + 1, STRIP):
-                h_strip[b, m0] = (codes[:, m0 - lo : m0 - lo + STRIP], plane[:, m0 - lo : m0 - lo + STRIP])
+        def quantize_h(name):
+            tile, pieces = h_bf[name]
+            width = sum(hi - lo for b, lo, hi in pieces)
+            codes = held([P, width], U32, f"h_codes{name}")
+            plane = held([P, width], U8, f"h_plane{name}")
+            nc.vector.quantize_mx(out=codes[:].bitcast(FP8X4), scales=plane[:], in_=tile[:])
+            column = 0
+            for b, lo, hi in pieces:
+                h_operand[b, lo] = (codes[:, column : column + hi - lo], plane[:, column : column + hi - lo])
+                column = column + hi - lo
 
         y_f32 = [held([P, PACK, STRIP], F32, f"y_f32_{strip}") for strip in range(M // STRIP - 1)]
         y_last = {m0: held([P, PACK, BANK_M], F32, f"y_last{m0}") for m0 in range(M - STRIP, M, BANK_M)}
@@ -384,8 +389,8 @@ def tile_list_listed_hardswish_bottleneck_kernel(
                         out=bank[:, s, :],
                         lhsT=wd_codes[b][:, s, :].bitcast(FP8X4),
                         lhsT_scale=wd_plane[b][:, s, :],
-                        rhs=h_codes[b, m0].bitcast(FP8X4),
-                        rhs_scale=h_plane[b, m0],
+                        rhs=h_operand[b, m0][0].bitcast(FP8X4),
+                        rhs_scale=h_operand[b, m0][1],
                         start=False,
                         stop=(b == PASSES - 1 and s == PACK - 1),
                     )
@@ -395,7 +400,7 @@ def tile_list_listed_hardswish_bottleneck_kernel(
             for m0 in range(lo, hi, BANK_M):
                 y_bf_bank[m0] = y_bf[lo][:, m0 - lo : m0 - lo + BANK_M, :]
 
-        def down_strip(lo, rounded_end):
+        def down_strip(lo):
             values = y_f32[lo // STRIP]
             banks = [banked([P, 2, STRIP], f"y_bank{lo}_{pair}", Y_BANK[lo] + pair) for pair in range(2)]
             for s in range(PACK):
@@ -414,19 +419,19 @@ def tile_list_listed_hardswish_bottleneck_kernel(
                         out=banks[s // 2][:, s % 2, :],
                         lhsT=wd_codes[b][:, s, :].bitcast(FP8X4),
                         lhsT_scale=wd_plane[b][:, s, :],
-                        rhs=h_strip[b, lo][0].bitcast(FP8X4),
-                        rhs_scale=h_strip[b, lo][1],
+                        rhs=h_operand[b, lo][0].bitcast(FP8X4),
+                        rhs_scale=h_operand[b, lo][1],
                         start=False,
                         stop=(b == PASSES - 1 and s % 2 == 1),
                     )
             for pair in range(2):
                 nc.scalar.copy(values[:, 2 * pair : 2 * pair + 2, :], banks[pair][:])
             nc.sync.dma_start(y_rows[:, :, lo : lo + STRIP], values[:])
-            if rounded_end > lo:
-                nc.scalar.copy(
-                    y_bf[lo][:, : rounded_end - lo, :].rearrange("p (c e) s -> p c s e", e=2),
-                    values[:, :, : rounded_end - lo].rearrange("p s (c e) -> p c s e", e=2),
-                )
+
+        def round_y_scalar(into, values):
+            nc.scalar.copy(
+                into.rearrange("p (c e) s -> p c s e", e=2), values.rearrange("p s (c e) -> p c s e", e=2)
+            )
 
         def down_last(m0, queue):
             bank = banked([P, PACK, BANK_M], f"y_bank{m0}", Y_BANK[m0])
@@ -449,8 +454,8 @@ def tile_list_listed_hardswish_bottleneck_kernel(
         def store_words(lo, hi):
             nc.sync.dma_start(y_words[:, lo * PACK : hi * PACK].bitcast(I32), y_codes[:, lo:hi].bitcast(I32))
 
-        first, second, third = (0, 0, 256), (0, 256, 512), (1, 0, 512)
-        fourth, fifth, sixth, seventh = (0, 512, 768), (1, 512, 768), (0, 768, 1024), (1, 768, 1024)
+        first, second, third, fourth = (0, 0, 256), (1, 0, 256), (0, 256, 512), (1, 256, 512)
+        fifth, sixth, seventh, eighth = (0, 512, 768), (1, 512, 768), (0, 768, 1024), (1, 768, 1024)
 
         x_bf0 = held([P, STRIP * PACK], BF16, "x_bf0")
         round_x_scalar(0, x_bf0[:])
@@ -461,17 +466,18 @@ def tile_list_listed_hardswish_bottleneck_kernel(
         gather_codes(1)
         x_bf1 = held([P, STRIP * PACK], BF16, "x_bf1")
         round_x_pool(1, x_bf1[:])
-        bound_gain(fourth[0])
         project(first, lift)
-        quantize_x(256, 512, x_bf1[:])
         project(second, lift)
+        quantize_x(256, 512, x_bf1[:])
         project(third, lift)
+        project(fourth, lift)
         w4_codes = deal_w4_codes()
+        bound_gain(seventh[0])
         gate(first)
         gate(second)
-        hold_h(0, 0, 512)
-        swish(first, 0, 256, 0)
-        swish(second, 256, 512, 0)
+        hold_h("0", (first, second))
+        swish(first, 0, 256)
+        swish(second, 0, 256)
 
         pair_words[0] = held([P, T], U32, "pair_words0")
         round_wd("00", 0, POOL_COLUMNS, nc.gpsimd.tensor_copy)
@@ -479,73 +485,77 @@ def tile_list_listed_hardswish_bottleneck_kernel(
         round_wd("01", HALF, T, nc.scalar.copy)
         x_bf2 = held([P, STRIP * PACK], BF16, "x_bf2")
         round_x_scalar(2, x_bf2[:])
-        quantize_h(0, 0, 512)
         gate(third)
+        gate(fourth)
+        quantize_h("0")
         quantize_x(512, 768, x_bf2[:])
-        project(fourth, lift_gained)
+        project(fifth, lift)
         w4_plane = deal_w4_plane()
         pair_words[1] = held([P, T], U32, "pair_words1")
-        round_wd("10", 0, POOL_COLUMNS, nc.gpsimd.tensor_copy)
-        round_wd("10", POOL_COLUMNS, HALF, nc.scalar.copy)
-        round_wd("11", HALF, T, nc.scalar.copy)
-        gate_pool(fourth)
+        round_wd("10", 0, HALF, nc.gpsimd.tensor_copy)
+        round_wd("11", HALF, MID_LAST, nc.scalar.copy)
+        round_wd("12", MID_LAST, T - POOL_LAST, nc.scalar.copy)
+        round_wd("13", T - POOL_LAST, T, nc.gpsimd.tensor_copy)
         x_bf3 = held([P, STRIP * PACK], BF16, "x_bf3")
         round_x_pool(3, x_bf3[:])
         gather_wd(0, 0)
         gather_wd(0, 1)
         copy_turned(0, 0)
         copy_turned(0, 1)
-        swish_tile(third, 0, 256)
+        hold_h("256", (third, fourth))
+        swish(third, 256, 512)
+        swish(fourth, 256, 512)
+        project(sixth, lift)
         for b in range(PASSES):
             gather_wd(1, b)
             copy_turned(1, b)
-        project(fifth, lift)
-        swish_tile(third, 256, 512)
-        quantize_h(1, 0, 256)
-        quantize_wd(0)
-        quantize_wd(1)
         quantize_x(768, 1024, x_bf3[:])
-
-        down_strip(0, 0)
-        project(sixth, lift)
-        quantize_h(1, 256, 512)
+        project(seventh, lift_gained)
         gate(fifth)
-        swish_tile(fourth, 512, 768)
-        project(seventh, lift)
-        down_strip(256, 256)
-        swish_tile(fifth, 512, 768)
-        quantize_h(0, 512, 768)
+        quantize_wd(0)
+        quantize_h("256")
+        quantize_wd(1)
+
+        down_strip(0)
         gate(sixth)
-        quantize_h(1, 512, 768)
-        gate(seventh)
-        hold_y(0, 512)
-        pool_round(y_bf[0][:, :STRIP, :], y_f32[0][:].rearrange("p s m -> p m s"))
-        nc.scalar.copy(
-            y_bf[0][:, STRIP:, :].rearrange("p (c e) s -> p c s e", e=2),
-            y_f32[1][:].rearrange("p s (c e) -> p c s e", e=2),
-        )
+        gate_pool(seventh)
+        hold_h("512", (fifth, sixth))
+        swish(fifth, 512, 768)
+        project(eighth, lift)
+        down_strip(256)
+        swish(sixth, 512, 768)
+        gate(eighth)
+        quantize_h("512")
+        hold_y(0, 256)
+        pool_round(y_bf[0][:], y_f32[0][:].rearrange("p s m -> p m s"))
         hold_y(512, 768)
-        down_strip(512, 640)
-        swish_tile(sixth, 768, 1024)
-        swish_tile(seventh, 768, 896)
-        quantize_h(0, 768, 1024)
-        quantize_h(1, 768, 896)
+        down_strip(512)
+        hold_y(256, 512)
+        round_y_scalar(y_bf[256][:], y_f32[1][:])
+        hold_h("768", ((0, 768, 896), (0, 896, 1024)))
+        swish(seventh, 768, 1024)
+        hold_h("768b", ((1, 768, 896),))
+        swish(eighth, 768, 896)
+        quantize_h("768")
+        quantize_h("768b")
         hold_y(768, 896)
         hold_y(896, 1024)
         down_last(768, nc.sync)
-        swish_tile(seventh, 896, 1024)
-        round_y_vector(640, y_f32[2][:, :, BANK_M:])
-        quantize_h(1, 896, 1024)
+        round_y_scalar(y_bf_bank[512], y_f32[2][:, :, :BANK_M])
+        hold_h("896", ((1, 896, 1024),))
+        swish(eighth, 896, 1024)
+        quantize_y(0, 256)
+        quantize_h("896")
         down_last(896, nc.scalar)
-        quantize_y(0, 512)
+        quantize_y(256, 512)
         store_words(0, 512)
+        round_y_vector(640, y_f32[2][:, :, BANK_M:])
         round_y_vector(768, y_last[768][:])
         quantize_y(512, 768)
-        store_words(512, 768)
         round_y_vector(896, y_last[896][:])
         quantize_y(768, 896)
         quantize_y(896, 1024)
-        store_words(768, 1024)
+        store_words(512, 1024)
         for q in range(QUADRANTS):
             queue = nc.sync if q < QUADRANTS // 2 else nc.scalar
             queue.dma_start(

@@ -27,10 +27,11 @@ STRIP = 256
 HALF = T // 2
 GROUP = 16
 POOL_COLUMNS = 896
-POOL_LAST = 448
-MID_LAST = (HALF + T - POOL_LAST) // 2
-WD_LOADS = {"00": (0, 0, HALF), "01": (0, HALF, T), "10": (1, 0, HALF), "11": (1, HALF, MID_LAST),
-            "12": (1, MID_LAST, T - POOL_LAST), "13": (1, T - POOL_LAST, T)}
+POOL_EARLY = 576
+POOL_LAST = 768
+WD_LOADS = {"00": (0, 0, HALF), "01": (0, HALF, T), "10": (1, 0, POOL_EARLY), "11": (1, POOL_EARLY, T - POOL_LAST),
+            "12": (1, T - POOL_LAST, T)}
+POOL_PIXELS = 192
 BANK_BYTES = 2048
 A_BANK = {(0, 0): 0, (0, 128): 1, (1, 0): 2, (1, 128): 3, (0, 256): 4, (0, 384): 5, (1, 256): 6, (1, 384): 7,
           (0, 512): 0, (0, 640): 1, (1, 512): 4, (1, 640): 5, (0, 768): 2, (0, 896): 3, (1, 768): 0, (1, 896): 1}
@@ -41,38 +42,45 @@ KIB = 1024
 ALIGN = 64
 WIDTH = {F32: 4, BF16: 2, U32: 4, U8: 1}
 
-REGIONS = (("early", 12 * KIB), ("first_x", 4 * KIB), ("third_x", 8 * KIB), ("last_wd", 22 * KIB), ("last_pick", 4 * KIB), ("last_x", 7 * KIB))
+REGIONS = (("early", 17 * KIB), ("first_x", 4 * KIB), ("second_x", 8 * KIB), ("first_pick", 5 * KIB), ("third_x", 7 * KIB), ("last_wd", 16 * KIB), ("last_pick", 4 * KIB), ("last_x", 7 * KIB), ("third_h", 3 * KIB))
 
 TENANTS = {
     "x_raw0": ("first_x", 0),
     "v_codes0": ("first_x", 0),
     "v_codes1": ("first_x", 2 * KIB),
     "x_bf1": ("x_bf0", 0),
+    "x_second0": ("second_x", 2 * KIB),
+    "x_second1": ("second_x", 4 * KIB),
+    "lifted0_0": ("second_x", 0),
+    "gated0_0": ("second_x", 4 * KIB),
     "w4_codes": ("x_bf0", 0),
     "lifted1_0": ("early", 6 * KIB),
     "h_bf0": ("early", 8 * KIB),
     "pair_words0": ("early", 0),
-    "x_raw2": ("third_x", 1 * KIB),
-    "picked00": ("third_x", 0),
-    "picked01": ("third_x", 2 * KIB),
-    "h_bf256": ("third_x", 4 * KIB),
-    "w4_plane": ("x_bf2", 0),
+    "picked00": ("first_pick", 0),
+    "x_codes512": ("first_pick", 0),
+    "h_bf256": ("first_pick", 1 * KIB),
+    "w4_plane0": ("early", 8 * KIB),
+    "pair_words1": ("early", 8 * KIB + N),
+    "x_bf2": ("third_x", 0),
+    "wd_raw10": ("third_x", 2 * KIB),
+    "w4_plane3": ("third_x", 2 * KIB - ALIGN),
     "x_bf3": ("lifted1_256", 0),
     "x_raw3": ("last_x", 3 * KIB),
     "gated0_512": ("last_x", 0),
     "h_codes256": ("last_x", 4 * KIB),
-    "wd_raw11": ("last_wd", 6 * KIB),
-    "wd_raw12": ("last_wd", 15 * KIB),
-    "wd_bf0": ("last_wd", 3 * KIB),
-    "lifted0_512": ("last_wd", 7 * KIB),
-    "lifted1_512": ("last_wd", 12 * KIB),
-    "wd_bf1": ("last_wd", 16 * KIB),
-    "gated1_512": ("last_wd", 0),
-    "h_bf512": ("last_wd", 16 * KIB),
+    "wd_raw11": ("last_wd", 7 * KIB + N),
+    "lifted512": ("last_wd", 0),
+    "wd_bf0": ("last_wd", 8 * KIB),
+    "wd_bf1": ("last_wd", 12 * KIB),
+    "gated1_512": ("wd_bf0", 0),
+    "h_bf512": ("wd_bf1", 0),
     "picked11": ("last_pick", 0),
     "lifted0_768": ("last_pick", 0),
-    "gated0_768": ("lifted1_512", 0),
+    "gated0_768": ("lifted512", 0),
     "y_bf0": ("h_bf512", 0),
+    "h_codes512": ("third_h", 0),
+    "y_bf384": ("third_h", 0),
 }
 
 
@@ -135,19 +143,21 @@ def tile_list_listed_hardswish_bottleneck_kernel(
             wd_raw[piece] = held([P, 2, hi - lo], F32, f"wd_raw{piece}")
             nc.sync.dma_start(wd_raw[piece][:], wd_rows[:, 2 * pair : 2 * pair + 2, lo:hi])
 
-        g_rows = held([P, PASSES * P], F32, "g_rows")
+        g_raw = held([PASSES, PACK * P], F32, "g_raw")
+        g_rows = held([P, PACK, P], F32, "g_rows")
         nc.gpsimd.memset(g_rows[:], 0.0)
         w4_plane_raw = held([P, N], U8, "w4_plane_raw")
         nc.gpsimd.memset(w4_plane_raw[:].bitcast(I32), 0)
 
         load_x(0)
         load_plane(tab_plane, tab_scales[0])
+        nc.sync.dma_start(g_raw[:], g.rearrange("(b j) -> b j", b=PASSES))
         tab_codes = held([P, T], U32, "tab_codes")
         nc.sync.dma_start(tab_codes[:].bitcast(I32), tab_words[0].rearrange("p c i -> p (c i)").bitcast(I32))
-        load_x(1)
-        nc.sync.dma_start(
-            g_rows[:PACK, :].rearrange("t (q r) -> t q r", r=RUN), g.rearrange("(q t r) -> t q r", t=PACK, r=RUN)
-        )
+        x_second = [held([P, PACK, BANK_M], F32, f"x_second{half}") for half in range(2)]
+        for half in range(2):
+            lo = STRIP + half * BANK_M
+            nc.sync.dma_start(x_second[half][:], x_rows[:, :, lo : lo + BANK_M])
         nc.sync.dma_start(w4_raw[:].bitcast(I32), w4_words[0].bitcast(I32))
         load_wd("00")
         load_wd("01")
@@ -156,7 +166,6 @@ def tile_list_listed_hardswish_bottleneck_kernel(
         load_wd("10")
         load_wd("11")
         load_wd("12")
-        load_wd("13")
         load_x(3)
 
         ident = held([P, P], F32, "ident")
@@ -185,10 +194,14 @@ def tile_list_listed_hardswish_bottleneck_kernel(
         gain = held([P, PASSES, PACK], F32, "gain")
 
         def turn_gain():
-            g_bank = banked([P, PASSES, P], "g_bank", GAIN_BANK)
-            for b in range(PASSES):
-                nc.tensor.transpose(g_bank[:, b, :], g_rows[:, b * P : (b + 1) * P], ident[:])
-            nc.scalar.copy(gain[:], g_bank[:, :, :PACK])
+            nc.scalar.copy(
+                g_rows[:PASSES].rearrange("b t (q r) -> b t q r", r=RUN),
+                g_raw[:].rearrange("b (q t r) -> b t q r", t=PACK, r=RUN),
+            )
+            g_bank = banked([P, PACK, P], "g_bank", GAIN_BANK)
+            for t in range(PACK):
+                nc.tensor.transpose(g_bank[:, t, :], g_rows[:, t, :], ident[:])
+            nc.scalar.copy(gain[:], g_bank[:, :, :PASSES].rearrange("p t b -> p b t"))
 
         gain_shift = held([P, PACK], F32, "gain_shift")
         gain_upper = held([P, PACK], F32, "gain_upper")
@@ -263,10 +276,13 @@ def tile_list_listed_hardswish_bottleneck_kernel(
             nc.vector.tensor_copy(codes[:].bitcast(U16), w4_raw[:].bitcast(U16).rearrange("p (c s) -> p s c", s=PACK))
             return codes
 
-        def deal_w4_plane():
-            plane = held([P, PACK, P], U8, "w4_plane")
-            nc.gpsimd.tensor_copy(plane[:], w4_plane_raw[:].rearrange("p (c s) -> p s c", s=PACK))
-            return plane
+        w4_plane = {}
+
+        def deal_w4_plane(first, end):
+            plane = held([P, end - first, P], U8, f"w4_plane{first}")
+            nc.gpsimd.tensor_copy(plane[:], w4_plane_raw[:].rearrange("p (c s) -> p s c", s=PACK)[:, first:end, :])
+            for s in range(first, end):
+                w4_plane[s] = plane[:, s - first, :]
 
         a_banks = {}
         lifted = {}
@@ -307,7 +323,8 @@ def tile_list_listed_hardswish_bottleneck_kernel(
 
         def project(unit, lifter):
             b, lo, hi = unit
-            lifted[unit] = held([P, PACK, hi - lo], F32, f"lifted{b}_{lo}")
+            if unit not in lifted:
+                lifted[unit] = held([P, PACK, hi - lo], F32, f"lifted{b}_{lo}")
             for m0 in range(lo, hi, BANK_M):
                 bank = banked([P, PACK, BANK_M], f"a_bank{b}_{m0}", A_BANK[b, m0])
                 a_banks[b, m0] = bank
@@ -377,7 +394,7 @@ def tile_list_listed_hardswish_bottleneck_kernel(
                 nc.tensor.matmul_mx(
                     out=bank[:, s, :],
                     lhsT=w4_codes[:, s, :].bitcast(FP4X4),
-                    lhsT_scale=w4_plane[:, s, :],
+                    lhsT_scale=w4_plane[s],
                     rhs=x_codes[m0].bitcast(FP8X4),
                     rhs_scale=x_plane[:, m0 : m0 + BANK_M],
                     start=(s == 0),
@@ -407,7 +424,7 @@ def tile_list_listed_hardswish_bottleneck_kernel(
                 nc.tensor.matmul_mx(
                     out=banks[s // 2][:, s % 2, :],
                     lhsT=w4_codes[:, s, :].bitcast(FP4X4),
-                    lhsT_scale=w4_plane[:, s, :],
+                    lhsT_scale=w4_plane[s],
                     rhs=x_strip[lo].bitcast(FP8X4),
                     rhs_scale=x_plane[:, lo : lo + STRIP],
                     start=(s % 2 == 0),
@@ -439,9 +456,9 @@ def tile_list_listed_hardswish_bottleneck_kernel(
             nc.scalar.copy(y_last[m0][:], bank[:])
             queue.dma_start(y_rows[:, :, m0 : m0 + BANK_M], y_last[m0][:])
 
-        def round_y_vector(m0, values):
+        def round_y_vector(into, values):
             nc.vector.tensor_copy(
-                y_bf_bank[m0].rearrange("p (c e) s -> p c s e", e=2), values.rearrange("p s (c e) -> p c s e", e=2)
+                into.rearrange("p (c e) s -> p c s e", e=2), values.rearrange("p s (c e) -> p c s e", e=2)
             )
 
         def quantize_y(lo, hi):
@@ -465,7 +482,13 @@ def tile_list_listed_hardswish_bottleneck_kernel(
         gather_codes(0)
         gather_codes(1)
         x_bf1 = held([P, STRIP * PACK], BF16, "x_bf1")
-        round_x_pool(1, x_bf1[:])
+        nc.scalar.copy(
+            x_bf1[:, : BANK_M * PACK].rearrange("p (c e i) -> p c i e", e=2, i=PACK),
+            x_second[0][:].rearrange("p i (c e) -> p c i e", e=2),
+        )
+        pool_round(
+            x_bf1[:, BANK_M * PACK :].rearrange("p (c i) -> p c i", i=PACK), x_second[1][:].rearrange("p i c -> p c i")
+        )
         project(first, lift)
         project(second, lift)
         quantize_x(256, 512, x_bf1[:])
@@ -488,20 +511,23 @@ def tile_list_listed_hardswish_bottleneck_kernel(
         gate(third)
         gate(fourth)
         quantize_h("0")
-        quantize_x(512, 768, x_bf2[:])
-        project(fifth, lift)
-        w4_plane = deal_w4_plane()
-        pair_words[1] = held([P, T], U32, "pair_words1")
-        round_wd("10", 0, HALF, nc.gpsimd.tensor_copy)
-        round_wd("11", HALF, MID_LAST, nc.scalar.copy)
-        round_wd("12", MID_LAST, T - POOL_LAST, nc.scalar.copy)
-        round_wd("13", T - POOL_LAST, T, nc.gpsimd.tensor_copy)
-        x_bf3 = held([P, STRIP * PACK], BF16, "x_bf3")
-        round_x_pool(3, x_bf3[:])
         gather_wd(0, 0)
         gather_wd(0, 1)
+        quantize_x(512, 768, x_bf2[:])
+        deal_w4_plane(0, PACK - 1)
+        pair_words[1] = held([P, T], U32, "pair_words1")
+        round_wd("10", 0, POOL_EARLY, nc.gpsimd.tensor_copy)
+        deal_w4_plane(PACK - 1, PACK)
+        round_wd("11", POOL_EARLY, T - POOL_LAST, nc.scalar.copy)
+        round_wd("12", T - POOL_LAST, T, nc.gpsimd.tensor_copy)
+        x_bf3 = held([P, STRIP * PACK], BF16, "x_bf3")
+        round_x_pool(3, x_bf3[:])
         copy_turned(0, 0)
         copy_turned(0, 1)
+        lifted_third = held([P, PASSES, PACK, STRIP], F32, "lifted512")
+        lifted[fifth] = lifted_third[:, 0]
+        lifted[sixth] = lifted_third[:, 1]
+        project(fifth, lift)
         hold_h("256", (third, fourth))
         swish(third, 256, 512)
         swish(fourth, 256, 512)
@@ -527,11 +553,13 @@ def tile_list_listed_hardswish_bottleneck_kernel(
         gate(eighth)
         quantize_h("512")
         hold_y(0, 256)
-        pool_round(y_bf[0][:], y_f32[0][:].rearrange("p s m -> p m s"))
-        hold_y(512, 768)
+        pool_round(y_bf[0][:, :POOL_PIXELS, :], y_f32[0][:, :, :POOL_PIXELS].rearrange("p s m -> p m s"))
+        round_y_scalar(y_bf[0][:, POOL_PIXELS:, :], y_f32[0][:, :, POOL_PIXELS:])
+        hold_y(256, 384)
+        round_y_scalar(y_bf[256][:], y_f32[1][:, :, :BANK_M])
         down_strip(512)
-        hold_y(256, 512)
-        round_y_scalar(y_bf[256][:], y_f32[1][:])
+        hold_y(384, 768)
+        round_y_scalar(y_bf_bank[384], y_f32[1][:, :, BANK_M:])
         hold_h("768", ((0, 768, 896), (0, 896, 1024)))
         swish(seventh, 768, 1024)
         hold_h("768b", ((1, 768, 896),))
@@ -541,21 +569,21 @@ def tile_list_listed_hardswish_bottleneck_kernel(
         hold_y(768, 896)
         hold_y(896, 1024)
         down_last(768, nc.sync)
-        round_y_scalar(y_bf_bank[512], y_f32[2][:, :, :BANK_M])
         hold_h("896", ((1, 896, 1024),))
         swish(eighth, 896, 1024)
         quantize_y(0, 256)
         quantize_h("896")
         down_last(896, nc.scalar)
-        quantize_y(256, 512)
-        store_words(0, 512)
-        round_y_vector(640, y_f32[2][:, :, BANK_M:])
-        round_y_vector(768, y_last[768][:])
-        quantize_y(512, 768)
-        round_y_vector(896, y_last[896][:])
+        round_y_vector(y_bf[384][:, BANK_M:, :], y_f32[2][:])
+        quantize_y(256, 384)
+        store_words(0, 384)
+        round_y_vector(y_bf_bank[768], y_last[768][:])
+        quantize_y(384, 768)
+        store_words(384, 768)
+        round_y_vector(y_bf_bank[896], y_last[896][:])
         quantize_y(768, 896)
         quantize_y(896, 1024)
-        store_words(512, 1024)
+        store_words(768, 1024)
         for q in range(QUADRANTS):
             queue = nc.sync if q < QUADRANTS // 2 else nc.scalar
             queue.dma_start(

from contextlib import ExitStack

import concourse.mybir as mybir
from concourse.masks import make_identity

K, T, S, M, N = 512, 2048, 1024, 1024, 512
FLOPS = 2 * M * (K * S + S * N + K * N)

F32 = mybir.dt.float32
BF16 = mybir.dt.bfloat16
I32 = mybir.dt.int32
U32 = mybir.dt.uint32
U16 = mybir.dt.uint16
U8 = mybir.dt.uint8
FP8X4 = mybir.dt.float8_e4m3fn_x4
FP4X4 = mybir.dt.float4_e2m1fn_x4
ALU = mybir.AluOpType
ACT = mybir.ActivationFunctionType

P = 128
PACK = 4
RUN = 8
PASSES = S // (P * PACK)
QUADRANTS = 4
BANK_M = 128
STRIP = 256
HALF = T // 2
GROUP = 16
POOL_COLUMNS = 896
POOL_EARLY = 576
POOL_LAST = 768
WD_LOADS = {"00": (0, 0, HALF), "01": (0, HALF, T), "10": (1, 0, POOL_EARLY), "11": (1, POOL_EARLY, T - POOL_LAST),
            "12": (1, T - POOL_LAST, T)}
POOL_PIXELS = 192
BANK_BYTES = 2048
A_BANK = {(0, 0): 0, (0, 128): 1, (1, 0): 2, (1, 128): 3, (0, 256): 4, (0, 384): 5, (1, 256): 6, (1, 384): 7,
          (0, 512): 0, (0, 640): 1, (1, 512): 4, (1, 640): 5, (0, 768): 2, (0, 896): 3, (1, 768): 0, (1, 896): 1}
TURN_BANK = {(0, 0): 2, (0, 1): 3, (1, 0): 2, (1, 1): 3}
Y_BANK = {0: 6, 256: 6, 512: 4, 768: 2, 896: 3}
GAIN_BANK = 7
KIB = 1024
ALIGN = 64
WIDTH = {F32: 4, BF16: 2, U32: 4, U8: 1}

REGIONS = (("early", 17 * KIB), ("first_x", 4 * KIB), ("second_x", 8 * KIB), ("first_pick", 5 * KIB), ("third_x", 7 * KIB), ("last_wd", 16 * KIB), ("last_pick", 4 * KIB), ("last_x", 7 * KIB), ("third_h", 3 * KIB))

TENANTS = {
    "x_raw0": ("first_x", 0),
    "v_codes0": ("first_x", 0),
    "v_codes1": ("first_x", 2 * KIB),
    "x_bf1": ("x_bf0", 0),
    "x_second0": ("second_x", 2 * KIB),
    "x_second1": ("second_x", 4 * KIB),
    "lifted0_0": ("second_x", 0),
    "gated0_0": ("second_x", 4 * KIB),
    "w4_codes": ("x_bf0", 0),
    "lifted1_0": ("early", 6 * KIB),
    "h_bf0": ("early", 8 * KIB),
    "pair_words0": ("early", 0),
    "picked00": ("first_pick", 0),
    "x_codes512": ("first_pick", 0),
    "h_bf256": ("first_pick", 1 * KIB),
    "w4_plane0": ("early", 8 * KIB),
    "pair_words1": ("early", 8 * KIB + N),
    "x_bf2": ("third_x", 0),
    "wd_raw10": ("third_x", 2 * KIB),
    "w4_plane3": ("third_x", 2 * KIB - ALIGN),
    "x_bf3": ("lifted1_256", 0),
    "x_raw3": ("last_x", 3 * KIB),
    "gated0_512": ("last_x", 0),
    "h_codes256": ("last_x", 4 * KIB),
    "wd_raw11": ("last_wd", 7 * KIB + N),
    "lifted512": ("last_wd", 0),
    "wd_bf0": ("last_wd", 8 * KIB),
    "wd_bf1": ("last_wd", 12 * KIB),
    "gated1_512": ("wd_bf0", 0),
    "h_bf512": ("wd_bf1", 0),
    "picked11": ("last_pick", 0),
    "lifted0_768": ("last_pick", 0),
    "gated0_768": ("lifted512", 0),
    "y_bf0": ("h_bf512", 0),
    "h_codes512": ("third_h", 0),
    "y_bf384": ("third_h", 0),
}


def tile_list_listed_hardswish_bottleneck_kernel(
    tc, tab_words, tab_scales, offs, x, w4_words, w4_scales, wdT, g, out_0, out_1, out_2
):
    nc = tc.nc
    with ExitStack() as ctx:
        lists = ctx.enter_context(tc.tile_pool(name="lists", bufs=1))
        keep = ctx.enter_context(tc.tile_pool(name="keep", bufs=1))
        psum = ctx.enter_context(tc.psum_pool(name="psum", bufs=1))

        def banked(shape, name, bank):
            return psum.tile(shape, F32, name=name, offset=bank * BANK_BYTES)

        places = {"top": 0}

        def reserve(name, size):
            places[name] = places["top"]
            places["top"] = places["top"] + (size + ALIGN - 1) // ALIGN * ALIGN

        for region, region_size in REGIONS:
            reserve(region, region_size)

        def held(shape, dtype, name):
            if name in TENANTS:
                host, skip = TENANTS[name]
                places[name] = places[host] + skip
            else:
                size = WIDTH[dtype]
                for extent in shape[1:]:
                    size = size * extent
                reserve(name, size)
            return keep.tile(shape, dtype, name=name, align_bytes=ALIGN, offset=places[name])

        def load_plane(plane, scale_rows):
            for q in range(QUADRANTS):
                nc.sync.dma_start(
                    plane[32 * q : 32 * q + 4, :].bitcast(I32), scale_rows[4 * q : 4 * q + 4, :].bitcast(I32)
                )

        offsets = lists.tile([P, S // GROUP], U16, name="offsets")
        nc.sync.dma_start(offsets[:], offs)
        w4_raw = held([P, 2 * N], U8, "w4_raw")
        tab_plane = held([P, T], U8, "tab_plane")
        nc.vector.memset(tab_plane[:].bitcast(I32), 0)

        x_rows = x.rearrange("(p i) m -> p i m", i=PACK)
        x_raw = {}

        def load_x(strip):
            x_raw[strip] = held([P, PACK, STRIP], F32, f"x_raw{strip}")
            nc.sync.dma_start(x_raw[strip][:], x_rows[:, :, strip * STRIP : (strip + 1) * STRIP])

        wd_rows = wdT.rearrange("(p s) c -> p s c", s=PACK)
        wd_raw = {}

        def load_wd(piece):
            pair, lo, hi = WD_LOADS[piece]
            wd_raw[piece] = held([P, 2, hi - lo], F32, f"wd_raw{piece}")
            nc.sync.dma_start(wd_raw[piece][:], wd_rows[:, 2 * pair : 2 * pair + 2, lo:hi])

        g_raw = held([PASSES, PACK * P], F32, "g_raw")
        g_rows = held([P, PACK, P], F32, "g_rows")
        nc.gpsimd.memset(g_rows[:], 0.0)
        w4_plane_raw = held([P, N], U8, "w4_plane_raw")
        nc.gpsimd.memset(w4_plane_raw[:].bitcast(I32), 0)

        load_x(0)
        load_plane(tab_plane, tab_scales[0])
        nc.sync.dma_start(g_raw[:], g.rearrange("(b j) -> b j", b=PASSES))
        tab_codes = held([P, T], U32, "tab_codes")
        nc.sync.dma_start(tab_codes[:].bitcast(I32), tab_words[0].rearrange("p c i -> p (c i)").bitcast(I32))
        x_second = [held([P, PACK, BANK_M], F32, f"x_second{half}") for half in range(2)]
        for half in range(2):
            lo = STRIP + half * BANK_M
            nc.sync.dma_start(x_second[half][:], x_rows[:, :, lo : lo + BANK_M])
        nc.sync.dma_start(w4_raw[:].bitcast(I32), w4_words[0].bitcast(I32))
        load_wd("00")
        load_wd("01")
        load_x(2)
        load_plane(w4_plane_raw, w4_scales[0])
        load_wd("10")
        load_wd("11")
        load_wd("12")
        load_x(3)

        ident = held([P, P], F32, "ident")
        make_identity(nc, ident[:])

        def dealt(words):
            return words.rearrange("p (t q r) -> p q t r", t=PACK, r=RUN)

        def listed(b):
            return offsets[:, b * P * PACK // GROUP : (b + 1) * P * PACK // GROUP]

        v_codes = [held([P, PACK * P], U32, f"v_codes{b}") for b in range(PASSES)]
        picked_plane = held([P, S], U8, "picked_plane")
        v_plane = held([P, S], U8, "v_plane")

        def gather_codes(b):
            nc.vector.tensor_copy(dealt(v_codes[b][:]), tab_codes[:].indirect(listed(b)))

        def gather_plane():
            nc.vector.tensor_copy(picked_plane[:], tab_plane[:].indirect(offsets[:]))
            nc.vector.tensor_copy(
                v_plane[:].bitcast(I32).rearrange("p (t q w) -> p t q w", t=PACK, w=RUN // 4),
                picked_plane[:].bitcast(I32).rearrange("p (q t w) -> p t q w", t=PACK, w=RUN // 4),
            )

        gain = held([P, PASSES, PACK], F32, "gain")

        def turn_gain():
            nc.scalar.copy(
                g_rows[:PASSES].rearrange("b t (q r) -> b t q r", r=RUN),
                g_raw[:].rearrange("b (q t r) -> b t q r", t=PACK, r=RUN),
            )
            g_bank = banked([P, PACK, P], "g_bank", GAIN_BANK)
            for t in range(PACK):
                nc.tensor.transpose(g_bank[:, t, :], g_rows[:, t, :], ident[:])
            nc.scalar.copy(gain[:], g_bank[:, :, :PASSES].rearrange("p t b -> p b t"))

        gain_shift = held([P, PACK], F32, "gain_shift")
        gain_upper = held([P, PACK], F32, "gain_upper")
        gain_lower = held([P, PACK], F32, "gain_lower")

        def bound_gain(b):
            nc.vector.tensor_scalar(gain_shift[:], gain[:, b, :], 3.0, 0.0, ALU.mult, ALU.add)
            nc.vector.tensor_scalar(gain_upper[:], gain[:, b, :], 6.0, 0.0, ALU.mult, ALU.max)
            nc.vector.tensor_scalar(gain_lower[:], gain[:, b, :], 6.0, 0.0, ALU.mult, ALU.min)

        def pool_round(into, values):
            nc.gpsimd.tensor_scalar(into, values, 1.0, 0.0, ALU.mult, ALU.add)

        x_codes = {}
        x_strip = {}
        x_plane = held([P, M], U8, "x_plane")

        def round_x_scalar(strip, into):
            nc.scalar.copy(
                into.rearrange("p (c e i) -> p c i e", e=2, i=PACK),
                x_raw[strip][:].rearrange("p i (c e) -> p c i e", e=2),
            )

        def round_x_pool(strip, into):
            pool_round(into.rearrange("p (c i) -> p c i", i=PACK), x_raw[strip][:].rearrange("p i c -> p c i"))

        def quantize_x(lo, hi, x_bf):
            codes = held([P, hi - lo], U32, f"x_codes{lo}")
            nc.vector.quantize_mx(out=codes[:].bitcast(FP8X4), scales=x_plane[:, lo:hi], in_=x_bf)
            for m0 in range(lo, hi, BANK_M):
                x_codes[m0] = codes[:, m0 - lo : m0 - lo + BANK_M]
            for m0 in range(lo, hi, STRIP):
                x_strip[m0] = codes[:, m0 - lo : m0 - lo + STRIP]

        wd_codes = [held([P, PACK, P], U32, f"wd_codes{b}") for b in range(PASSES)]
        wd_plane = [held([P, PACK, P], U8, f"wd_plane{b}") for b in range(PASSES)]
        wd_bf = {}
        pair_words = {}
        turned = {}

        def round_wd(piece, lo, hi, copy):
            pair, first_column, end_column = WD_LOADS[piece]
            copy(
                pair_words[pair][:, lo:hi].bitcast(BF16).rearrange("p (c e) -> p c e", e=2),
                wd_raw[piece][:, :, lo - first_column : hi - first_column].rearrange("p e c -> p c e"),
            )

        def gather_wd(pair, b):
            picked = held([P, PACK * P], U32, f"picked{pair}{b}")
            nc.vector.tensor_copy(dealt(picked[:]), pair_words[pair][:].indirect(listed(b)))
            turned[pair, b] = banked([P, PACK, P], f"turned{pair}{b}", TURN_BANK[pair, b])
            for t in range(PACK):
                nc.tensor.transpose(turned[pair, b][:, t, :], picked[:, t * P : (t + 1) * P].bitcast(F32), ident[:])

        def copy_turned(pair, b):
            if pair == 0:
                wd_bf[b] = held([P, PACK, P, PACK], BF16, f"wd_bf{b}")
            nc.scalar.copy(
                wd_bf[b][:, 2 * pair : 2 * pair + 2, :, :],
                turned[pair, b][:].bitcast(BF16).rearrange("p t (c e) -> p e c t", e=2),
            )

        def quantize_wd(b):
            nc.vector.quantize_mx(
                out=wd_codes[b][:].rearrange("p s c -> p (s c)").bitcast(FP8X4),
                scales=wd_plane[b][:].rearrange("p s c -> p (s c)"),
                in_=wd_bf[b][:].rearrange("p s c t -> p (s c t)"),
            )

        def deal_w4_codes():
            codes = held([P, PACK, 2 * P], U8, "w4_codes")
            nc.vector.tensor_copy(codes[:].bitcast(U16), w4_raw[:].bitcast(U16).rearrange("p (c s) -> p s c", s=PACK))
            return codes

        w4_plane = {}

        def deal_w4_plane(first, end):
            plane = held([P, end - first, P], U8, f"w4_plane{first}")
            nc.gpsimd.tensor_copy(plane[:], w4_plane_raw[:].rearrange("p (c s) -> p s c", s=PACK)[:, first:end, :])
            for s in range(first, end):
                w4_plane[s] = plane[:, s - first, :]

        a_banks = {}
        lifted = {}
        gated = {}
        h_bf = {}
        h_bank = {}
        h_operand = {}

        def lift(unit, m0):
            b, lo, hi = unit
            nc.scalar.activation(
                lifted[unit][:, :, m0 - lo : m0 - lo + BANK_M], a_banks[b, m0][:], ACT.Relu, bias=3.0
            )

        def lift_gained(unit, m0):
            b, lo, hi = unit
            for t in range(PACK):
                nc.scalar.activation(
                    lifted[unit][:, t, m0 - lo : m0 - lo + BANK_M],
                    a_banks[b, m0][:, t, :],
                    ACT.Identity,
                    bias=gain_shift[:, t : t + 1],
                    scale=gain[:, b, t : t + 1],
                )

        def gate_pool(unit):
            b, lo, hi = unit
            gated[unit] = held([P, PACK, hi - lo], F32, f"gated{b}_{lo}")
            for t in range(PACK):
                nc.gpsimd.tensor_scalar(
                    gated[unit][:, t, :],
                    lifted[unit][:, t, :],
                    gain_upper[:, t : t + 1],
                    gain_lower[:, t : t + 1],
                    ALU.min,
                    ALU.max,
                )

        def project(unit, lifter):
            b, lo, hi = unit
            if unit not in lifted:
                lifted[unit] = held([P, PACK, hi - lo], F32, f"lifted{b}_{lo}")
            for m0 in range(lo, hi, BANK_M):
                bank = banked([P, PACK, BANK_M], f"a_bank{b}_{m0}", A_BANK[b, m0])
                a_banks[b, m0] = bank
                for t in range(PACK):
                    plane0 = (t * PASSES + b) * P
                    nc.tensor.matmul_mx(
                        out=bank[:, t, :],
                        lhsT=v_codes[b][:, t * P : (t + 1) * P].bitcast(FP8X4),
                        lhsT_scale=v_plane[:, plane0 : plane0 + P],
                        rhs=x_codes[m0].bitcast(FP8X4),
                        rhs_scale=x_plane[:, m0 : m0 + BANK_M],
                        start=True,
                        stop=True,
                    )
                lifter(unit, m0)

        def gate(unit):
            b, lo, hi = unit
            gated[unit] = held([P, PACK, hi - lo], F32, f"gated{b}_{lo}")
            for t in range(PACK):
                nc.vector.tensor_scalar(
                    gated[unit][:, t, :], lifted[unit][:, t, :], 6.0, gain[:, b, t : t + 1], ALU.min, ALU.mult
                )

        def hold_h(name, pieces):
            tile = held([P, sum(hi - lo for b, lo, hi in pieces) * PACK], BF16, f"h_bf{name}")
            h_bf[name] = (tile, pieces)
            column = 0
            for b, lo, hi in pieces:
                for m0 in range(lo, hi, BANK_M):
                    h_bank[b, m0] = tile[:, column * PACK : (column + BANK_M) * PACK]
                    column = column + BANK_M

        def swish(unit, first, end):
            b, lo, hi = unit
            for m0 in range(first, end, BANK_M):
                c0 = m0 - lo
                nc.vector.tensor_tensor(
                    h_bank[b, m0].rearrange("p (c e t) -> p c t e", e=2, t=PACK),
                    a_banks[b, m0][:].rearrange("p t (c e) -> p c t e", e=2),
                    gated[unit][:, :, c0 : c0 + BANK_M].rearrange("p t (c e) -> p c t e", e=2),
                    ALU.mult,
                )

        def quantize_h(name):
            tile, pieces = h_bf[name]
            width = sum(hi - lo for b, lo, hi in pieces)
            codes = held([P, width], U32, f"h_codes{name}")
            plane = held([P, width], U8, f"h_plane{name}")
            nc.vector.quantize_mx(out=codes[:].bitcast(FP8X4), scales=plane[:], in_=tile[:])
            column = 0
            for b, lo, hi in pieces:
                h_operand[b, lo] = (codes[:, column : column + hi - lo], plane[:, column : column + hi - lo])
                column = column + hi - lo

        y_f32 = [held([P, PACK, STRIP], F32, f"y_f32_{strip}") for strip in range(M // STRIP - 1)]
        y_last = {m0: held([P, PACK, BANK_M], F32, f"y_last{m0}") for m0 in range(M - STRIP, M, BANK_M)}
        y_bf = {}
        y_bf_bank = {}
        y_codes = held([P, M], U32, "y_codes")
        y_plane = held([P, M], U8, "y_plane")
        y_rows = out_0.rearrange("(p s) m -> p s m", s=PACK)
        y_words = out_1[0].rearrange("p m s -> p (m s)")

        def down(m0, bank):
            for s in range(PACK):
                nc.tensor.matmul_mx(
                    out=bank[:, s, :],
                    lhsT=w4_codes[:, s, :].bitcast(FP4X4),
                    lhsT_scale=w4_plane[s],
                    rhs=x_codes[m0].bitcast(FP8X4),
                    rhs_scale=x_plane[:, m0 : m0 + BANK_M],
                    start=(s == 0),
                    stop=False,
                )
            for b in range(PASSES):
                for s in range(PACK):
                    nc.tensor.matmul_mx(
                        out=bank[:, s, :],
                        lhsT=wd_codes[b][:, s, :].bitcast(FP8X4),
                        lhsT_scale=wd_plane[b][:, s, :],
                        rhs=h_operand[b, m0][0].bitcast(FP8X4),
                        rhs_scale=h_operand[b, m0][1],
                        start=False,
                        stop=(b == PASSES - 1 and s == PACK - 1),
                    )

        def hold_y(lo, hi):
            y_bf[lo] = held([P, hi - lo, PACK], BF16, f"y_bf{lo}")
            for m0 in range(lo, hi, BANK_M):
                y_bf_bank[m0] = y_bf[lo][:, m0 - lo : m0 - lo + BANK_M, :]

        def down_strip(lo):
            values = y_f32[lo // STRIP]
            banks = [banked([P, 2, STRIP], f"y_bank{lo}_{pair}", Y_BANK[lo] + pair) for pair in range(2)]
            for s in range(PACK):
                nc.tensor.matmul_mx(
                    out=banks[s // 2][:, s % 2, :],
                    lhsT=w4_codes[:, s, :].bitcast(FP4X4),
                    lhsT_scale=w4_plane[s],
                    rhs=x_strip[lo].bitcast(FP8X4),
                    rhs_scale=x_plane[:, lo : lo + STRIP],
                    start=(s % 2 == 0),
                    stop=False,
                )
            for b in range(PASSES):
                for s in range(PACK):
                    nc.tensor.matmul_mx(
                        out=banks[s // 2][:, s % 2, :],
                        lhsT=wd_codes[b][:, s, :].bitcast(FP8X4),
                        lhsT_scale=wd_plane[b][:, s, :],
                        rhs=h_operand[b, lo][0].bitcast(FP8X4),
                        rhs_scale=h_operand[b, lo][1],
                        start=False,
                        stop=(b == PASSES - 1 and s % 2 == 1),
                    )
            for pair in range(2):
                nc.scalar.copy(values[:, 2 * pair : 2 * pair + 2, :], banks[pair][:])
            nc.sync.dma_start(y_rows[:, :, lo : lo + STRIP], values[:])

        def round_y_scalar(into, values):
            nc.scalar.copy(
                into.rearrange("p (c e) s -> p c s e", e=2), values.rearrange("p s (c e) -> p c s e", e=2)
            )

        def down_last(m0, queue):
            bank = banked([P, PACK, BANK_M], f"y_bank{m0}", Y_BANK[m0])
            down(m0, bank)
            nc.scalar.copy(y_last[m0][:], bank[:])
            queue.dma_start(y_rows[:, :, m0 : m0 + BANK_M], y_last[m0][:])

        def round_y_vector(into, values):
            nc.vector.tensor_copy(
                into.rearrange("p (c e) s -> p c s e", e=2), values.rearrange("p s (c e) -> p c s e", e=2)
            )

        def quantize_y(lo, hi):
            nc.vector.quantize_mx(
                out=y_codes[:, lo:hi].bitcast(FP8X4),
                scales=y_plane[:, lo:hi],
                in_=y_bf[lo][:].rearrange("p m s -> p (m s)"),
            )

        def store_words(lo, hi):
            nc.sync.dma_start(y_words[:, lo * PACK : hi * PACK].bitcast(I32), y_codes[:, lo:hi].bitcast(I32))

        first, second, third, fourth = (0, 0, 256), (1, 0, 256), (0, 256, 512), (1, 256, 512)
        fifth, sixth, seventh, eighth = (0, 512, 768), (1, 512, 768), (0, 768, 1024), (1, 768, 1024)

        x_bf0 = held([P, STRIP * PACK], BF16, "x_bf0")
        round_x_scalar(0, x_bf0[:])
        turn_gain()
        gather_plane()
        quantize_x(0, 256, x_bf0[:])
        gather_codes(0)
        gather_codes(1)
        x_bf1 = held([P, STRIP * PACK], BF16, "x_bf1")
        nc.scalar.copy(
            x_bf1[:, : BANK_M * PACK].rearrange("p (c e i) -> p c i e", e=2, i=PACK),
            x_second[0][:].rearrange("p i (c e) -> p c i e", e=2),
        )
        pool_round(
            x_bf1[:, BANK_M * PACK :].rearrange("p (c i) -> p c i", i=PACK), x_second[1][:].rearrange("p i c -> p c i")
        )
        project(first, lift)
        project(second, lift)
        quantize_x(256, 512, x_bf1[:])
        project(third, lift)
        project(fourth, lift)
        w4_codes = deal_w4_codes()
        bound_gain(seventh[0])
        gate(first)
        gate(second)
        hold_h("0", (first, second))
        swish(first, 0, 256)
        swish(second, 0, 256)

        pair_words[0] = held([P, T], U32, "pair_words0")
        round_wd("00", 0, POOL_COLUMNS, nc.gpsimd.tensor_copy)
        round_wd("00", POOL_COLUMNS, HALF, nc.scalar.copy)
        round_wd("01", HALF, T, nc.scalar.copy)
        x_bf2 = held([P, STRIP * PACK], BF16, "x_bf2")
        round_x_scalar(2, x_bf2[:])
        gate(third)
        gate(fourth)
        quantize_h("0")
        gather_wd(0, 0)
        gather_wd(0, 1)
        quantize_x(512, 768, x_bf2[:])
        deal_w4_plane(0, PACK - 1)
        pair_words[1] = held([P, T], U32, "pair_words1")
        round_wd("10", 0, POOL_EARLY, nc.gpsimd.tensor_copy)
        deal_w4_plane(PACK - 1, PACK)
        round_wd("11", POOL_EARLY, T - POOL_LAST, nc.scalar.copy)
        round_wd("12", T - POOL_LAST, T, nc.gpsimd.tensor_copy)
        x_bf3 = held([P, STRIP * PACK], BF16, "x_bf3")
        round_x_pool(3, x_bf3[:])
        copy_turned(0, 0)
        copy_turned(0, 1)
        lifted_third = held([P, PASSES, PACK, STRIP], F32, "lifted512")
        lifted[fifth] = lifted_third[:, 0]
        lifted[sixth] = lifted_third[:, 1]
        project(fifth, lift)
        hold_h("256", (third, fourth))
        swish(third, 256, 512)
        swish(fourth, 256, 512)
        project(sixth, lift)
        for b in range(PASSES):
            gather_wd(1, b)
            copy_turned(1, b)
        quantize_x(768, 1024, x_bf3[:])
        project(seventh, lift_gained)
        gate(fifth)
        quantize_wd(0)
        quantize_h("256")
        quantize_wd(1)

        down_strip(0)
        gate(sixth)
        gate_pool(seventh)
        hold_h("512", (fifth, sixth))
        swish(fifth, 512, 768)
        project(eighth, lift)
        down_strip(256)
        swish(sixth, 512, 768)
        gate(eighth)
        quantize_h("512")
        hold_y(0, 256)
        pool_round(y_bf[0][:, :POOL_PIXELS, :], y_f32[0][:, :, :POOL_PIXELS].rearrange("p s m -> p m s"))
        round_y_scalar(y_bf[0][:, POOL_PIXELS:, :], y_f32[0][:, :, POOL_PIXELS:])
        hold_y(256, 384)
        round_y_scalar(y_bf[256][:], y_f32[1][:, :, :BANK_M])
        down_strip(512)
        hold_y(384, 768)
        round_y_scalar(y_bf_bank[384], y_f32[1][:, :, BANK_M:])
        hold_h("768", ((0, 768, 896), (0, 896, 1024)))
        swish(seventh, 768, 1024)
        hold_h("768b", ((1, 768, 896),))
        swish(eighth, 768, 896)
        quantize_h("768")
        quantize_h("768b")
        hold_y(768, 896)
        hold_y(896, 1024)
        down_last(768, nc.sync)
        hold_h("896", ((1, 896, 1024),))
        swish(eighth, 896, 1024)
        quantize_y(0, 256)
        quantize_h("896")
        down_last(896, nc.scalar)
        round_y_vector(y_bf[384][:, BANK_M:, :], y_f32[2][:])
        quantize_y(256, 384)
        store_words(0, 384)
        round_y_vector(y_bf_bank[768], y_last[768][:])
        quantize_y(384, 768)
        store_words(384, 768)
        round_y_vector(y_bf_bank[896], y_last[896][:])
        quantize_y(768, 896)
        quantize_y(896, 1024)
        store_words(768, 1024)
        for q in range(QUADRANTS):
            queue = nc.sync if q < QUADRANTS // 2 else nc.scalar
            queue.dma_start(
                out_2[0, 4 * q : 4 * q + 4, :].bitcast(I32), y_plane[32 * q : 32 * q + 4, :].bitcast(I32)
            )
